import numpy as np
import ml_dtypes


def mxq(x, axis, fmt="e4m3"):
    dtype, down = {"e4m3": (ml_dtypes.float8_e4m3fn, 7), "e5m2": (ml_dtypes.float8_e5m2, 14)}[fmt]
    v = np.moveaxis(np.asarray(x, np.float32).astype(ml_dtypes.bfloat16).astype(np.float64), axis, -1)
    blocks = v.reshape(v.shape[:-1] + (-1, 32))
    amax = np.abs(blocks).max(-1, keepdims=True)
    byte = np.maximum(np.where(amax > 0, np.frexp(amax)[1] - 1 + 127, 0) - down, 1)
    scale = np.exp2(byte - 127.0)
    codes = (blocks / scale).astype(np.float32).astype(dtype).astype(np.float64)
    return np.moveaxis((codes * scale).reshape(v.shape), -1, axis)


WIDE = False


def mx_kscale(k):
    if not WIDE:
        return np.ones(k)
    levels = np.array([10, -10, 5, -5, 0])
    if k % 512:
        return np.exp2(np.random.permutation(np.resize(levels, k // 32))).repeat(32)
    a = np.empty((k // 512, 16))
    for p in range(k // 512):
        a[p, :8] = np.random.permutation(np.resize(levels, 8))
        for g in range(8):
            far = levels[np.abs(levels - a[p, g]) >= 10]
            a[p, g + 8] = far[np.random.randint(len(far))]
    return np.exp2(a.ravel()).repeat(32)


def f64(x):
    return np.asarray(x).astype(np.float64)


def striped(idx):
    return np.tile(idx.reshape(-1, 16).T, (8, 1)).astype(np.uint16)


def unstriped(offs):
    return offs[:16].T.reshape(-1).astype(np.int64)


E2M1 = np.array([0.0, 0.5, 1.0, 1.5, 2.0, 3.0, 4.0, 6.0, -0.0, -0.5, -1.0, -1.5, -2.0, -3.0, -4.0, -6.0])


def pack_weight(w, fmt):
    k, n = w.shape
    w = f64(np.asarray(w, np.float32).astype(ml_dtypes.bfloat16)).reshape(k // 32, 32, n)
    amax = np.abs(w).max(1)
    if fmt == "e4m3":
        byte = np.frexp(amax)[1] - 1 + 127 - 7
    else:
        mant, ex = np.frexp(amax / 6.0)
        byte = np.where(mant > 0.5, ex, ex - 1) + 127
    byte = np.clip(np.where(amax > 0, byte, 1), 1, 254)
    scaled = (w * np.exp2(127.0 - byte)[:, None, :]).reshape(k, n).astype(np.float32)
    by_word = np.ascontiguousarray(scaled.reshape(k // 512, 128, 4, n).transpose(0, 1, 3, 2))
    if fmt == "e4m3":
        words = by_word.astype(ml_dtypes.float8_e4m3fn).view(np.uint8)
    else:
        c = by_word.astype(ml_dtypes.float4_e2m1fn).view(np.uint8) & 0xF
        words = (c[..., 0::2] | (c[..., 1::2] << 4)).reshape(k // 512, 128, 2 * n)
    return np.ascontiguousarray(words), np.ascontiguousarray(byte.astype(np.uint8).reshape(k // 512, 16, n))


def unpack_weight(words, scales, fmt):
    g, _, n = scales.shape
    words = np.ascontiguousarray(words).reshape(g, 128, n, -1)
    if fmt == "e4m3":
        vals = words.view(ml_dtypes.float8_e4m3fn).astype(np.float64)
    else:
        nib = np.empty((g, 128, n, 4), np.uint8)
        nib[..., 0::2] = words & 0xF
        nib[..., 1::2] = words >> 4
        vals = E2M1[nib]
    vals = vals * np.repeat(np.exp2(scales.astype(np.float64) - 127.0), 8, axis=1)[..., None]
    return vals.transpose(0, 1, 3, 2).reshape(g * 512, n)


def gelu(v):
    return 0.5 * v * (1.0 + np.tanh(np.sqrt(2.0 / np.pi) * (v + 0.044715 * v**3)))


def striped8(idx):
    return np.concatenate([v.reshape(-1, 16).T for v in idx]).astype(np.uint16)


def unstriped8(offs):
    return np.stack([offs[16 * g:16 * g + 16].T.reshape(-1) for g in range(8)]).astype(np.int64)


def runs(v, idx8):
    k = np.arange(v.shape[0])
    return v[k[:, None], idx8[k % 512 // 64]]


def often(T, S):
    return np.random.permutation(T)[(T * np.random.uniform(0, 1, S) ** 4).astype(np.int64)]


K, T, S, H, N = 1024, 2048, 1024, 512, 384

def setup_inputs():
    n = np.random.standard_normal
    s = mx_kscale(K)[:, None]
    u = mx_kscale(H)[:, None]
    tab_words, tab_scales = pack_weight(n((K, T)) * s, "e4m3")
    offs = striped8(np.stack([often(T, S) for _ in range(8)]))
    w1_words, w1_scales = pack_weight(1.5 * n((K, H)) / np.sqrt(K) / s, "e2m1")
    w2 = (n((K, H)) / np.sqrt(K) / s * u.T).astype(np.float32)
    w3_words, w3_scales = pack_weight(n((K, H)) / np.sqrt(K) / s * u.T, "e4m3")
    w4 = (1.2 * n((H, N)) / np.sqrt(H) / u).astype(np.float32)
    src = (0.5 * n(N)).astype(np.float32)
    return {"tab_words": tab_words, "tab_scales": tab_scales, "offs": offs,
            "w1_words": w1_words, "w1_scales": w1_scales, "w2": w2,
            "w3_words": w3_words, "w3_scales": w3_scales,
            "w4": w4, "src": src}

def reference(tab_words, tab_scales, offs, w1_words, w1_scales, w2,
              w3_words, w3_scales, w4, src):
    v = runs(unpack_weight(tab_words, tab_scales, "e4m3"), unstriped8(offs))
    w1 = unpack_weight(w1_words, w1_scales, "e2m1")
    w3 = unpack_weight(w3_words, w3_scales, "e4m3")
    f = 1.0 / (1.0 + np.exp(-(w1.T @ v)))
    left = mxq(f64(w2), 0, "e4m3").T @ v
    right = w3.T @ v
    h = left + f * (right - left)
    y = mxq(f64(w4), 0, "e4m3").T @ mxq(h, 0, "e4m3")
    return y + f64(src)[:, None]

@@ -1,0 +1,306 @@
+from contextlib import ExitStack
+
+import concourse.mybir as mybir
+
+K, T, S, H, N = 1024, 2048, 1024, 512, 384
+FLOPS = 2 * S * (3 * K * H + H * N)
+
+F32 = mybir.dt.float32
+BF16 = mybir.dt.bfloat16
+I32 = mybir.dt.int32
+U32 = mybir.dt.uint32
+U16 = mybir.dt.uint16
+U8 = mybir.dt.uint8
+FP8X4 = mybir.dt.float8_e4m3fn_x4
+FP4X4 = mybir.dt.float4_e2m1fn_x4
+ALU = mybir.AluOpType
+ACT = mybir.ActivationFunctionType
+
+P = 128
+PASSES = K // 512
+QUARTER = 256
+QUARTERS = S // QUARTER
+N_TILES = N // P
+W1_AT, W3_AT, PLANE = S, S + H, S + 2 * H
+
+
+def tile_list_tracer_departure_blend_kernel(
+    tc, tab_words, tab_scales, offs, w1_words, w1_scales, w2, w3_words, w3_scales, w4, src, out
+):
+    nc = tc.nc
+    with ExitStack() as ctx:
+        keep = ctx.enter_context(tc.tile_pool(name="keep", bufs=1))
+        psum = ctx.enter_context(tc.psum_pool(name="psum", bufs=8))
+
+        def held(shape, dtype, name, tag=""):
+            return keep.tile(shape, dtype, name=name, tag=tag or name, align_bytes=64)
+
+        offsets = keep.tile([P, S // 16], U16, name="offsets")
+        nc.sync.dma_start(offsets[:], offs)
+
+        raw_w1 = held([P, PASSES, H // 2], I32, "raw_w1")
+        nc.sync.dma_start(raw_w1[:], w1_words.bitcast(I32).rearrange("a p c -> p a c"))
+        scale_window = held([P, T], U8, "scale_window")
+        nc.vector.memset(scale_window[:].bitcast(I32), 0)
+        nc.sync.dma_start(
+            scale_window[:].bitcast(I32)[0:P:4, :], tab_scales.bitcast(I32).rearrange("a q t -> q a t")
+        )
+        raw_scales = held([P, 2, H // 4], I32, "raw_scales")
+        nc.gpsimd.memset(raw_scales[:], 0)
+        for w, scales in enumerate((w1_scales, w3_scales)):
+            nc.sync.dma_start(raw_scales[0:P:4, w, :], scales.bitcast(I32).rearrange("a q c -> q a c"))
+        plane = held([P, PASSES, PLANE], U8, "plane")
+        plane_words = plane[:].rearrange("p a s -> p (a s)").bitcast(I32)
+        nc.gpsimd.memset(plane_words, 0)
+
+        raw_w3 = held([P, PASSES, H], I32, "raw_w3")
+        nc.sync.dma_start(
+            raw_w3[:], w3_words.rearrange("a p c i -> a p (c i)").bitcast(I32).rearrange("a p c -> p a c")
+        )
+        word_window = []
+        for a in range(PASSES):
+            window = held([P, T], I32, "word_window%d" % a, tag="late%d" % a)
+            nc.sync.dma_start(window[:], tab_words[a].rearrange("p t i -> p (t i)").bitcast(I32))
+            word_window.append(window)
+
+        warm = held([P, 2], F32, "warm")
+        nc.gpsimd.memset(warm[:, 0:1], 0.0)
+        nc.scalar.activation(warm[:, 1:2], warm[:, 0:1], ACT.Sigmoid)
+
+        picked_scales = held([P, S], U8, "picked_scales")
+        nc.vector.tensor_copy(picked_scales[:], scale_window[:].indirect(offsets[:]))
+        spread = held([P, PLANE // 4], I32, "spread")
+        nc.vector.tensor_copy(
+            spread[:, W1_AT // 4 :].rearrange("p (w t c) -> p w t c", w=2, t=4),
+            raw_scales[:].rearrange("p w (c t) -> p w t c", t=4),
+        )
+        nc.vector.tensor_copy(spread[:, : S // 4], picked_scales[:].bitcast(I32))
+        for d in range(4):
+            nc.scalar.dma_start(plane_words[32 * d : 32 * d + 4, :], spread[32 * d : 32 * d + 32 : 4, :])
+
+        w1_codes = held([P, PASSES, 4, 2 * P], U8, "w1_codes")
+        nc.vector.tensor_copy(
+            w1_codes[:].bitcast(I32).rearrange("p a t (c i) -> p a t c i", i=2),
+            raw_w1[:].rearrange("p a (c t i) -> p a t c i", t=4, i=2),
+        )
+        w3_codes = held([P, PASSES, 4, P], I32, "w3_codes")
+        nc.vector.tensor_copy(
+            w3_codes[:].rearrange("p a t (c i) -> p a t c i", i=4),
+            raw_w3[:].rearrange("p a (c t i) -> p a t c i", t=4, i=4),
+        )
+
+        raw_w2 = [held([P, 4, H], F32, "raw_w2_0", tag="raw_w3")]
+        nc.sync.dma_start(raw_w2[0][:], w2[0:512, :].rearrange("(p j) r -> p j r", j=4))
+
+        v_codes = {}
+
+        def gather_words(a, q):
+            picked = held([P, QUARTER], U32, "v_codes_%d_%d" % (a, q))
+            cols = slice(q * QUARTER // 16, (q + 1) * QUARTER // 16)
+            nc.vector.tensor_copy(picked[:], word_window[a][:].bitcast(U32).indirect(offsets[:, cols]))
+            v_codes[a, q] = picked
+
+        for q in range(QUARTERS):
+            gather_words(0, q)
+        late_w2 = held([P, 2, 4, H // 2], F32, "raw_w2_1", tag="late0")
+        for half in range(2):
+            rows = w2[512:1024, 256 * half : 256 * (half + 1)]
+            nc.sync.dma_start(late_w2[:, half, :, :], rows.rearrange("(p j) r -> p j r", j=4))
+        w4_rows = w4.rearrange("(c t i) n -> t c i n", t=4, i=4)
+        staged = {}
+
+        def load_w4():
+            staged["w4"] = held([P, 4, N], F32, "raw_w4", tag="late1")
+            for t in range(4):
+                nc.sync.dma_start(staged["w4"][:, t, :], w4_rows[t])
+
+        sources = held([P, N_TILES], F32, "sources", tag="scale_window")
+        with nc.allow_non_contiguous_dma(reason="one source value a partition"):
+            nc.gpsimd.dma_start(sources[:], src.rearrange("(c p) -> p c", p=P))
+
+        grouped = [held([P, 4, 32, 4, 4], BF16, "w2_grouped%d" % a) for a in range(PASSES)]
+        w2_codes = [held([P, H], U32, "w2_codes%d" % a) for a in range(PASSES)]
+        w2_scales = [held([P, H], U8, "w2_scales%d" % a) for a in range(PASSES)]
+
+        def round_w2(a, half):
+            dst = grouped[a][:, :, 16 * half : 16 * (half + 1), :, :].rearrange("p t c i j -> p t c j i")
+            if a == 0:
+                rows = raw_w2[0][:, :, 256 * half : 256 * (half + 1)]
+                nc.scalar.copy(dst, rows.rearrange("p j (c t i) -> p t c j i", t=4, i=4))
+            else:
+                nc.vector.tensor_copy(dst, late_w2[:, half, :, :].rearrange("p j (c t i) -> p t c j i", t=4, i=4))
+
+        def quantise_w2(a):
+            nc.vector.quantize_mx(
+                out=w2_codes[a][:].bitcast(FP8X4),
+                scales=w2_scales[a][:],
+                in_=grouped[a][:].rearrange("p t c i j -> p (t c i j)"),
+            )
+
+        w4_grouped = held([P, N, 4], BF16, "w4_grouped")
+        w4_codes = held([P, N], U32, "w4_codes")
+        w4_scales = held([P, N], U8, "w4_scales")
+
+        def round_w4():
+            nc.scalar.copy(
+                w4_grouped[:].rearrange("p (c i) t -> p c t i", i=4), staged["w4"][:].rearrange("p t (c i) -> p c t i", i=4)
+            )
+
+        def quantise_w4():
+            for lo, hi in ((0, 256), (256, N)):
+                nc.vector.quantize_mx(
+                    out=w4_codes[:, lo:hi].bitcast(FP8X4),
+                    scales=w4_scales[:, lo:hi],
+                    in_=w4_grouped[:, lo:hi, :].rearrange("p n t -> p (n t)"),
+                )
+
+        banks = {}
+
+        def passes(weight, q, u, which):
+            width, codes_of, scales_of = weights[weight]
+            if which[0] == 0:
+                banks[weight, q, u] = psum.tile([P, 2, QUARTER], F32, name="bank")
+            bank = banks[weight, q, u]
+            for a in which:
+                for e in range(2):
+                    for lo in range(0, QUARTER, width):
+                        nc.tensor.matmul_mx(
+                            out=bank[:, e, lo : lo + width],
+                            lhsT=codes_of(a, 2 * u + e),
+                            lhsT_scale=scales_of(a, 2 * u + e),
+                            rhs=v_codes[a, q][:, lo : lo + width].bitcast(FP8X4),
+                            rhs_scale=plane[:, a, q * QUARTER + lo : q * QUARTER + lo + width],
+                            start=(a == 0 and e == 0 and lo == 0),
+                            stop=(a == PASSES - 1 and e == 1 and lo + width == QUARTER),
+                        )
+            return bank[:].rearrange("p e j -> p j e")
+
+        weights = {
+            "w1": (
+                P,
+                lambda a, t: w1_codes[:, a, t, :].bitcast(FP4X4),
+                lambda a, t: plane[:, a, W1_AT + P * t : W1_AT + P * (t + 1)],
+            ),
+            "w2": (
+                QUARTER,
+                lambda a, t: w2_codes[a][:, P * t : P * (t + 1)].bitcast(FP8X4),
+                lambda a, t: w2_scales[a][:, P * t : P * (t + 1)],
+            ),
+            "w3": (
+                QUARTER,
+                lambda a, t: w3_codes[:, a, t, :].bitcast(FP8X4),
+                lambda a, t: plane[:, a, W3_AT + P * t : W3_AT + P * (t + 1)],
+            ),
+        }
+
+        out_rows = out.rearrange("(c p) j -> p c j", p=P)
+        fraction = [held([P, 2, QUARTER, 2], F32, "fraction%d" % q) for q in range(QUARTERS)]
+        right_part = [held([P, 2, QUARTER, 2], F32, "right_part%d" % q) for q in range(QUARTERS)]
+        left_part = [held([P, 2, QUARTER, 2], F32, "left_part%d" % q) for q in range(QUARTERS)]
+        blend = [held([P, QUARTER, 2, 2], BF16, "blend%d" % q) for q in range(QUARTERS)]
+        h_codes = [held([P, QUARTER], U32, "h_codes%d" % q) for q in range(QUARTERS)]
+        h_scales = [held([P, QUARTER], U8, "h_scales%d" % q) for q in range(QUARTERS)]
+        result = [held([P, N_TILES, QUARTER], F32, "result%d" % q) for q in range(QUARTERS)]
+
+        def open_right(q, u):
+            passes("w1", q, u, (0,))
+            passes("w3", q, u, (0,))
+
+        def right_side(q, u, which=(0, 1)):
+            logit = passes("w1", q, u, which)
+            nc.scalar.activation(fraction[q][:, u, :, :], logit, ACT.Sigmoid)
+            right = passes("w3", q, u, which)
+            nc.vector.tensor_tensor(right_part[q][:, u, :, :], right, fraction[q][:, u, :, :], ALU.mult)
+
+        def left_side(q, u):
+            left = passes("w2", q, u, (0, 1))
+            nc.vector.scalar_tensor_tensor(
+                left_part[q][:, u, :, :], fraction[q][:, u, :, :], 1.0, left, ALU.subtract, ALU.mult
+            )
+
+        def join(q, lo=0, hi=QUARTER, engine=nc.vector):
+            engine.tensor_tensor(
+                blend[q][:, lo:hi, :, :],
+                right_part[q][:, :, lo:hi, :].rearrange("p u j e -> p j u e"),
+                left_part[q][:, :, lo:hi, :].rearrange("p u j e -> p j u e"),
+                ALU.subtract,
+            )
+
+        def quantise_h(q, lo=0, hi=QUARTER):
+            nc.vector.quantize_mx(
+                out=h_codes[q][:, lo:hi].bitcast(FP8X4),
+                scales=h_scales[q][:, lo:hi],
+                in_=blend[q][:, lo:hi, :, :].rearrange("p j u e -> p (j u e)"),
+            )
+
+        def tendencies(q, lo=0, hi=QUARTER, last=False):
+            for first in range(0, N_TILES, 2):
+                bank = psum.tile([P, 2, QUARTER], F32, name="bank")
+                tiles = range(first, min(first + 2, N_TILES))
+                for c in tiles:
+                    nc.tensor.matmul_mx(
+                        out=bank[:, c - first, lo:hi],
+                        lhsT=w4_codes[:, P * c : P * (c + 1)].bitcast(FP8X4),
+                        lhsT_scale=w4_scales[:, P * c : P * (c + 1)],
+                        rhs=h_codes[q][:, lo:hi].bitcast(FP8X4),
+                        rhs_scale=h_scales[q][:, lo:hi],
+                        start=True,
+                        stop=True,
+                    )
+                for c in tiles:
+                    if last and first > 0:
+                        nc.vector.tensor_scalar(
+                            result[q][:, c, lo:hi], bank[:, c - first, lo:hi], sources[:, c : c + 1], None, ALU.add
+                        )
+                    else:
+                        nc.scalar.activation(
+                            result[q][:, c, lo:hi], bank[:, c - first, lo:hi], ACT.Identity, bias=sources[:, c : c + 1]
+                        )
+            nc.sync.dma_start(out_rows[:, :, q * QUARTER + lo : q * QUARTER + hi], result[q][:, :, lo:hi])
+
+        open_right(0, 0)
+        open_right(0, 1)
+        gather_words(1, 0)
+        gather_words(1, 1)
+        gather_words(1, 2)
+        right_side(0, 0, (1,))
+        gather_words(1, 3)
+        load_w4()
+        right_side(0, 1, (1,))
+        round_w2(0, 0)
+        round_w2(1, 0)
+        right_side(1, 0)
+        round_w2(0, 1)
+        round_w2(1, 1)
+        right_side(1, 1)
+        quantise_w2(0)
+        quantise_w2(1)
+        right_side(2, 0)
+        right_side(2, 1)
+        round_w4()
+        left_side(0, 0)
+        left_side(0, 1)
+        right_side(3, 0)
+        join(0)
+        quantise_w4()
+        left_side(1, 0)
+        quantise_h(0)
+        left_side(1, 1)
+        tendencies(0)
+        right_side(3, 1)
+        join(1)
+        left_side(2, 0)
+        quantise_h(1)
+        left_side(2, 1)
+        tendencies(1)
+        left_side(3, 0)
+        join(2)
+        left_side(3, 1)
+        quantise_h(2)
+        join(3, 0, 128)
+        tendencies(2)
+        join(3, 128, 256)
+        quantise_h(3, 0, 128)
+        quantise_h(3, 128, 256)
+        tendencies(3, 0, 128)
+        tendencies(3, 128, 256, True)

@@ -21,7 +21,8 @@ PASSES = K // 512
 QUARTER = 256
 QUARTERS = S // QUARTER
 N_TILES = N // P
-W1_AT, W3_AT, PLANE = S, S + H, S + 2 * H
+HALF = S // 2
+W1_AT, W3_AT, V_AT, PLANE = 0, H, 2 * H, 2 * H + HALF
 
 
 def tile_list_tracer_departure_blend_kernel(
@@ -46,12 +47,15 @@ def tile_list_tracer_departure_blend_kernel(
             scale_window[:].bitcast(I32)[0:P:4, :], tab_scales.bitcast(I32).rearrange("a q t -> q a t")
         )
         raw_scales = held([P, 2, H // 4], I32, "raw_scales")
-        nc.gpsimd.memset(raw_scales[:], 0)
+        nc.vector.memset(raw_scales[:], 0)
         for w, scales in enumerate((w1_scales, w3_scales)):
             nc.sync.dma_start(raw_scales[0:P:4, w, :], scales.bitcast(I32).rearrange("a q c -> q a c"))
         plane = held([P, PASSES, PLANE], U8, "plane")
         plane_words = plane[:].rearrange("p a s -> p (a s)").bitcast(I32)
-        nc.gpsimd.memset(plane_words, 0)
+        nc.vector.memset(plane_words, 0)
+        late_plane = held([P, PASSES, HALF], U8, "late_plane")
+        late_words = late_plane[:].rearrange("p a s -> p (a s)").bitcast(I32)
+        nc.vector.memset(late_words, 0)
 
         raw_w3 = held([P, PASSES, H], I32, "raw_w3")
         nc.sync.dma_start(
@@ -64,19 +68,30 @@ def tile_list_tracer_departure_blend_kernel(
             word_window.append(window)
 
         warm = held([P, 2], F32, "warm")
-        nc.gpsimd.memset(warm[:, 0:1], 0.0)
+        nc.vector.memset(warm[:, 0:1], 0.0)
         nc.scalar.activation(warm[:, 1:2], warm[:, 0:1], ACT.Sigmoid)
 
-        picked_scales = held([P, S], U8, "picked_scales")
-        nc.vector.tensor_copy(picked_scales[:], scale_window[:].indirect(offsets[:]))
+        picked_scales = [held([P, HALF], U8, "picked_scales0", tag="picked_scales")]
+        nc.vector.tensor_copy(picked_scales[0][:], scale_window[:].indirect(offsets[:, : HALF // 16]))
         spread = held([P, PLANE // 4], I32, "spread")
         nc.vector.tensor_copy(
-            spread[:, W1_AT // 4 :].rearrange("p (w t c) -> p w t c", w=2, t=4),
+            spread[:, : V_AT // 4].rearrange("p (w t c) -> p w t c", w=2, t=4),
             raw_scales[:].rearrange("p w (c t) -> p w t c", t=4),
         )
-        nc.vector.tensor_copy(spread[:, : S // 4], picked_scales[:].bitcast(I32))
+        nc.vector.tensor_copy(spread[:, V_AT // 4 :], picked_scales[0][:].bitcast(I32))
         for d in range(4):
             nc.scalar.dma_start(plane_words[32 * d : 32 * d + 4, :], spread[32 * d : 32 * d + 32 : 4, :])
+        picked_scales.append(held([P, HALF], U8, "picked_scales1", tag="picked_scales"))
+        nc.vector.tensor_copy(picked_scales[1][:], scale_window[:].indirect(offsets[:, HALF // 16 :]))
+        for d in range(4):
+            nc.scalar.dma_start(
+                late_words[32 * d : 32 * d + 4, :], picked_scales[1][:].bitcast(I32)[32 * d : 32 * d + 32 : 4, :]
+            )
+
+        def v_scales(a, lo, width):
+            if lo < HALF:
+                return plane[:, a, V_AT + lo : V_AT + lo + width]
+            return late_plane[:, a, lo - HALF : lo - HALF + width]
 
         w1_codes = held([P, PASSES, 4, 2 * P], U8, "w1_codes")
         nc.vector.tensor_copy(
@@ -110,25 +125,26 @@ def tile_list_tracer_departure_blend_kernel(
         staged = {}
 
         def load_w4():
-            staged["w4"] = held([P, 4, N], F32, "raw_w4", tag="late1")
+            staged["late"] = held([P, 4 * N + 8], F32, "raw_w4", tag="late1")
+            staged["w4"] = staged["late"][:, : 4 * N].rearrange("p (t n) -> p t n", t=4)
             for t in range(4):
                 nc.sync.dma_start(staged["w4"][:, t, :], w4_rows[t])
-
-        sources = held([P, N_TILES], F32, "sources", tag="scale_window")
-        with nc.allow_non_contiguous_dma(reason="one source value a partition"):
-            nc.gpsimd.dma_start(sources[:], src.rearrange("(c p) -> p c", p=P))
+            with nc.allow_non_contiguous_dma(reason="one source value a partition"):
+                nc.sync.dma_start(staged["late"][:, 4 * N : 4 * N + N_TILES], src.rearrange("(c p) -> p c", p=P))
 
         grouped = [held([P, 4, 32, 4, 4], BF16, "w2_grouped%d" % a) for a in range(PASSES)]
         w2_codes = [held([P, H], U32, "w2_codes%d" % a) for a in range(PASSES)]
         w2_scales = [held([P, H], U8, "w2_scales%d" % a) for a in range(PASSES)]
 
         def round_w2(a, half):
-            dst = grouped[a][:, :, 16 * half : 16 * (half + 1), :, :].rearrange("p t c i j -> p t c j i")
             if a == 0:
-                rows = raw_w2[0][:, :, 256 * half : 256 * (half + 1)]
-                nc.scalar.copy(dst, rows.rearrange("p j (c t i) -> p t c j i", t=4, i=4))
+                rows, copy = raw_w2[0][:, :, 256 * half : 256 * (half + 1)], nc.scalar.copy
             else:
-                nc.vector.tensor_copy(dst, late_w2[:, half, :, :].rearrange("p j (c t i) -> p t c j i", t=4, i=4))
+                rows, copy = late_w2[:, half, :, :], nc.vector.tensor_copy
+            rows = rows.rearrange("p j (c t i) -> p t c j i", t=4, i=4)
+            dst = grouped[a][:, :, 16 * half : 16 * (half + 1), :, :].rearrange("p t c i j -> p t c j i")
+            for pair in range(2):
+                copy(dst[:, :, :, :, 2 * pair : 2 * pair + 2], rows[:, :, :, :, 2 * pair : 2 * pair + 2])
 
         def quantise_w2(a):
             nc.vector.quantize_mx(
@@ -143,7 +159,7 @@ def tile_list_tracer_departure_blend_kernel(
 
         def round_w4():
             nc.scalar.copy(
-                w4_grouped[:].rearrange("p (c i) t -> p c t i", i=4), staged["w4"][:].rearrange("p t (c i) -> p c t i", i=4)
+                w4_grouped[:].rearrange("p (c i) t -> p c t i", i=2), staged["w4"].rearrange("p t (c i) -> p c t i", i=2)
             )
 
         def quantise_w4():
@@ -169,7 +185,7 @@ def tile_list_tracer_departure_blend_kernel(
                             lhsT=codes_of(a, 2 * u + e),
                             lhsT_scale=scales_of(a, 2 * u + e),
                             rhs=v_codes[a, q][:, lo : lo + width].bitcast(FP8X4),
-                            rhs_scale=plane[:, a, q * QUARTER + lo : q * QUARTER + lo + width],
+                            rhs_scale=v_scales(a, q * QUARTER + lo, width),
                             start=(a == 0 and e == 0 and lo == 0),
                             stop=(a == PASSES - 1 and e == 1 and lo + width == QUARTER),
                         )
@@ -210,7 +226,7 @@ def tile_list_tracer_departure_blend_kernel(
             logit = passes("w1", q, u, which)
             nc.scalar.activation(fraction[q][:, u, :, :], logit, ACT.Sigmoid)
             right = passes("w3", q, u, which)
-            nc.vector.tensor_tensor(right_part[q][:, u, :, :], right, fraction[q][:, u, :, :], ALU.mult)
+            nc.vector.tensor_tensor(right_part[q][:, u, :, :], fraction[q][:, u, :, :], right, ALU.mult)
 
         def left_side(q, u):
             left = passes("w2", q, u, (0, 1))
@@ -250,11 +266,11 @@ def tile_list_tracer_departure_blend_kernel(
                 for c in tiles:
                     if last and first > 0:
                         nc.vector.tensor_scalar(
-                            result[q][:, c, lo:hi], bank[:, c - first, lo:hi], sources[:, c : c + 1], None, ALU.add
+                            result[q][:, c, lo:hi], bank[:, c - first, lo:hi], staged["late"][:, 4 * N + c : 4 * N + c + 1], None, ALU.add
                         )
                     else:
                         nc.scalar.activation(
-                            result[q][:, c, lo:hi], bank[:, c - first, lo:hi], ACT.Identity, bias=sources[:, c : c + 1]
+                            result[q][:, c, lo:hi], bank[:, c - first, lo:hi], ACT.Identity, bias=staged["late"][:, 4 * N + c : 4 * N + c + 1]
                         )
             nc.sync.dma_start(out_rows[:, :, q * QUARTER + lo : q * QUARTER + hi], result[q][:, :, lo:hi])
 
@@ -272,9 +288,9 @@ def tile_list_tracer_departure_blend_kernel(
         right_side(1, 0)
         round_w2(0, 1)
         round_w2(1, 1)
-        right_side(1, 1)
         quantise_w2(0)
         quantise_w2(1)
+        right_side(1, 1)
         right_side(2, 0)
         right_side(2, 1)
         round_w4()
@@ -286,8 +302,8 @@ def tile_list_tracer_departure_blend_kernel(
         left_side(1, 0)
         quantise_h(0)
         left_side(1, 1)
-        tendencies(0)
         right_side(3, 1)
+        tendencies(0)
         join(1)
         left_side(2, 0)
         quantise_h(1)

@@ -17,12 +17,18 @@ ALU = mybir.AluOpType
 ACT = mybir.ActivationFunctionType
 
 P = 128
-PASSES = K // 512
+K_PASS = 4 * P
+PASSES = K // K_PASS
+PER_COLUMN = 16
+BANKS = 8
 QUARTER = 256
 QUARTERS = S // QUARTER
-N_TILES = N // P
 HALF = S // 2
+N_TILES = N // P
 W1_AT, W3_AT, V_AT, PLANE = 0, H, 2 * H, 2 * H + HALF
+W4_SPLIT = 256
+SRC_AT = 4 * N
+SRC_PAD = 8
 
 
 def tile_list_tracer_departure_blend_kernel(
@@ -31,16 +37,17 @@ def tile_list_tracer_departure_blend_kernel(
     nc = tc.nc
     with ExitStack() as ctx:
         keep = ctx.enter_context(tc.tile_pool(name="keep", bufs=1))
-        psum = ctx.enter_context(tc.psum_pool(name="psum", bufs=8))
+        psum = ctx.enter_context(tc.psum_pool(name="psum", bufs=BANKS))
 
         def held(shape, dtype, name, tag=""):
             return keep.tile(shape, dtype, name=name, tag=tag or name, align_bytes=64)
 
-        offsets = keep.tile([P, S // 16], U16, name="offsets")
+        offsets = keep.tile([P, S // PER_COLUMN], U16, name="offsets")
         nc.sync.dma_start(offsets[:], offs)
 
         raw_w1 = held([P, PASSES, H // 2], I32, "raw_w1")
         nc.sync.dma_start(raw_w1[:], w1_words.bitcast(I32).rearrange("a p c -> p a c"))
+
         scale_window = held([P, T], U8, "scale_window")
         nc.vector.memset(scale_window[:].bitcast(I32), 0)
         nc.sync.dma_start(
@@ -50,12 +57,13 @@ def tile_list_tracer_departure_blend_kernel(
         nc.vector.memset(raw_scales[:], 0)
         for w, scales in enumerate((w1_scales, w3_scales)):
             nc.sync.dma_start(raw_scales[0:P:4, w, :], scales.bitcast(I32).rearrange("a q c -> q a c"))
+
         plane = held([P, PASSES, PLANE], U8, "plane")
         plane_words = plane[:].rearrange("p a s -> p (a s)").bitcast(I32)
         nc.vector.memset(plane_words, 0)
         late_plane = held([P, PASSES, HALF], U8, "late_plane")
-        late_words = late_plane[:].rearrange("p a s -> p (a s)").bitcast(I32)
-        nc.vector.memset(late_words, 0)
+        late_plane_words = late_plane[:].rearrange("p a s -> p (a s)").bitcast(I32)
+        nc.vector.memset(late_plane_words, 0)
 
         raw_w3 = held([P, PASSES, H], I32, "raw_w3")
         nc.sync.dma_start(
@@ -63,7 +71,7 @@ def tile_list_tracer_departure_blend_kernel(
         )
         word_window = []
         for a in range(PASSES):
-            window = held([P, T], I32, "word_window%d" % a, tag="late%d" % a)
+            window = held([P, T], I32, "word_window%d" % a)
             nc.sync.dma_start(window[:], tab_words[a].rearrange("p t i -> p (t i)").bitcast(I32))
             word_window.append(window)
 
@@ -71,22 +79,32 @@ def tile_list_tracer_departure_blend_kernel(
         nc.vector.memset(warm[:, 0:1], 0.0)
         nc.scalar.activation(warm[:, 1:2], warm[:, 0:1], ACT.Sigmoid)
 
-        picked_scales = [held([P, HALF], U8, "picked_scales0", tag="picked_scales")]
-        nc.vector.tensor_copy(picked_scales[0][:], scale_window[:].indirect(offsets[:, : HALF // 16]))
+        def gather_scales(half):
+            picked = held([P, HALF], U8, "picked_scales%d" % half, tag="picked_scales")
+            cols = slice(half * HALF // PER_COLUMN, (half + 1) * HALF // PER_COLUMN)
+            nc.vector.tensor_copy(picked[:], scale_window[:].indirect(offsets[:, cols]))
+            return picked[:].bitcast(I32)
+
+        def rows_to_plane(dst_words, src_words):
+            for d in range(4):
+                nc.scalar.dma_start(dst_words[32 * d : 32 * d + 4, :], src_words[32 * d : 32 * d + 32 : 4, :])
+
+        first_picked = gather_scales(0)
         spread = held([P, PLANE // 4], I32, "spread")
         nc.vector.tensor_copy(
             spread[:, : V_AT // 4].rearrange("p (w t c) -> p w t c", w=2, t=4),
             raw_scales[:].rearrange("p w (c t) -> p w t c", t=4),
         )
-        nc.vector.tensor_copy(spread[:, V_AT // 4 :], picked_scales[0][:].bitcast(I32))
-        for d in range(4):
-            nc.scalar.dma_start(plane_words[32 * d : 32 * d + 4, :], spread[32 * d : 32 * d + 32 : 4, :])
-        picked_scales.append(held([P, HALF], U8, "picked_scales1", tag="picked_scales"))
-        nc.vector.tensor_copy(picked_scales[1][:], scale_window[:].indirect(offsets[:, HALF // 16 :]))
-        for d in range(4):
-            nc.scalar.dma_start(
-                late_words[32 * d : 32 * d + 4, :], picked_scales[1][:].bitcast(I32)[32 * d : 32 * d + 32 : 4, :]
-            )
+        nc.vector.tensor_copy(spread[:, V_AT // 4 :], first_picked)
+        rows_to_plane(plane_words, spread[:])
+
+        w3_codes = held([P, PASSES, 4, P], I32, "w3_codes")
+        nc.vector.tensor_copy(
+            w3_codes[:].rearrange("p a t (c i) -> p a t c i", i=4),
+            raw_w3[:].rearrange("p a (c t i) -> p a t c i", t=4, i=4),
+        )
+
+        rows_to_plane(late_plane_words, gather_scales(1))
 
         def v_scales(a, lo, width):
             if lo < HALF:
@@ -98,51 +116,50 @@ def tile_list_tracer_departure_blend_kernel(
             w1_codes[:].bitcast(I32).rearrange("p a t (c i) -> p a t c i", i=2),
             raw_w1[:].rearrange("p a (c t i) -> p a t c i", t=4, i=2),
         )
-        w3_codes = held([P, PASSES, 4, P], I32, "w3_codes")
-        nc.vector.tensor_copy(
-            w3_codes[:].rearrange("p a t (c i) -> p a t c i", i=4),
-            raw_w3[:].rearrange("p a (c t i) -> p a t c i", t=4, i=4),
-        )
 
-        raw_w2 = [held([P, 4, H], F32, "raw_w2_0", tag="raw_w3")]
-        nc.sync.dma_start(raw_w2[0][:], w2[0:512, :].rearrange("(p j) r -> p j r", j=4))
+        raw_w2 = []
+
+        def load_w2(a, tag):
+            raw = held([P, 2, 4, H // 2], F32, "raw_w2_%d" % a, tag=tag)
+            for half in range(2):
+                rows = w2[K_PASS * a : K_PASS * (a + 1), H // 2 * half : H // 2 * (half + 1)]
+                nc.sync.dma_start(raw[:, half, :, :], rows.rearrange("(p j) r -> p j r", j=4))
+            raw_w2.append(raw)
+
+        load_w2(0, "raw_w3")
 
         v_codes = {}
 
-        def gather_words(a, q):
-            picked = held([P, QUARTER], U32, "v_codes_%d_%d" % (a, q))
-            cols = slice(q * QUARTER // 16, (q + 1) * QUARTER // 16)
+        def gather_words(a, q, count):
+            picked = held([P, count * QUARTER], U32, "v_codes_%d_%d" % (a, q))
+            cols = slice(q * QUARTER // PER_COLUMN, (q + count) * QUARTER // PER_COLUMN)
             nc.vector.tensor_copy(picked[:], word_window[a][:].bitcast(U32).indirect(offsets[:, cols]))
-            v_codes[a, q] = picked
+            for n in range(count):
+                v_codes[a, q + n] = picked[:, n * QUARTER : (n + 1) * QUARTER]
 
-        for q in range(QUARTERS):
-            gather_words(0, q)
-        late_w2 = held([P, 2, 4, H // 2], F32, "raw_w2_1", tag="late0")
-        for half in range(2):
-            rows = w2[512:1024, 256 * half : 256 * (half + 1)]
-            nc.sync.dma_start(late_w2[:, half, :, :], rows.rearrange("(p j) r -> p j r", j=4))
-        w4_rows = w4.rearrange("(c t i) n -> t c i n", t=4, i=4)
-        staged = {}
+        for q in range(0, QUARTERS, 2):
+            gather_words(0, q, 2)
+        load_w2(1, "word_window0")
 
-        def load_w4():
-            staged["late"] = held([P, 4 * N + 8], F32, "raw_w4", tag="late1")
-            staged["w4"] = staged["late"][:, : 4 * N].rearrange("p (t n) -> p t n", t=4)
+        second = {}
+
+        def load_w4_and_src():
+            raw = held([P, SRC_AT + SRC_PAD], F32, "raw_w4", tag="word_window1")
+            second["raw_w4"] = raw[:, :SRC_AT].rearrange("p (t n) -> p t n", t=4)
+            second["src"] = raw[:, SRC_AT : SRC_AT + N_TILES]
+            rows = w4.rearrange("(c t i) n -> t c i n", t=4, i=4)
             for t in range(4):
-                nc.sync.dma_start(staged["w4"][:, t, :], w4_rows[t])
+                nc.sync.dma_start(second["raw_w4"][:, t, :], rows[t])
             with nc.allow_non_contiguous_dma(reason="one source value a partition"):
-                nc.sync.dma_start(staged["late"][:, 4 * N : 4 * N + N_TILES], src.rearrange("(c p) -> p c", p=P))
+                nc.sync.dma_start(second["src"], src.rearrange("(c p) -> p c", p=P))
 
-        grouped = [held([P, 4, 32, 4, 4], BF16, "w2_grouped%d" % a) for a in range(PASSES)]
+        w2_rounded = [held([P, 4, 32, 4, 4], BF16, "w2_rounded%d" % a) for a in range(PASSES)]
         w2_codes = [held([P, H], U32, "w2_codes%d" % a) for a in range(PASSES)]
         w2_scales = [held([P, H], U8, "w2_scales%d" % a) for a in range(PASSES)]
 
-        def round_w2(a, half):
-            if a == 0:
-                rows, copy = raw_w2[0][:, :, 256 * half : 256 * (half + 1)], nc.scalar.copy
-            else:
-                rows, copy = late_w2[:, half, :, :], nc.vector.tensor_copy
-            rows = rows.rearrange("p j (c t i) -> p t c j i", t=4, i=4)
-            dst = grouped[a][:, :, 16 * half : 16 * (half + 1), :, :].rearrange("p t c i j -> p t c j i")
+        def round_w2(a, half, copy):
+            rows = raw_w2[a][:, half, :, :].rearrange("p j (c t i) -> p t c j i", t=4, i=4)
+            dst = w2_rounded[a][:, :, 16 * half : 16 * (half + 1), :, :].rearrange("p t c i j -> p t c j i")
             for pair in range(2):
                 copy(dst[:, :, :, :, 2 * pair : 2 * pair + 2], rows[:, :, :, :, 2 * pair : 2 * pair + 2])
 
@@ -150,46 +167,26 @@ def tile_list_tracer_departure_blend_kernel(
             nc.vector.quantize_mx(
                 out=w2_codes[a][:].bitcast(FP8X4),
                 scales=w2_scales[a][:],
-                in_=grouped[a][:].rearrange("p t c i j -> p (t c i j)"),
+                in_=w2_rounded[a][:].rearrange("p t c i j -> p (t c i j)"),
             )
 
-        w4_grouped = held([P, N, 4], BF16, "w4_grouped")
-        w4_codes = held([P, N], U32, "w4_codes")
-        w4_scales = held([P, N], U8, "w4_scales")
+        w4_rounded = held([P, N, 4], BF16, "w4_rounded", tag="rounded")
 
         def round_w4():
             nc.scalar.copy(
-                w4_grouped[:].rearrange("p (c i) t -> p c t i", i=2), staged["w4"].rearrange("p t (c i) -> p c t i", i=2)
+                w4_rounded[:].rearrange("p (n e) t -> p n t e", e=2),
+                second["raw_w4"].rearrange("p t (n e) -> p n t e", e=2),
             )
 
         def quantise_w4():
-            for lo, hi in ((0, 256), (256, N)):
+            second["w4_codes"] = held([P, N], U32, "w4_codes", tag="right_part0")
+            second["w4_scales"] = held([P, N], U8, "w4_scales", tag="left_part0")
+            for lo, hi in ((0, W4_SPLIT), (W4_SPLIT, N)):
                 nc.vector.quantize_mx(
-                    out=w4_codes[:, lo:hi].bitcast(FP8X4),
-                    scales=w4_scales[:, lo:hi],
-                    in_=w4_grouped[:, lo:hi, :].rearrange("p n t -> p (n t)"),
+                    out=second["w4_codes"][:, lo:hi].bitcast(FP8X4),
+                    scales=second["w4_scales"][:, lo:hi],
+                    in_=w4_rounded[:, lo:hi, :].rearrange("p n t -> p (n t)"),
                 )
-
-        banks = {}
-
-        def passes(weight, q, u, which):
-            width, codes_of, scales_of = weights[weight]
-            if which[0] == 0:
-                banks[weight, q, u] = psum.tile([P, 2, QUARTER], F32, name="bank")
-            bank = banks[weight, q, u]
-            for a in which:
-                for e in range(2):
-                    for lo in range(0, QUARTER, width):
-                        nc.tensor.matmul_mx(
-                            out=bank[:, e, lo : lo + width],
-                            lhsT=codes_of(a, 2 * u + e),
-                            lhsT_scale=scales_of(a, 2 * u + e),
-                            rhs=v_codes[a, q][:, lo : lo + width].bitcast(FP8X4),
-                            rhs_scale=v_scales(a, q * QUARTER + lo, width),
-                            start=(a == 0 and e == 0 and lo == 0),
-                            stop=(a == PASSES - 1 and e == 1 and lo + width == QUARTER),
-                        )
-            return bank[:].rearrange("p e j -> p j e")
 
         weights = {
             "w1": (
@@ -208,115 +205,137 @@ def tile_list_tracer_departure_blend_kernel(
                 lambda a, t: plane[:, a, W3_AT + P * t : W3_AT + P * (t + 1)],
             ),
         }
+        banks = {}
+
+        def multiply(weight, q, u, passes):
+            width, codes_of, scales_of = weights[weight]
+            if passes[0] == 0:
+                banks[weight, q, u] = psum.tile([P, 2, QUARTER], F32, name="bank")
+            for a in passes:
+                for e in range(2):
+                    for lo in range(0, QUARTER, width):
+                        nc.tensor.matmul_mx(
+                            out=banks[weight, q, u][:, e, lo : lo + width],
+                            lhsT=codes_of(a, 2 * u + e),
+                            lhsT_scale=scales_of(a, 2 * u + e),
+                            rhs=v_codes[a, q][:, lo : lo + width].bitcast(FP8X4),
+                            rhs_scale=v_scales(a, q * QUARTER + lo, width),
+                            start=(a == 0 and e == 0 and lo == 0),
+                            stop=(a == PASSES - 1 and e == 1 and lo + width == QUARTER),
+                        )
+
+        def sums(weight, q, u):
+            return banks[weight, q, u][:].rearrange("p e j -> p j e")
 
         out_rows = out.rearrange("(c p) j -> p c j", p=P)
         fraction = [held([P, 2, QUARTER, 2], F32, "fraction%d" % q) for q in range(QUARTERS)]
-        right_part = [held([P, 2, QUARTER, 2], F32, "right_part%d" % q) for q in range(QUARTERS)]
         left_part = [held([P, 2, QUARTER, 2], F32, "left_part%d" % q) for q in range(QUARTERS)]
-        blend = [held([P, QUARTER, 2, 2], BF16, "blend%d" % q) for q in range(QUARTERS)]
         h_codes = [held([P, QUARTER], U32, "h_codes%d" % q) for q in range(QUARTERS)]
         h_scales = [held([P, QUARTER], U8, "h_scales%d" % q) for q in range(QUARTERS)]
         result = [held([P, N_TILES, QUARTER], F32, "result%d" % q) for q in range(QUARTERS)]
+        right_part, h_rounded = {}, {}
 
-        def open_right(q, u):
-            passes("w1", q, u, (0,))
-            passes("w3", q, u, (0,))
+        def fraction_and_right(q, u, passes=(0, 1)):
+            multiply("w1", q, u, passes)
+            nc.scalar.activation(fraction[q][:, u, :, :], sums("w1", q, u), ACT.Sigmoid)
+            multiply("w3", q, u, passes)
 
-        def right_side(q, u, which=(0, 1)):
-            logit = passes("w1", q, u, which)
-            nc.scalar.activation(fraction[q][:, u, :, :], logit, ACT.Sigmoid)
-            right = passes("w3", q, u, which)
-            nc.vector.tensor_tensor(right_part[q][:, u, :, :], fraction[q][:, u, :, :], right, ALU.mult)
+        def weigh_right(q, u):
+            if u == 0:
+                tag = "fraction%d" % (q - 1) if q > 0 else "right_part0"
+                right_part[q] = held([P, 2, QUARTER, 2], F32, "right_part%d" % q, tag=tag)
+            nc.vector.tensor_tensor(right_part[q][:, u, :, :], fraction[q][:, u, :, :], sums("w3", q, u), ALU.mult)
 
-        def left_side(q, u):
-            left = passes("w2", q, u, (0, 1))
+        def weigh_left(q, u):
+            multiply("w2", q, u, (0, 1))
             nc.vector.scalar_tensor_tensor(
-                left_part[q][:, u, :, :], fraction[q][:, u, :, :], 1.0, left, ALU.subtract, ALU.mult
+                left_part[q][:, u, :, :], fraction[q][:, u, :, :], 1.0, sums("w2", q, u), ALU.subtract, ALU.mult
             )
 
-        def join(q, lo=0, hi=QUARTER, engine=nc.vector):
+        def join(engine, q, lo, hi):
+            if lo == 0:
+                tag = "rounded" if 0 < q < QUARTERS - 1 else "h_rounded%d" % q
+                h_rounded[q] = held([P, QUARTER, 2, 2], BF16, "h_rounded%d" % q, tag=tag)
             engine.tensor_tensor(
-                blend[q][:, lo:hi, :, :],
+                h_rounded[q][:, lo:hi, :, :],
                 right_part[q][:, :, lo:hi, :].rearrange("p u j e -> p j u e"),
                 left_part[q][:, :, lo:hi, :].rearrange("p u j e -> p j u e"),
                 ALU.subtract,
             )
 
-        def quantise_h(q, lo=0, hi=QUARTER):
+        def quantise_h(q, lo, hi):
             nc.vector.quantize_mx(
                 out=h_codes[q][:, lo:hi].bitcast(FP8X4),
                 scales=h_scales[q][:, lo:hi],
-                in_=blend[q][:, lo:hi, :, :].rearrange("p j u e -> p (j u e)"),
+                in_=h_rounded[q][:, lo:hi, :, :].rearrange("p j u e -> p (j u e)"),
             )
 
-        def tendencies(q, lo=0, hi=QUARTER, last=False):
+        def tendencies(q, lo, hi, share_with_vector=False):
             for first in range(0, N_TILES, 2):
                 bank = psum.tile([P, 2, QUARTER], F32, name="bank")
                 tiles = range(first, min(first + 2, N_TILES))
                 for c in tiles:
                     nc.tensor.matmul_mx(
                         out=bank[:, c - first, lo:hi],
-                        lhsT=w4_codes[:, P * c : P * (c + 1)].bitcast(FP8X4),
-                        lhsT_scale=w4_scales[:, P * c : P * (c + 1)],
+                        lhsT=second["w4_codes"][:, P * c : P * (c + 1)].bitcast(FP8X4),
+                        lhsT_scale=second["w4_scales"][:, P * c : P * (c + 1)],
                         rhs=h_codes[q][:, lo:hi].bitcast(FP8X4),
                         rhs_scale=h_scales[q][:, lo:hi],
                         start=True,
                         stop=True,
                     )
                 for c in tiles:
-                    if last and first > 0:
-                        nc.vector.tensor_scalar(
-                            result[q][:, c, lo:hi], bank[:, c - first, lo:hi], staged["late"][:, 4 * N + c : 4 * N + c + 1], None, ALU.add
-                        )
+                    dst, acc, bias = result[q][:, c, lo:hi], bank[:, c - first, lo:hi], second["src"][:, c : c + 1]
+                    if share_with_vector and first == 0:
+                        nc.vector.tensor_scalar(dst, acc, bias, None, ALU.add)
                     else:
-                        nc.scalar.activation(
-                            result[q][:, c, lo:hi], bank[:, c - first, lo:hi], ACT.Identity, bias=staged["late"][:, 4 * N + c : 4 * N + c + 1]
-                        )
+                        nc.scalar.activation(dst, acc, ACT.Identity, bias=bias)
             nc.sync.dma_start(out_rows[:, :, q * QUARTER + lo : q * QUARTER + hi], result[q][:, :, lo:hi])
 
-        open_right(0, 0)
-        open_right(0, 1)
-        gather_words(1, 0)
-        gather_words(1, 1)
-        gather_words(1, 2)
-        right_side(0, 0, (1,))
-        gather_words(1, 3)
-        load_w4()
-        right_side(0, 1, (1,))
-        round_w2(0, 0)
-        round_w2(1, 0)
-        right_side(1, 0)
-        round_w2(0, 1)
-        round_w2(1, 1)
-        quantise_w2(0)
-        quantise_w2(1)
-        right_side(1, 1)
-        right_side(2, 0)
-        right_side(2, 1)
+        round_w2(0, 0, nc.scalar.copy)
+        for u in range(2):
+            multiply("w1", 0, u, (0,))
+            multiply("w3", 0, u, (0,))
+        gather_words(1, 0, 1)
+        gather_words(1, 1, 1)
+        gather_words(1, 2, 2)
+        load_w4_and_src()
+        fraction_and_right(0, 0, (1,))
+        weigh_right(0, 0)
+        round_w2(0, 1, nc.scalar.copy)
+        fraction_and_right(0, 1, (1,))
+        round_w2(1, 0, nc.scalar.copy)
+        round_w2(1, 1, nc.vector.tensor_copy)
+        for a in range(PASSES):
+            quantise_w2(a)
+        weigh_right(0, 1)
+        for u in range(2):
+            fraction_and_right(1, u)
         round_w4()
-        left_side(0, 0)
-        left_side(0, 1)
-        right_side(3, 0)
-        join(0)
-        quantise_w4()
-        left_side(1, 0)
-        quantise_h(0)
-        left_side(1, 1)
-        right_side(3, 1)
-        tendencies(0)
-        join(1)
-        left_side(2, 0)
-        quantise_h(1)
-        left_side(2, 1)
-        tendencies(1)
-        left_side(3, 0)
-        join(2)
-        left_side(3, 1)
-        quantise_h(2)
-        join(3, 0, 128)
-        tendencies(2)
-        join(3, 128, 256)
-        quantise_h(3, 0, 128)
-        quantise_h(3, 128, 256)
-        tendencies(3, 0, 128)
-        tendencies(3, 128, 256, True)
+        for u in range(2):
+            weigh_left(0, u)
+
+        remaining = [(q, u) for q in range(2, QUARTERS) for u in range(2)]
+        for q in range(QUARTERS - 1):
+            join(nc.gpsimd, q, 0, QUARTER)
+            fraction_and_right(*remaining[q + min(q, 1)])
+            for u in range(2):
+                weigh_right(q + 1, u)
+            for u in range(2):
+                weigh_left(q + 1, u)
+            if q == 0:
+                fraction_and_right(*remaining[1])
+            else:
+                tendencies(q - 1, 0, QUARTER)
+            quantise_h(q, 0, QUARTER)
+            if q == 0:
+                quantise_w4()
+
+        last, middle = QUARTERS - 1, QUARTER // 2
+        join(nc.vector, last, 0, middle)
+        tendencies(last - 1, 0, QUARTER)
+        join(nc.vector, last, middle, QUARTER)
+        quantise_h(last, 0, middle)
+        quantise_h(last, middle, QUARTER)
+        tendencies(last, 0, middle)
+        tendencies(last, middle, QUARTER, share_with_vector=True)

@@ -75,10 +75,6 @@ def tile_list_tracer_departure_blend_kernel(
             nc.sync.dma_start(window[:], tab_words[a].rearrange("p t i -> p (t i)").bitcast(I32))
             word_window.append(window)
 
-        warm = held([P, 2], F32, "warm")
-        nc.vector.memset(warm[:, 0:1], 0.0)
-        nc.scalar.activation(warm[:, 1:2], warm[:, 0:1], ACT.Sigmoid)
-
         def gather_scales(half):
             picked = held([P, HALF], U8, "picked_scales%d" % half, tag="picked_scales")
             cols = slice(half * HALF // PER_COLUMN, (half + 1) * HALF // PER_COLUMN)

@@ -25,10 +25,18 @@ QUARTER = 256
 QUARTERS = S // QUARTER
 HALF = S // 2
 N_TILES = N // P
-W1_AT, W3_AT, V_AT, PLANE = 0, H, 2 * H, 2 * H + HALF
+V_AT, PLANE = H, H + HALF
 W4_SPLIT = 256
 SRC_AT = 4 * N
 SRC_PAD = 8
+PARTS_BYTES = 4 * 4 * 2 * QUARTER
+OVERLAP = 64
+ROUNDED_BYTES = PARTS_BYTES + 2 * OVERLAP
+ROUNDED_STEP = ROUNDED_BYTES - OVERLAP
+PARTS0_AT = QUARTERS * ROUNDED_STEP + OVERLAP
+RAW_W2_BYTES = 4 * 4 * H
+PICKED_AT = PARTS0_AT + 2 * PARTS_BYTES + RAW_W2_BYTES - OVERLAP
+RAW_W2_AT = (PICKED_AT + OVERLAP - RAW_W2_BYTES, PICKED_AT + 2 * HALF - 2 * OVERLAP)
 
 
 def tile_list_tracer_departure_blend_kernel(
@@ -38,6 +46,11 @@ def tile_list_tracer_departure_blend_kernel(
     with ExitStack() as ctx:
         keep = ctx.enter_context(tc.tile_pool(name="keep", bufs=1))
         psum = ctx.enter_context(tc.psum_pool(name="psum", bufs=BANKS))
+
+        chain = ctx.enter_context(tc.tile_pool(name="chain", bufs=1))
+
+        def placed(shape, dtype, name, at):
+            return chain.tile(shape, dtype, name=name, offset=at, align_bytes=64)
 
         def held(shape, dtype, name, tag=""):
             return keep.tile(shape, dtype, name=name, tag=tag or name, align_bytes=64)
@@ -58,71 +71,50 @@ def tile_list_tracer_departure_blend_kernel(
         for w, scales in enumerate((w1_scales, w3_scales)):
             nc.sync.dma_start(raw_scales[0:P:4, w, :], scales.bitcast(I32).rearrange("a q c -> q a c"))
 
-        plane = held([P, PASSES, PLANE], U8, "plane")
-        plane_words = plane[:].rearrange("p a s -> p (a s)").bitcast(I32)
-        nc.vector.memset(plane_words, 0)
-        late_plane = held([P, PASSES, HALF], U8, "late_plane")
-        late_plane_words = late_plane[:].rearrange("p a s -> p (a s)").bitcast(I32)
-        nc.vector.memset(late_plane_words, 0)
+        planes, plane_words = [], []
+        for half in range(2):
+            plane = held([P, PASSES, PLANE], U8, "plane%d" % half)
+            words = plane[:].rearrange("p a s -> p (a s)").bitcast(I32)
+            nc.vector.memset(words, 0)
+            planes.append(plane)
+            plane_words.append(words)
 
-        raw_w3 = held([P, PASSES, H], I32, "raw_w3")
-        nc.sync.dma_start(
-            raw_w3[:], w3_words.rearrange("a p c i -> a p (c i)").bitcast(I32).rearrange("a p c -> p a c")
-        )
         word_window = []
         for a in range(PASSES):
             window = held([P, T], I32, "word_window%d" % a)
             nc.sync.dma_start(window[:], tab_words[a].rearrange("p t i -> p (t i)").bitcast(I32))
             word_window.append(window)
 
-        def gather_scales(half):
-            picked = held([P, HALF], U8, "picked_scales%d" % half, tag="picked_scales")
+        raw_w2 = {}
+
+        def make_plane(half):
+            picked = placed([P, HALF], U8, "picked_scales%d" % half, PICKED_AT + half * (HALF - OVERLAP))
             cols = slice(half * HALF // PER_COLUMN, (half + 1) * HALF // PER_COLUMN)
             nc.vector.tensor_copy(picked[:], scale_window[:].indirect(offsets[:, cols]))
-            return picked[:].bitcast(I32)
-
-        def rows_to_plane(dst_words, src_words):
+            spread = held([P, PLANE // 4], I32, "spread%d" % half)
+            nc.vector.tensor_copy(
+                spread[:, : V_AT // 4].rearrange("p (t c) -> p t c", t=4),
+                raw_scales[:, half, :].rearrange("p (c t) -> p t c", t=4),
+            )
+            nc.vector.tensor_copy(spread[:, V_AT // 4 :], picked[:].bitcast(I32))
             for d in range(4):
-                nc.scalar.dma_start(dst_words[32 * d : 32 * d + 4, :], src_words[32 * d : 32 * d + 32 : 4, :])
+                nc.scalar.dma_start(plane_words[half][32 * d : 32 * d + 4, :], spread[32 * d : 32 * d + 32 : 4, :])
+            a = half
+            raw = placed([P, 4 * H], F32, "raw_w2_%d" % a, RAW_W2_AT[a])
+            raw_w2[a] = raw[:].rearrange("p (j r) -> p j r", j=4)
+            nc.sync.dma_start(raw_w2[a], w2[K_PASS * a : K_PASS * (a + 1), :].rearrange("(p j) r -> p j r", j=4))
 
-        first_picked = gather_scales(0)
-        spread = held([P, PLANE // 4], I32, "spread")
-        nc.vector.tensor_copy(
-            spread[:, : V_AT // 4].rearrange("p (w t c) -> p w t c", w=2, t=4),
-            raw_scales[:].rearrange("p w (c t) -> p w t c", t=4),
-        )
-        nc.vector.tensor_copy(spread[:, V_AT // 4 :], first_picked)
-        rows_to_plane(plane_words, spread[:])
-
-        w3_codes = held([P, PASSES, 4, P], I32, "w3_codes")
-        nc.vector.tensor_copy(
-            w3_codes[:].rearrange("p a t (c i) -> p a t c i", i=4),
-            raw_w3[:].rearrange("p a (c t i) -> p a t c i", t=4, i=4),
-        )
-
-        rows_to_plane(late_plane_words, gather_scales(1))
-
-        def v_scales(a, lo, width):
-            if lo < HALF:
-                return plane[:, a, V_AT + lo : V_AT + lo + width]
-            return late_plane[:, a, lo - HALF : lo - HALF + width]
-
+        make_plane(0)
         w1_codes = held([P, PASSES, 4, 2 * P], U8, "w1_codes")
         nc.vector.tensor_copy(
             w1_codes[:].bitcast(I32).rearrange("p a t (c i) -> p a t c i", i=2),
             raw_w1[:].rearrange("p a (c t i) -> p a t c i", t=4, i=2),
         )
+        make_plane(1)
 
-        raw_w2 = []
-
-        def load_w2(a, tag):
-            raw = held([P, 2, 4, H // 2], F32, "raw_w2_%d" % a, tag=tag)
-            for half in range(2):
-                rows = w2[K_PASS * a : K_PASS * (a + 1), H // 2 * half : H // 2 * (half + 1)]
-                nc.sync.dma_start(raw[:, half, :, :], rows.rearrange("(p j) r -> p j r", j=4))
-            raw_w2.append(raw)
-
-        load_w2(0, "raw_w3")
+        def v_scales(a, lo, width):
+            half = lo // HALF
+            return planes[half][:, a, V_AT + lo - half * HALF : V_AT + lo - half * HALF + width]
 
         v_codes = {}
 
@@ -133,50 +125,64 @@ def tile_list_tracer_departure_blend_kernel(
             for n in range(count):
                 v_codes[a, q + n] = picked[:, n * QUARTER : (n + 1) * QUARTER]
 
-        for q in range(0, QUARTERS, 2):
-            gather_words(0, q, 2)
-        load_w2(1, "word_window0")
+        for a in range(PASSES):
+            for q in range(2):
+                gather_words(a, q, 1)
+        gather_words(0, 2, 2)
+        raw_w3 = held([P, PASSES, H], I32, "raw_w3", tag="word_window0")
+        nc.sync.dma_start(
+            raw_w3[:], w3_words.rearrange("a p c i -> a p (c i)").bitcast(I32).rearrange("a p c -> p a c")
+        )
+        gather_words(1, 2, 2)
 
-        second = {}
+        raw4 = held([P, SRC_AT + SRC_PAD], F32, "raw_w4", tag="word_window1")
+        raw_w4 = raw4[:, :SRC_AT].rearrange("p (t n) -> p t n", t=4)
+        src_col = raw4[:, SRC_AT : SRC_AT + N_TILES]
+        w4_rows = w4.rearrange("(c t i) n -> t c i n", t=4, i=4)
+        for t in range(4):
+            nc.sync.dma_start(raw_w4[:, t, :], w4_rows[t])
+        with nc.allow_non_contiguous_dma(reason="one source value a partition"):
+            nc.sync.dma_start(src_col, src.rearrange("(c p) -> p c", p=P))
 
-        def load_w4_and_src():
-            raw = held([P, SRC_AT + SRC_PAD], F32, "raw_w4", tag="word_window1")
-            second["raw_w4"] = raw[:, :SRC_AT].rearrange("p (t n) -> p t n", t=4)
-            second["src"] = raw[:, SRC_AT : SRC_AT + N_TILES]
-            rows = w4.rearrange("(c t i) n -> t c i n", t=4, i=4)
-            for t in range(4):
-                nc.sync.dma_start(second["raw_w4"][:, t, :], rows[t])
-            with nc.allow_non_contiguous_dma(reason="one source value a partition"):
-                nc.sync.dma_start(second["src"], src.rearrange("(c p) -> p c", p=P))
+        w2_rounded, w2_codes, w2_scales = {}, {}, {}
+        for a in range(PASSES):
+            for u in range(2):
+                w2_rounded[a, u] = held([P, 2, 32, 4, 4], BF16, "w2_rounded%d_%d" % (a, u))
+                w2_codes[a, u] = held([P, 2 * P], U32, "w2_codes%d_%d" % (a, u))
+                w2_scales[a, u] = held([P, 2 * P], U8, "w2_scales%d_%d" % (a, u))
 
-        w2_rounded = [held([P, 4, 32, 4, 4], BF16, "w2_rounded%d" % a) for a in range(PASSES)]
-        w2_codes = [held([P, H], U32, "w2_codes%d" % a) for a in range(PASSES)]
-        w2_scales = [held([P, H], U8, "w2_scales%d" % a) for a in range(PASSES)]
+        def round_w2(a, u, copy):
+            rows = raw_w2[a].rearrange("p j (c t i) -> p t c j i", t=4, i=4)[:, 2 * u : 2 * u + 2]
+            copy(w2_rounded[a, u][:].rearrange("p t c i j -> p t c j i"), rows)
 
-        def round_w2(a, half, copy):
-            rows = raw_w2[a][:, half, :, :].rearrange("p j (c t i) -> p t c j i", t=4, i=4)
-            dst = w2_rounded[a][:, :, 16 * half : 16 * (half + 1), :, :].rearrange("p t c i j -> p t c j i")
-            for pair in range(2):
-                copy(dst[:, :, :, :, 2 * pair : 2 * pair + 2], rows[:, :, :, :, 2 * pair : 2 * pair + 2])
-
-        def quantise_w2(a):
+        def quantise_w2(a, u):
             nc.vector.quantize_mx(
-                out=w2_codes[a][:].bitcast(FP8X4),
-                scales=w2_scales[a][:],
-                in_=w2_rounded[a][:].rearrange("p t c i j -> p (t c i j)"),
+                out=w2_codes[a, u][:].bitcast(FP8X4),
+                scales=w2_scales[a, u][:],
+                in_=w2_rounded[a, u][:].rearrange("p t c i j -> p (t c i j)"),
             )
 
-        w4_rounded = held([P, N, 4], BF16, "w4_rounded", tag="rounded")
+        w3_codes = held([P, PASSES, 4, P], I32, "w3_codes")
+
+        def move_w3():
+            nc.vector.tensor_copy(
+                w3_codes[:].rearrange("p a t (c i) -> p a t c i", i=4),
+                raw_w3[:].rearrange("p a (c t i) -> p a t c i", t=4, i=4),
+            )
+
+        w4_rounded = held([P, N, 4], BF16, "w4_rounded")
 
         def round_w4():
             nc.scalar.copy(
-                w4_rounded[:].rearrange("p (n e) t -> p n t e", e=2),
-                second["raw_w4"].rearrange("p t (n e) -> p n t e", e=2),
+                w4_rounded[:].rearrange("p (n e) t -> p n t e", e=4),
+                raw_w4.rearrange("p t (n e) -> p n t e", e=4),
             )
 
+        second = {}
+
         def quantise_w4():
-            second["w4_codes"] = held([P, N], U32, "w4_codes", tag="right_part0")
-            second["w4_scales"] = held([P, N], U8, "w4_scales", tag="left_part0")
+            second["w4_codes"] = placed([P, N], U32, "w4_codes", PARTS0_AT)
+            second["w4_scales"] = placed([P, N], U8, "w4_scales", PARTS0_AT + 4 * N)
             for lo, hi in ((0, W4_SPLIT), (W4_SPLIT, N)):
                 nc.vector.quantize_mx(
                     out=second["w4_codes"][:, lo:hi].bitcast(FP8X4),
@@ -188,17 +194,17 @@ def tile_list_tracer_departure_blend_kernel(
             "w1": (
                 P,
                 lambda a, t: w1_codes[:, a, t, :].bitcast(FP4X4),
-                lambda a, t: plane[:, a, W1_AT + P * t : W1_AT + P * (t + 1)],
+                lambda a, t: planes[0][:, a, P * t : P * (t + 1)],
             ),
             "w2": (
                 QUARTER,
-                lambda a, t: w2_codes[a][:, P * t : P * (t + 1)].bitcast(FP8X4),
-                lambda a, t: w2_scales[a][:, P * t : P * (t + 1)],
+                lambda a, t: w2_codes[a, t // 2][:, P * (t % 2) : P * (t % 2 + 1)].bitcast(FP8X4),
+                lambda a, t: w2_scales[a, t // 2][:, P * (t % 2) : P * (t % 2 + 1)],
             ),
             "w3": (
                 QUARTER,
                 lambda a, t: w3_codes[:, a, t, :].bitcast(FP8X4),
-                lambda a, t: plane[:, a, W3_AT + P * t : W3_AT + P * (t + 1)],
+                lambda a, t: planes[1][:, a, P * t : P * (t + 1)],
             ),
         }
         banks = {}
@@ -225,37 +231,37 @@ def tile_list_tracer_departure_blend_kernel(
 
         out_rows = out.rearrange("(c p) j -> p c j", p=P)
         fraction = [held([P, 2, QUARTER, 2], F32, "fraction%d" % q) for q in range(QUARTERS)]
-        left_part = [held([P, 2, QUARTER, 2], F32, "left_part%d" % q) for q in range(QUARTERS)]
         h_codes = [held([P, QUARTER], U32, "h_codes%d" % q) for q in range(QUARTERS)]
         h_scales = [held([P, QUARTER], U8, "h_scales%d" % q) for q in range(QUARTERS)]
         result = [held([P, N_TILES, QUARTER], F32, "result%d" % q) for q in range(QUARTERS)]
-        right_part, h_rounded = {}, {}
+        parts, h_rounded = {}, {}
 
-        def fraction_and_right(q, u, passes=(0, 1)):
-            multiply("w1", q, u, passes)
+        def take_fraction(q, u):
             nc.scalar.activation(fraction[q][:, u, :, :], sums("w1", q, u), ACT.Sigmoid)
-            multiply("w3", q, u, passes)
 
-        def weigh_right(q, u):
-            if u == 0:
-                tag = "fraction%d" % (q - 1) if q > 0 else "right_part0"
-                right_part[q] = held([P, 2, QUARTER, 2], F32, "right_part%d" % q, tag=tag)
-            nc.vector.tensor_tensor(right_part[q][:, u, :, :], fraction[q][:, u, :, :], sums("w3", q, u), ALU.mult)
+        def products(q):
+            for weight in ("w2", "w3"):
+                for u in range(2):
+                    multiply(weight, q, u, (0, 1))
 
-        def weigh_left(q, u):
-            multiply("w2", q, u, (0, 1))
-            nc.vector.scalar_tensor_tensor(
-                left_part[q][:, u, :, :], fraction[q][:, u, :, :], 1.0, sums("w2", q, u), ALU.subtract, ALU.mult
-            )
+        def weigh(q):
+            at = PARTS0_AT + q * PARTS_BYTES if q < 2 else (q - 2) * ROUNDED_BYTES
+            parts[q] = placed([P, 2, 2, QUARTER, 2], F32, "parts%d" % q, at)
+            for u in range(2):
+                nc.vector.scalar_tensor_tensor(
+                    parts[q][:, 0, u, :, :], fraction[q][:, u, :, :], 1.0, sums("w2", q, u), ALU.subtract, ALU.mult
+                )
+            for u in range(2):
+                nc.vector.tensor_tensor(parts[q][:, 1, u, :, :], fraction[q][:, u, :, :], sums("w3", q, u), ALU.mult)
 
         def join(engine, q, lo, hi):
             if lo == 0:
-                tag = "rounded" if 0 < q < QUARTERS - 1 else "h_rounded%d" % q
-                h_rounded[q] = held([P, QUARTER, 2, 2], BF16, "h_rounded%d" % q, tag=tag)
+                padded = placed([P, ROUNDED_BYTES // 2], BF16, "h_rounded%d" % q, q * ROUNDED_STEP)
+                h_rounded[q] = padded[:, : 4 * QUARTER].rearrange("p (j u e) -> p j u e", u=2, e=2)
             engine.tensor_tensor(
                 h_rounded[q][:, lo:hi, :, :],
-                right_part[q][:, :, lo:hi, :].rearrange("p u j e -> p j u e"),
-                left_part[q][:, :, lo:hi, :].rearrange("p u j e -> p j u e"),
+                parts[q][:, 1, :, lo:hi, :].rearrange("p u j e -> p j u e"),
+                parts[q][:, 0, :, lo:hi, :].rearrange("p u j e -> p j u e"),
                 ALU.subtract,
             )
 
@@ -281,55 +287,48 @@ def tile_list_tracer_departure_blend_kernel(
                         stop=True,
                     )
                 for c in tiles:
-                    dst, acc, bias = result[q][:, c, lo:hi], bank[:, c - first, lo:hi], second["src"][:, c : c + 1]
+                    dst, acc, bias = result[q][:, c, lo:hi], bank[:, c - first, lo:hi], src_col[:, c : c + 1]
                     if share_with_vector and first == 0:
                         nc.vector.tensor_scalar(dst, acc, bias, None, ALU.add)
                     else:
                         nc.scalar.activation(dst, acc, ACT.Identity, bias=bias)
             nc.sync.dma_start(out_rows[:, :, q * QUARTER + lo : q * QUARTER + hi], result[q][:, :, lo:hi])
 
-        round_w2(0, 0, nc.scalar.copy)
-        for u in range(2):
-            multiply("w1", 0, u, (0,))
-            multiply("w3", 0, u, (0,))
-        gather_words(1, 0, 1)
-        gather_words(1, 1, 1)
-        gather_words(1, 2, 2)
-        load_w4_and_src()
-        fraction_and_right(0, 0, (1,))
-        weigh_right(0, 0)
-        round_w2(0, 1, nc.scalar.copy)
-        fraction_and_right(0, 1, (1,))
-        round_w2(1, 0, nc.scalar.copy)
-        round_w2(1, 1, nc.vector.tensor_copy)
         for a in range(PASSES):
-            quantise_w2(a)
-        weigh_right(0, 1)
+            for q in range(2):
+                for u in range(2):
+                    multiply("w1", q, u, (a,))
         for u in range(2):
-            fraction_and_right(1, u)
+            round_w2(0, u, nc.scalar.copy)
+        for q in range(2, QUARTERS):
+            for u in range(2):
+                multiply("w1", q, u, (0, 1))
+        for q in range(QUARTERS):
+            for u in range(2):
+                take_fraction(q, u)
+        for u in range(2):
+            quantise_w2(0, u)
+            round_w2(1, u, nc.vector.tensor_copy)
+        for u in range(2):
+            quantise_w2(1, u)
+        move_w3()
         round_w4()
-        for u in range(2):
-            weigh_left(0, u)
-
-        remaining = [(q, u) for q in range(2, QUARTERS) for u in range(2)]
-        for q in range(QUARTERS - 1):
-            join(nc.gpsimd, q, 0, QUARTER)
-            fraction_and_right(*remaining[q + min(q, 1)])
-            for u in range(2):
-                weigh_right(q + 1, u)
-            for u in range(2):
-                weigh_left(q + 1, u)
-            if q == 0:
-                fraction_and_right(*remaining[1])
-            else:
-                tendencies(q - 1, 0, QUARTER)
-            quantise_h(q, 0, QUARTER)
-            if q == 0:
-                quantise_w4()
+        products(0)
+        products(1)
+        weigh(0)
 
         last, middle = QUARTERS - 1, QUARTER // 2
+        for q in range(last):
+            join(nc.gpsimd, q, 0, QUARTER)
+            weigh(q + 1)
+            if q + 2 < QUARTERS:
+                products(q + 2)
+            if q == 0:
+                quantise_w4()
+            quantise_h(q, 0, QUARTER)
+            tendencies(q, 0, QUARTER)
+
         join(nc.vector, last, 0, middle)
-        tendencies(last - 1, 0, QUARTER)
         join(nc.vector, last, middle, QUARTER)
         quantise_h(last, 0, middle)
         quantise_h(last, middle, QUARTER)

@@ -29,14 +29,20 @@ V_AT, PLANE = H, H + HALF
 W4_SPLIT = 256
 SRC_AT = 4 * N
 SRC_PAD = 8
+PAIR_OF = {"w1": (0, 1, 2, 0), "w2": (3, 3, 2, 0), "w3": (0, 1, 3, 2)}
+OUT_PAIR = {(0, 0): 1, (1, 0): 3, (2, 0): 1, (3, 0): 0, (3, QUARTER // 2): 2}
 PARTS_BYTES = 4 * 4 * 2 * QUARTER
 OVERLAP = 64
 ROUNDED_BYTES = PARTS_BYTES + 2 * OVERLAP
 ROUNDED_STEP = ROUNDED_BYTES - OVERLAP
 PARTS0_AT = QUARTERS * ROUNDED_STEP + OVERLAP
 RAW_W2_BYTES = 4 * 4 * H
-PICKED_AT = PARTS0_AT + 2 * PARTS_BYTES + RAW_W2_BYTES - OVERLAP
-RAW_W2_AT = (PICKED_AT + OVERLAP - RAW_W2_BYTES, PICKED_AT + 2 * HALF - 2 * OVERLAP)
+FRACTION_BYTES = 4 * 4 * QUARTER
+W1_CODES_AT = PARTS0_AT + 2 * PARTS_BYTES
+PICKED_AT = W1_CODES_AT + PASSES * 2 * H - OVERLAP
+RAW_W2_1_AT = PICKED_AT + 2 * HALF - 2 * OVERLAP
+RAW_W2_AT = (RAW_W2_1_AT + 3 * FRACTION_BYTES, RAW_W2_1_AT)
+FRACTION_AT = [RAW_W2_AT[0]] + [RAW_W2_AT[1] + n * FRACTION_BYTES for n in range(QUARTERS - 1)]
 
 
 def tile_list_tracer_departure_blend_kernel(
@@ -45,7 +51,7 @@ def tile_list_tracer_departure_blend_kernel(
     nc = tc.nc
     with ExitStack() as ctx:
         keep = ctx.enter_context(tc.tile_pool(name="keep", bufs=1))
-        psum = ctx.enter_context(tc.psum_pool(name="psum", bufs=BANKS))
+        psum = ctx.enter_context(tc.psum_pool(name="psum", bufs=1))
 
         chain = ctx.enter_context(tc.tile_pool(name="chain", bufs=1))
 
@@ -71,6 +77,10 @@ def tile_list_tracer_departure_blend_kernel(
         for w, scales in enumerate((w1_scales, w3_scales)):
             nc.sync.dma_start(raw_scales[0:P:4, w, :], scales.bitcast(I32).rearrange("a q c -> q a c"))
 
+        warm = held([P, 16], F32, "warm")
+        nc.vector.memset(warm[:, 0:8], 0.0)
+        nc.scalar.activation(warm[:, 8:9], warm[:, 0:1], ACT.Sigmoid)
+
         planes, plane_words = [], []
         for half in range(2):
             plane = held([P, PASSES, PLANE], U8, "plane%d" % half)
@@ -79,13 +89,18 @@ def tile_list_tracer_departure_blend_kernel(
             planes.append(plane)
             plane_words.append(words)
 
-        word_window = []
-        for a in range(PASSES):
-            window = held([P, T], I32, "word_window%d" % a)
-            nc.sync.dma_start(window[:], tab_words[a].rearrange("p t i -> p (t i)").bitcast(I32))
-            word_window.append(window)
+        word_window, raw_w2 = {}, {}
 
-        raw_w2 = {}
+        def load_words(a, window):
+            nc.sync.dma_start(window[:], tab_words[a].rearrange("p t i -> p (t i)").bitcast(I32))
+            word_window[a] = window
+
+        def load_w2(a, raw):
+            raw_w2[a] = raw[:, : 4 * H].rearrange("p (j r) -> p j r", j=4)
+            nc.sync.dma_start(raw_w2[a], w2[K_PASS * a : K_PASS * (a + 1), :].rearrange("(p j) r -> p j r", j=4))
+
+        load_words(0, held([P, T], I32, "word_window0"))
+        load_w2(0, placed([P, 4 * H], F32, "raw_w2_0", RAW_W2_AT[0]))
 
         def make_plane(half):
             picked = placed([P, HALF], U8, "picked_scales%d" % half, PICKED_AT + half * (HALF - OVERLAP))
@@ -97,20 +112,19 @@ def tile_list_tracer_departure_blend_kernel(
                 raw_scales[:, half, :].rearrange("p (c t) -> p t c", t=4),
             )
             nc.vector.tensor_copy(spread[:, V_AT // 4 :], picked[:].bitcast(I32))
+            queue = nc.sync if half else nc.scalar
             for d in range(4):
-                nc.scalar.dma_start(plane_words[half][32 * d : 32 * d + 4, :], spread[32 * d : 32 * d + 32 : 4, :])
-            a = half
-            raw = placed([P, 4 * H], F32, "raw_w2_%d" % a, RAW_W2_AT[a])
-            raw_w2[a] = raw[:].rearrange("p (j r) -> p j r", j=4)
-            nc.sync.dma_start(raw_w2[a], w2[K_PASS * a : K_PASS * (a + 1), :].rearrange("(p j) r -> p j r", j=4))
+                queue.dma_start(plane_words[half][32 * d : 32 * d + 4, :], spread[32 * d : 32 * d + 32 : 4, :])
 
         make_plane(0)
-        w1_codes = held([P, PASSES, 4, 2 * P], U8, "w1_codes")
+        w1_codes = placed([P, PASSES, 4, 2 * P], U8, "w1_codes", W1_CODES_AT)
         nc.vector.tensor_copy(
             w1_codes[:].bitcast(I32).rearrange("p a t (c i) -> p a t c i", i=2),
             raw_w1[:].rearrange("p a (c t i) -> p a t c i", t=4, i=2),
         )
+        load_words(1, held([P, T], I32, "word_window1", tag="raw_w1"))
         make_plane(1)
+        load_w2(1, placed([P, 3 * FRACTION_BYTES // 4], F32, "raw_w2_1", RAW_W2_AT[1]))
 
         def v_scales(a, lo, width):
             half = lo // HALF
@@ -118,24 +132,25 @@ def tile_list_tracer_departure_blend_kernel(
 
         v_codes = {}
 
-        def gather_words(a, q, count):
-            picked = held([P, count * QUARTER], U32, "v_codes_%d_%d" % (a, q))
+        def gather_words(a, q, count, tag=""):
+            picked = held([P, count * QUARTER], U32, "v_codes_%d_%d" % (a, q), tag=tag)
             cols = slice(q * QUARTER // PER_COLUMN, (q + count) * QUARTER // PER_COLUMN)
             nc.vector.tensor_copy(picked[:], word_window[a][:].bitcast(U32).indirect(offsets[:, cols]))
             for n in range(count):
                 v_codes[a, q + n] = picked[:, n * QUARTER : (n + 1) * QUARTER]
 
-        for a in range(PASSES):
-            for q in range(2):
-                gather_words(a, q, 1)
+        gather_words(0, 0, 1)
+        gather_words(0, 1, 1)
         gather_words(0, 2, 2)
         raw_w3 = held([P, PASSES, H], I32, "raw_w3", tag="word_window0")
         nc.sync.dma_start(
             raw_w3[:], w3_words.rearrange("a p c i -> a p (c i)").bitcast(I32).rearrange("a p c -> p a c")
         )
-        gather_words(1, 2, 2)
+        gather_words(1, 0, 1)
+        gather_words(1, 1, 1)
+        gather_words(1, 2, 1)
 
-        raw4 = held([P, SRC_AT + SRC_PAD], F32, "raw_w4", tag="word_window1")
+        raw4 = placed([P, SRC_AT + SRC_PAD], F32, "raw_w4", RAW_W2_AT[0] + RAW_W2_BYTES - OVERLAP)
         raw_w4 = raw4[:, :SRC_AT].rearrange("p (t n) -> p t n", t=4)
         src_col = raw4[:, SRC_AT : SRC_AT + N_TILES]
         w4_rows = w4.rearrange("(c t i) n -> t c i n", t=4, i=4)
@@ -153,7 +168,9 @@ def tile_list_tracer_departure_blend_kernel(
 
         def round_w2(a, u, copy):
             rows = raw_w2[a].rearrange("p j (c t i) -> p t c j i", t=4, i=4)[:, 2 * u : 2 * u + 2]
-            copy(w2_rounded[a, u][:].rearrange("p t c i j -> p t c j i"), rows)
+            dst = w2_rounded[a, u][:].rearrange("p t c i j -> p t c j i")
+            for pair in range(2):
+                copy(dst[:, :, :, :, 2 * pair : 2 * pair + 2], rows[:, :, :, :, 2 * pair : 2 * pair + 2])
 
         def quantise_w2(a, u):
             nc.vector.quantize_mx(
@@ -174,15 +191,15 @@ def tile_list_tracer_departure_blend_kernel(
 
         def round_w4():
             nc.scalar.copy(
-                w4_rounded[:].rearrange("p (n e) t -> p n t e", e=4),
-                raw_w4.rearrange("p t (n e) -> p n t e", e=4),
+                w4_rounded[:].rearrange("p (n e) t -> p n t e", e=2),
+                raw_w4.rearrange("p t (n e) -> p n t e", e=2),
             )
 
         second = {}
 
         def quantise_w4():
             second["w4_codes"] = placed([P, N], U32, "w4_codes", PARTS0_AT)
-            second["w4_scales"] = placed([P, N], U8, "w4_scales", PARTS0_AT + 4 * N)
+            second["w4_scales"] = placed([P, N], U8, "w4_scales", FRACTION_AT[1] + FRACTION_BYTES // 2)
             for lo, hi in ((0, W4_SPLIT), (W4_SPLIT, N)):
                 nc.vector.quantize_mx(
                     out=second["w4_codes"][:, lo:hi].bitcast(FP8X4),
@@ -209,10 +226,13 @@ def tile_list_tracer_departure_blend_kernel(
         }
         banks = {}
 
+        def bank_tile(pair, u):
+            return psum.tile([P, 2, QUARTER], F32, name="bank", tag="bank%d" % (2 * pair + u))
+
         def multiply(weight, q, u, passes):
             width, codes_of, scales_of = weights[weight]
             if passes[0] == 0:
-                banks[weight, q, u] = psum.tile([P, 2, QUARTER], F32, name="bank")
+                banks[weight, q, u] = bank_tile(PAIR_OF[weight][q], u)
             for a in passes:
                 for e in range(2):
                     for lo in range(0, QUARTER, width):
@@ -230,19 +250,20 @@ def tile_list_tracer_departure_blend_kernel(
             return banks[weight, q, u][:].rearrange("p e j -> p j e")
 
         out_rows = out.rearrange("(c p) j -> p c j", p=P)
-        fraction = [held([P, 2, QUARTER, 2], F32, "fraction%d" % q) for q in range(QUARTERS)]
-        h_codes = [held([P, QUARTER], U32, "h_codes%d" % q) for q in range(QUARTERS)]
-        h_scales = [held([P, QUARTER], U8, "h_scales%d" % q) for q in range(QUARTERS)]
+        fraction = {}
+        h_codes, h_scales = {}, {}
         result = [held([P, N_TILES, QUARTER], F32, "result%d" % q) for q in range(QUARTERS)]
         parts, h_rounded = {}, {}
 
         def take_fraction(q, u):
+            if u == 0:
+                shape = [P, 2, QUARTER, 2]
+                fraction[q] = placed(shape, F32, "fraction%d" % q, FRACTION_AT[q])
             nc.scalar.activation(fraction[q][:, u, :, :], sums("w1", q, u), ACT.Sigmoid)
 
-        def products(q):
-            for weight in ("w2", "w3"):
-                for u in range(2):
-                    multiply(weight, q, u, (0, 1))
+        def product(weight, q):
+            for u in range(2):
+                multiply(weight, q, u, (0, 1))
 
         def weigh(q):
             at = PARTS0_AT + q * PARTS_BYTES if q < 2 else (q - 2) * ROUNDED_BYTES
@@ -266,6 +287,10 @@ def tile_list_tracer_departure_blend_kernel(
             )
 
         def quantise_h(q, lo, hi):
+            if lo == 0:
+                at = FRACTION_AT[(q + 1) % QUARTERS]
+                h_codes[q] = placed([P, QUARTER], U32, "h_codes%d" % q, at)
+                h_scales[q] = placed([P, QUARTER], U8, "h_scales%d" % q, at + 4 * QUARTER)
             nc.vector.quantize_mx(
                 out=h_codes[q][:, lo:hi].bitcast(FP8X4),
                 scales=h_scales[q][:, lo:hi],
@@ -274,7 +299,7 @@ def tile_list_tracer_departure_blend_kernel(
 
         def tendencies(q, lo, hi, share_with_vector=False):
             for first in range(0, N_TILES, 2):
-                bank = psum.tile([P, 2, QUARTER], F32, name="bank")
+                bank = bank_tile(OUT_PAIR[q, lo], first // 2)
                 tiles = range(first, min(first + 2, N_TILES))
                 for c in tiles:
                     nc.tensor.matmul_mx(
@@ -294,35 +319,39 @@ def tile_list_tracer_departure_blend_kernel(
                         nc.scalar.activation(dst, acc, ACT.Identity, bias=bias)
             nc.sync.dma_start(out_rows[:, :, q * QUARTER + lo : q * QUARTER + hi], result[q][:, :, lo:hi])
 
+        last, middle = QUARTERS - 1, QUARTER // 2
         for a in range(PASSES):
-            for q in range(2):
+            for q in range(last):
                 for u in range(2):
                     multiply("w1", q, u, (a,))
         for u in range(2):
             round_w2(0, u, nc.scalar.copy)
-        for q in range(2, QUARTERS):
-            for u in range(2):
-                multiply("w1", q, u, (0, 1))
-        for q in range(QUARTERS):
+            quantise_w2(0, u)
+        round_w2(1, 0, nc.scalar.copy)
+        round_w2(1, 1, nc.vector.tensor_copy)
+        for q in range(last):
             for u in range(2):
                 take_fraction(q, u)
-        for u in range(2):
-            quantise_w2(0, u)
-            round_w2(1, u, nc.vector.tensor_copy)
-        for u in range(2):
-            quantise_w2(1, u)
+        quantise_w2(1, 1)
         move_w3()
+        quantise_w2(1, 0)
+        gather_words(1, last, 1, tag="w2_rounded1_0")
+        product("w2", 0)
+        product("w3", 0)
         round_w4()
-        products(0)
-        products(1)
         weigh(0)
+        product("w2", 1)
+        product("w3", 1)
+        product("w1", last)
+        for u in range(2):
+            take_fraction(last, u)
 
-        last, middle = QUARTERS - 1, QUARTER // 2
         for q in range(last):
             join(nc.gpsimd, q, 0, QUARTER)
             weigh(q + 1)
             if q + 2 < QUARTERS:
-                products(q + 2)
+                product("w2", q + 2)
+                product("w3", q + 2)
             if q == 0:
                 quantise_w4()
             quantise_h(q, 0, QUARTER)

@@ -25,12 +25,12 @@ QUARTER = 256
 QUARTERS = S // QUARTER
 HALF = S // 2
 N_TILES = N // P
-V_AT, PLANE = H, H + HALF
+W1_AT, W3_AT, V_AT, PLANE = 0, H, 2 * H, 2 * H + S
 W4_SPLIT = 256
 SRC_AT = 4 * N
 SRC_PAD = 8
-PAIR_OF = {"w1": (0, 1, 2, 0), "w2": (3, 3, 2, 0), "w3": (0, 1, 3, 2)}
-OUT_PAIR = {(0, 0): 1, (1, 0): 3, (2, 0): 1, (3, 0): 0, (3, QUARTER // 2): 2}
+PAIR_OF = {"w3": (0, 2, 0, 3), "w2": (1, 3, 1, 0)}
+OUT_PAIR = {(0, 0): 2, (1, 0): 1, (2, 0): 2, (3, 0): 3, (3, QUARTER // 2): 0}
 PARTS_BYTES = 4 * 4 * 2 * QUARTER
 OVERLAP = 64
 ROUNDED_BYTES = PARTS_BYTES + 2 * OVERLAP
@@ -40,9 +40,15 @@ RAW_W2_BYTES = 4 * 4 * H
 FRACTION_BYTES = 4 * 4 * QUARTER
 W1_CODES_AT = PARTS0_AT + 2 * PARTS_BYTES
 PICKED_AT = W1_CODES_AT + PASSES * 2 * H - OVERLAP
-RAW_W2_1_AT = PICKED_AT + 2 * HALF - 2 * OVERLAP
-RAW_W2_AT = (RAW_W2_1_AT + 3 * FRACTION_BYTES, RAW_W2_1_AT)
-FRACTION_AT = [RAW_W2_AT[0]] + [RAW_W2_AT[1] + n * FRACTION_BYTES for n in range(QUARTERS - 1)]
+PICKED_BYTES = 4 * HALF + 2 * OVERLAP
+V0_AT = (PICKED_AT + OVERLAP, PICKED_AT + OVERLAP + 4 * HALF)
+WINDOW1_AT = V0_AT[1] + 4 * HALF
+RAW_W1_AT = WINDOW1_AT + 4 * T - OVERLAP
+ROUNDED_W2_BYTES = 2 * 2 * H
+RAW_W1_BYTES = 2 * ROUNDED_W2_BYTES + 2 * OVERLAP
+RAW_W2_1_AT = RAW_W1_AT + RAW_W1_BYTES - OVERLAP
+RAW_W2_AT = (RAW_W2_1_AT + RAW_W2_BYTES, RAW_W2_1_AT)
+FRACTION_AT = [RAW_W2_AT[q // 2] + q % 2 * FRACTION_BYTES for q in range(QUARTERS)]
 
 
 def tile_list_tracer_departure_blend_kernel(
@@ -64,30 +70,29 @@ def tile_list_tracer_departure_blend_kernel(
         offsets = keep.tile([P, S // PER_COLUMN], U16, name="offsets")
         nc.sync.dma_start(offsets[:], offs)
 
-        raw_w1 = held([P, PASSES, H // 2], I32, "raw_w1")
-        nc.sync.dma_start(raw_w1[:], w1_words.bitcast(I32).rearrange("a p c -> p a c"))
+        padded_w1 = placed([P, RAW_W1_BYTES // 4], I32, "raw_w1", RAW_W1_AT)
+        raw_w1 = padded_w1[:, :H].rearrange("p (a c) -> p a c", a=PASSES)
+        nc.sync.dma_start(raw_w1, w1_words.bitcast(I32).rearrange("a p c -> p a c"))
 
         scale_window = held([P, T], U8, "scale_window")
         nc.vector.memset(scale_window[:].bitcast(I32), 0)
         nc.sync.dma_start(
             scale_window[:].bitcast(I32)[0:P:4, :], tab_scales.bitcast(I32).rearrange("a q t -> q a t")
         )
-        raw_scales = held([P, 2, H // 4], I32, "raw_scales")
-        nc.vector.memset(raw_scales[:], 0)
+        raw_scales = []
         for w, scales in enumerate((w1_scales, w3_scales)):
-            nc.sync.dma_start(raw_scales[0:P:4, w, :], scales.bitcast(I32).rearrange("a q c -> q a c"))
+            raw = held([P, H // 4], I32, "raw_scales%d" % w)
+            nc.vector.memset(raw[:], 0)
+            nc.sync.dma_start(raw[0:P:4, :], scales.bitcast(I32).rearrange("a q c -> q a c"))
+            raw_scales.append(raw)
 
         warm = held([P, 16], F32, "warm")
         nc.vector.memset(warm[:, 0:8], 0.0)
         nc.scalar.activation(warm[:, 8:9], warm[:, 0:1], ACT.Sigmoid)
 
-        planes, plane_words = [], []
-        for half in range(2):
-            plane = held([P, PASSES, PLANE], U8, "plane%d" % half)
-            words = plane[:].rearrange("p a s -> p (a s)").bitcast(I32)
-            nc.vector.memset(words, 0)
-            planes.append(plane)
-            plane_words.append(words)
+        plane = held([P, PASSES, PLANE], U8, "plane")
+        plane_words = plane[:].rearrange("p a s -> p (a s)").bitcast(I32)
+        nc.vector.memset(plane_words, 0)
 
         word_window, raw_w2 = {}, {}
 
@@ -100,57 +105,58 @@ def tile_list_tracer_departure_blend_kernel(
             nc.sync.dma_start(raw_w2[a], w2[K_PASS * a : K_PASS * (a + 1), :].rearrange("(p j) r -> p j r", j=4))
 
         load_words(0, held([P, T], I32, "word_window0"))
-        load_w2(0, placed([P, 4 * H], F32, "raw_w2_0", RAW_W2_AT[0]))
+        load_w2(0, placed([P, 4 * H + OVERLAP // 4], F32, "raw_w2_0", RAW_W2_AT[0]))
 
-        def make_plane(half):
-            picked = placed([P, HALF], U8, "picked_scales%d" % half, PICKED_AT + half * (HALF - OVERLAP))
-            cols = slice(half * HALF // PER_COLUMN, (half + 1) * HALF // PER_COLUMN)
-            nc.vector.tensor_copy(picked[:], scale_window[:].indirect(offsets[:, cols]))
-            spread = held([P, PLANE // 4], I32, "spread%d" % half)
-            nc.vector.tensor_copy(
-                spread[:, : V_AT // 4].rearrange("p (t c) -> p t c", t=4),
-                raw_scales[:, half, :].rearrange("p (c t) -> p t c", t=4),
-            )
-            nc.vector.tensor_copy(spread[:, V_AT // 4 :], picked[:].bitcast(I32))
-            queue = nc.sync if half else nc.scalar
-            for d in range(4):
-                queue.dma_start(plane_words[half][32 * d : 32 * d + 4, :], spread[32 * d : 32 * d + 32 : 4, :])
-
-        make_plane(0)
-        w1_codes = placed([P, PASSES, 4, 2 * P], U8, "w1_codes", W1_CODES_AT)
-        nc.vector.tensor_copy(
-            w1_codes[:].bitcast(I32).rearrange("p a t (c i) -> p a t c i", i=2),
-            raw_w1[:].rearrange("p a (c t i) -> p a t c i", t=4, i=2),
-        )
-        load_words(1, held([P, T], I32, "word_window1", tag="raw_w1"))
-        make_plane(1)
-        load_w2(1, placed([P, 3 * FRACTION_BYTES // 4], F32, "raw_w2_1", RAW_W2_AT[1]))
-
-        def v_scales(a, lo, width):
-            half = lo // HALF
-            return planes[half][:, a, V_AT + lo - half * HALF : V_AT + lo - half * HALF + width]
-
-        v_codes = {}
-
-        def gather_words(a, q, count, tag=""):
-            picked = held([P, count * QUARTER], U32, "v_codes_%d_%d" % (a, q), tag=tag)
-            cols = slice(q * QUARTER // PER_COLUMN, (q + count) * QUARTER // PER_COLUMN)
-            nc.vector.tensor_copy(picked[:], word_window[a][:].bitcast(U32).indirect(offsets[:, cols]))
-            for n in range(count):
-                v_codes[a, q + n] = picked[:, n * QUARTER : (n + 1) * QUARTER]
-
-        gather_words(0, 0, 1)
-        gather_words(0, 1, 1)
-        gather_words(0, 2, 2)
-        raw_w3 = held([P, PASSES, H], I32, "raw_w3", tag="word_window0")
+        raw_w3 = held([P, PASSES, H], I32, "raw_w3")
         nc.sync.dma_start(
             raw_w3[:], w3_words.rearrange("a p c i -> a p (c i)").bitcast(I32).rearrange("a p c -> p a c")
         )
-        gather_words(1, 0, 1)
-        gather_words(1, 1, 1)
-        gather_words(1, 2, 1)
 
-        raw4 = placed([P, SRC_AT + SRC_PAD], F32, "raw_w4", RAW_W2_AT[0] + RAW_W2_BYTES - OVERLAP)
+        picked = placed([P, PICKED_BYTES], U8, "picked_scales", PICKED_AT)[:, :S]
+        nc.vector.tensor_copy(picked, scale_window[:].indirect(offsets[:]))
+        spread = held([P, PLANE // 4], I32, "spread")
+        for w, raw in enumerate(raw_scales):
+            nc.vector.tensor_copy(
+                spread[:, w * H // 4 : (w + 1) * H // 4].rearrange("p (t c) -> p t c", t=4),
+                raw[:].rearrange("p (c t) -> p t c", t=4),
+            )
+        nc.vector.tensor_copy(spread[:, V_AT // 4 :], picked.bitcast(I32))
+        for d in range(4):
+            nc.sync.dma_start(plane_words[32 * d : 32 * d + 4, :], spread[32 * d : 32 * d + 32 : 4, :])
+
+        w1_codes = placed([P, PASSES, 4, 2 * P], U8, "w1_codes", W1_CODES_AT)
+        nc.vector.tensor_copy(
+            w1_codes[:].bitcast(I32).rearrange("p a t (c i) -> p a t c i", i=2),
+            raw_w1.rearrange("p a (c t i) -> p a t c i", t=4, i=2),
+        )
+        load_words(1, placed([P, T], I32, "word_window1", WINDOW1_AT))
+        load_w2(1, placed([P, 4 * H], F32, "raw_w2_1", RAW_W2_AT[1]))
+
+        def v_scales(a, lo, width):
+            return plane[:, a, V_AT + lo : V_AT + lo + width]
+
+        v_codes, v_halves = {}, {}
+
+        def gather_words(a, q, count, tag=""):
+            shape, name = [P, count * QUARTER], "v_codes_%d_%d" % (a, q)
+            picked = placed(shape, U32, name, V0_AT[q // 2]) if a == 0 else held(shape, U32, name)
+            cols = slice(q * QUARTER // PER_COLUMN, (q + count) * QUARTER // PER_COLUMN)
+            nc.vector.tensor_copy(picked[:], word_window[a][:].bitcast(U32).indirect(offsets[:, cols]))
+            v_halves[a, q // 2] = picked
+            for n in range(count):
+                v_codes[a, q + n] = picked[:, n * QUARTER : (n + 1) * QUARTER]
+
+        gather_words(0, 0, 2)
+        gather_words(0, 2, 2)
+        w3_codes = held([P, PASSES, 4, P], I32, "w3_codes", tag="word_window0")
+        nc.vector.tensor_copy(
+            w3_codes[:].rearrange("p a t (c i) -> p a t c i", i=4),
+            raw_w3[:].rearrange("p a (c t i) -> p a t c i", t=4, i=4),
+        )
+        gather_words(1, 0, 2)
+        gather_words(1, 2, 2)
+
+        raw4 = placed([P, SRC_AT + SRC_PAD], F32, "raw_w4", RAW_W2_AT[0] + RAW_W2_BYTES)
         raw_w4 = raw4[:, :SRC_AT].rearrange("p (t n) -> p t n", t=4)
         src_col = raw4[:, SRC_AT : SRC_AT + N_TILES]
         w4_rows = w4.rearrange("(c t i) n -> t c i n", t=4, i=4)
@@ -162,7 +168,9 @@ def tile_list_tracer_departure_blend_kernel(
         w2_rounded, w2_codes, w2_scales = {}, {}, {}
         for a in range(PASSES):
             for u in range(2):
-                w2_rounded[a, u] = held([P, 2, 32, 4, 4], BF16, "w2_rounded%d_%d" % (a, u))
+                shape, name = [P, 2, 32, 4, 4], "w2_rounded%d_%d" % (a, u)
+                at = RAW_W1_AT + OVERLAP + u * ROUNDED_W2_BYTES
+                w2_rounded[a, u] = placed(shape, BF16, name, at) if a == 0 else held(shape, BF16, name)
                 w2_codes[a, u] = held([P, 2 * P], U32, "w2_codes%d_%d" % (a, u))
                 w2_scales[a, u] = held([P, 2 * P], U8, "w2_scales%d_%d" % (a, u))
 
@@ -177,14 +185,6 @@ def tile_list_tracer_departure_blend_kernel(
                 out=w2_codes[a, u][:].bitcast(FP8X4),
                 scales=w2_scales[a, u][:],
                 in_=w2_rounded[a, u][:].rearrange("p t c i j -> p (t c i j)"),
-            )
-
-        w3_codes = held([P, PASSES, 4, P], I32, "w3_codes")
-
-        def move_w3():
-            nc.vector.tensor_copy(
-                w3_codes[:].rearrange("p a t (c i) -> p a t c i", i=4),
-                raw_w3[:].rearrange("p a (c t i) -> p a t c i", t=4, i=4),
             )
 
         w4_rounded = held([P, N, 4], BF16, "w4_rounded")
@@ -211,7 +211,7 @@ def tile_list_tracer_departure_blend_kernel(
             "w1": (
                 P,
                 lambda a, t: w1_codes[:, a, t, :].bitcast(FP4X4),
-                lambda a, t: planes[0][:, a, P * t : P * (t + 1)],
+                lambda a, t: plane[:, a, W1_AT + P * t : W1_AT + P * (t + 1)],
             ),
             "w2": (
                 QUARTER,
@@ -221,7 +221,7 @@ def tile_list_tracer_departure_blend_kernel(
             "w3": (
                 QUARTER,
                 lambda a, t: w3_codes[:, a, t, :].bitcast(FP8X4),
-                lambda a, t: planes[1][:, a, P * t : P * (t + 1)],
+                lambda a, t: plane[:, a, W3_AT + P * t : W3_AT + P * (t + 1)],
             ),
         }
         banks = {}
@@ -246,6 +246,20 @@ def tile_list_tracer_departure_blend_kernel(
                             stop=(a == PASSES - 1 and e == 1 and lo + width == QUARTER),
                         )
 
+        def fraction_product(half, a):
+            for t in range(4):
+                if a == 0:
+                    banks["w1", half, t] = psum.tile([P, HALF], F32, name="bank", tag="bank%d" % (4 * half + t))
+                nc.tensor.matmul_mx(
+                    out=banks["w1", half, t][:],
+                    lhsT=w1_codes[:, a, t, :].bitcast(FP4X4),
+                    lhsT_scale=plane[:, a, W1_AT + P * t : W1_AT + P * (t + 1)],
+                    rhs=v_halves[a, half][:].bitcast(FP8X4),
+                    rhs_scale=v_scales(a, half * HALF, HALF),
+                    start=(a == 0),
+                    stop=(a == PASSES - 1),
+                )
+
         def sums(weight, q, u):
             return banks[weight, q, u][:].rearrange("p e j -> p j e")
 
@@ -255,11 +269,16 @@ def tile_list_tracer_departure_blend_kernel(
         result = [held([P, N_TILES, QUARTER], F32, "result%d" % q) for q in range(QUARTERS)]
         parts, h_rounded = {}, {}
 
-        def take_fraction(q, u):
-            if u == 0:
-                shape = [P, 2, QUARTER, 2]
-                fraction[q] = placed(shape, F32, "fraction%d" % q, FRACTION_AT[q])
-            nc.scalar.activation(fraction[q][:, u, :, :], sums("w1", q, u), ACT.Sigmoid)
+        def take_fractions(half):
+            for q in (2 * half, 2 * half + 1):
+                fraction[q] = placed([P, 4, QUARTER], F32, "fraction%d" % q, FRACTION_AT[q])
+            for t in range(4):
+                for n in range(2):
+                    sums_t = banks["w1", half, t][:, n * QUARTER : (n + 1) * QUARTER]
+                    nc.scalar.activation(fraction[2 * half + n][:, t, :], sums_t, ACT.Sigmoid)
+
+        def fractions(q, u):
+            return fraction[q][:, 2 * u : 2 * u + 2, :].rearrange("p e j -> p j e")
 
         def product(weight, q):
             for u in range(2):
@@ -269,11 +288,11 @@ def tile_list_tracer_departure_blend_kernel(
             at = PARTS0_AT + q * PARTS_BYTES if q < 2 else (q - 2) * ROUNDED_BYTES
             parts[q] = placed([P, 2, 2, QUARTER, 2], F32, "parts%d" % q, at)
             for u in range(2):
-                nc.vector.scalar_tensor_tensor(
-                    parts[q][:, 0, u, :, :], fraction[q][:, u, :, :], 1.0, sums("w2", q, u), ALU.subtract, ALU.mult
-                )
+                nc.vector.tensor_tensor(parts[q][:, 1, u, :, :], fractions(q, u), sums("w3", q, u), ALU.mult)
             for u in range(2):
-                nc.vector.tensor_tensor(parts[q][:, 1, u, :, :], fraction[q][:, u, :, :], sums("w3", q, u), ALU.mult)
+                nc.vector.scalar_tensor_tensor(
+                    parts[q][:, 0, u, :, :], fractions(q, u), 1.0, sums("w2", q, u), ALU.subtract, ALU.mult
+                )
 
         def join(engine, q, lo, hi):
             if lo == 0:
@@ -321,37 +340,30 @@ def tile_list_tracer_departure_blend_kernel(
 
         last, middle = QUARTERS - 1, QUARTER // 2
         for a in range(PASSES):
-            for q in range(last):
-                for u in range(2):
-                    multiply("w1", q, u, (a,))
+            for half in range(2):
+                fraction_product(half, a)
         for u in range(2):
             round_w2(0, u, nc.scalar.copy)
             quantise_w2(0, u)
-        round_w2(1, 0, nc.scalar.copy)
+        round_w2(1, 0, nc.vector.tensor_copy)
         round_w2(1, 1, nc.vector.tensor_copy)
-        for q in range(last):
-            for u in range(2):
-                take_fraction(q, u)
-        quantise_w2(1, 1)
-        move_w3()
+        for half in range(2):
+            take_fractions(half)
         quantise_w2(1, 0)
-        gather_words(1, last, 1, tag="w2_rounded1_0")
-        product("w2", 0)
+        quantise_w2(1, 1)
         product("w3", 0)
+        product("w2", 0)
+        product("w3", 1)
+        product("w2", 1)
         round_w4()
         weigh(0)
-        product("w2", 1)
-        product("w3", 1)
-        product("w1", last)
-        for u in range(2):
-            take_fraction(last, u)
 
         for q in range(last):
             join(nc.gpsimd, q, 0, QUARTER)
             weigh(q + 1)
             if q + 2 < QUARTERS:
-                product("w2", q + 2)
                 product("w3", q + 2)
+                product("w2", q + 2)
             if q == 0:
                 quantise_w4()
             quantise_h(q, 0, QUARTER)

@@ -86,10 +86,6 @@ def tile_list_tracer_departure_blend_kernel(
             nc.sync.dma_start(raw[0:P:4, :], scales.bitcast(I32).rearrange("a q c -> q a c"))
             raw_scales.append(raw)
 
-        warm = held([P, 16], F32, "warm")
-        nc.vector.memset(warm[:, 0:8], 0.0)
-        nc.scalar.activation(warm[:, 8:9], warm[:, 0:1], ACT.Sigmoid)
-
         plane = held([P, PASSES, PLANE], U8, "plane")
         plane_words = plane[:].rearrange("p a s -> p (a s)").bitcast(I32)
         nc.vector.memset(plane_words, 0)

@@ -170,6 +170,10 @@ def tile_list_tracer_departure_blend_kernel(
                 w2_codes[a, u] = held([P, 2 * P], U32, "w2_codes%d_%d" % (a, u))
                 w2_scales[a, u] = held([P, 2 * P], U8, "w2_scales%d_%d" % (a, u))
 
+        def round_w2_on_vector(a, u):
+            rows = raw_w2[a].rearrange("p j (c t i) -> p t c i j", t=4, i=4)[:, 2 * u : 2 * u + 2]
+            nc.vector.tensor_copy(w2_rounded[a, u][:], rows)
+
         def round_w2(a, u, copy):
             rows = raw_w2[a].rearrange("p j (c t i) -> p t c j i", t=4, i=4)[:, 2 * u : 2 * u + 2]
             dst = w2_rounded[a, u][:].rearrange("p t c i j -> p t c j i")
@@ -341,8 +345,8 @@ def tile_list_tracer_departure_blend_kernel(
         for u in range(2):
             round_w2(0, u, nc.scalar.copy)
             quantise_w2(0, u)
-        round_w2(1, 0, nc.vector.tensor_copy)
-        round_w2(1, 1, nc.vector.tensor_copy)
+        round_w2_on_vector(1, 0)
+        round_w2_on_vector(1, 1)
         for half in range(2):
             take_fractions(half)
         quantise_w2(1, 0)

@@ -29,8 +29,7 @@ W1_AT, W3_AT, V_AT, PLANE = 0, H, 2 * H, 2 * H + S
 W4_SPLIT = 256
 SRC_AT = 4 * N
 SRC_PAD = 8
-PAIR_OF = {"w3": (0, 2, 0, 3), "w2": (1, 3, 1, 0)}
-OUT_PAIR = {(0, 0): 2, (1, 0): 1, (2, 0): 2, (3, 0): 3, (3, QUARTER // 2): 0}
+EIGHTH = QUARTER // 2
 PARTS_BYTES = 4 * 4 * 2 * QUARTER
 OVERLAP = 64
 ROUNDED_BYTES = PARTS_BYTES + 2 * OVERLAP
@@ -38,7 +37,7 @@ ROUNDED_STEP = ROUNDED_BYTES - OVERLAP
 PARTS0_AT = QUARTERS * ROUNDED_STEP + OVERLAP
 RAW_W2_BYTES = 4 * 4 * H
 FRACTION_BYTES = 4 * 4 * QUARTER
-W1_CODES_AT = PARTS0_AT + 2 * PARTS_BYTES
+W1_CODES_AT = PARTS0_AT + 3 * PARTS_BYTES
 PICKED_AT = W1_CODES_AT + PASSES * 2 * H - OVERLAP
 PICKED_BYTES = 4 * HALF + 2 * OVERLAP
 V0_AT = (PICKED_AT + OVERLAP, PICKED_AT + OVERLAP + 4 * HALF)
@@ -171,14 +170,15 @@ def tile_list_tracer_departure_blend_kernel(
                 w2_scales[a, u] = held([P, 2 * P], U8, "w2_scales%d_%d" % (a, u))
 
         def round_w2_on_vector(a, u):
-            rows = raw_w2[a].rearrange("p j (c t i) -> p t c i j", t=4, i=4)[:, 2 * u : 2 * u + 2]
-            nc.vector.tensor_copy(w2_rounded[a, u][:], rows)
+            for e in range(2):
+                rows = raw_w2[a].rearrange("p j (c t i) -> p t c i j", t=4, i=4)[:, 2 * u + e]
+                nc.vector.tensor_scalar(w2_rounded[a, u][:, e], rows, -1.0, None, ALU.mult)
 
-        def round_w2(a, u, copy):
-            rows = raw_w2[a].rearrange("p j (c t i) -> p t c j i", t=4, i=4)[:, 2 * u : 2 * u + 2]
-            dst = w2_rounded[a, u][:].rearrange("p t c i j -> p t c j i")
-            for pair in range(2):
-                copy(dst[:, :, :, :, 2 * pair : 2 * pair + 2], rows[:, :, :, :, 2 * pair : 2 * pair + 2])
+        def round_w2_on_scalar(a, u):
+            for e in range(2):
+                rows = raw_w2[a].rearrange("p j (c t i) -> p t c j i", t=4, i=4)[:, 2 * u + e]
+                dst = w2_rounded[a, u][:, e].rearrange("p c i j -> p c j i")
+                nc.scalar.activation(dst, rows, ACT.Copy, scale=-1.0)
 
         def quantise_w2(a, u):
             nc.vector.quantize_mx(
@@ -208,48 +208,64 @@ def tile_list_tracer_departure_blend_kernel(
                 )
 
         weights = {
-            "w1": (
-                P,
-                lambda a, t: w1_codes[:, a, t, :].bitcast(FP4X4),
-                lambda a, t: plane[:, a, W1_AT + P * t : W1_AT + P * (t + 1)],
-            ),
             "w2": (
-                QUARTER,
                 lambda a, t: w2_codes[a, t // 2][:, P * (t % 2) : P * (t % 2 + 1)].bitcast(FP8X4),
                 lambda a, t: w2_scales[a, t // 2][:, P * (t % 2) : P * (t % 2 + 1)],
             ),
             "w3": (
-                QUARTER,
                 lambda a, t: w3_codes[:, a, t, :].bitcast(FP8X4),
                 lambda a, t: plane[:, a, W3_AT + P * t : W3_AT + P * (t + 1)],
             ),
         }
         banks = {}
 
-        def bank_tile(pair, u):
-            return psum.tile([P, 2, QUARTER], F32, name="bank", tag="bank%d" % (2 * pair + u))
+        def bank_tile(key, number, shape):
+            banks[key] = psum.tile([P] + shape, F32, name="bank", tag="bank%d" % number)
+            return banks[key]
 
-        def multiply(weight, q, u, passes):
-            width, codes_of, scales_of = weights[weight]
+        def one_pass(dst, weight, a, t, q, lo, width, start, stop):
+            codes_of, scales_of = weights[weight]
+            nc.tensor.matmul_mx(
+                out=dst,
+                lhsT=codes_of(a, t),
+                lhsT_scale=scales_of(a, t),
+                rhs=v_codes[a, q][:, lo : lo + width].bitcast(FP8X4),
+                rhs_scale=v_scales(a, q * QUARTER + lo, width),
+                start=start,
+                stop=stop,
+            )
+
+        def multiply(weight, q, u, number, passes):
             if passes[0] == 0:
-                banks[weight, q, u] = bank_tile(PAIR_OF[weight][q], u)
+                bank_tile((weight, q, u), number, [2, QUARTER])
             for a in passes:
                 for e in range(2):
-                    for lo in range(0, QUARTER, width):
-                        nc.tensor.matmul_mx(
-                            out=banks[weight, q, u][:, e, lo : lo + width],
-                            lhsT=codes_of(a, 2 * u + e),
-                            lhsT_scale=scales_of(a, 2 * u + e),
-                            rhs=v_codes[a, q][:, lo : lo + width].bitcast(FP8X4),
-                            rhs_scale=v_scales(a, q * QUARTER + lo, width),
-                            start=(a == 0 and e == 0 and lo == 0),
-                            stop=(a == PASSES - 1 and e == 1 and lo + width == QUARTER),
-                        )
+                    one_pass(
+                        banks[weight, q, u][:, e, :], weight, a, 2 * u + e, q, 0, QUARTER,
+                        a == 0 and e == 0, a == PASSES - 1 and e == 1,
+                    )
+
+        def product(q, first, passes=(0, 1)):
+            for n, weight in enumerate(("w3", "w2")):
+                for u in range(2):
+                    multiply(weight, q, u, first + 2 * n + u, passes)
+
+        def difference_product(q, u, number):
+            bank = bank_tile(("difference", u), number, [2, QUARTER])
+            steps = [(w, a, e) for w in ("w3", "w2") for a in range(PASSES) for e in range(2)]
+            for n, (w, a, e) in enumerate(steps):
+                one_pass(bank[:, e, :], w, a, 2 * u + e, q, 0, QUARTER, n == 0, n == len(steps) - 1)
+
+        def left_product(q, side, number):
+            bank = bank_tile(("left", side), number, [4, EIGHTH])
+            steps = [(a, t) for a in range(PASSES) for t in range(4)]
+            for n, (a, t) in enumerate(steps):
+                one_pass(bank[:, t, :], "w2", a, t, q, side * EIGHTH, EIGHTH, n == 0, n == len(steps) - 1)
 
         def fraction_product(half, a):
             for t in range(4):
                 if a == 0:
-                    banks["w1", half, t] = psum.tile([P, HALF], F32, name="bank", tag="bank%d" % (4 * half + t))
+                    bank_tile(("w1", half, t), 4 * half + t, [HALF])
                 nc.tensor.matmul_mx(
                     out=banks["w1", half, t][:],
                     lhsT=w1_codes[:, a, t, :].bitcast(FP4X4),
@@ -260,8 +276,8 @@ def tile_list_tracer_departure_blend_kernel(
                     stop=(a == PASSES - 1),
                 )
 
-        def sums(weight, q, u):
-            return banks[weight, q, u][:].rearrange("p e j -> p j e")
+        def sums(key):
+            return banks[key][:].rearrange("p e j -> p j e")
 
         out_rows = out.rearrange("(c p) j -> p c j", p=P)
         fraction = {}
@@ -280,98 +296,136 @@ def tile_list_tracer_departure_blend_kernel(
         def fractions(q, u):
             return fraction[q][:, 2 * u : 2 * u + 2, :].rearrange("p e j -> p j e")
 
-        def product(weight, q):
-            for u in range(2):
-                multiply(weight, q, u, (0, 1))
+        last = QUARTERS - 1
+        right_part, left_part = {}, {}
 
         def weigh(q):
-            at = PARTS0_AT + q * PARTS_BYTES if q < 2 else (q - 2) * ROUNDED_BYTES
-            parts[q] = placed([P, 2, 2, QUARTER, 2], F32, "parts%d" % q, at)
+            right_part[q] = placed([P, 2, QUARTER, 2], F32, "right_part%d" % q, PARTS0_AT + q * PARTS_BYTES)
             for u in range(2):
-                nc.vector.tensor_tensor(parts[q][:, 1, u, :, :], fractions(q, u), sums("w3", q, u), ALU.mult)
-            for u in range(2):
-                nc.vector.scalar_tensor_tensor(
-                    parts[q][:, 0, u, :, :], fractions(q, u), 1.0, sums("w2", q, u), ALU.subtract, ALU.mult
-                )
+                nc.vector.tensor_tensor(right_part[q][:, u], fractions(q, u), sums(("w3", q, u)), ALU.mult)
+            runs = ((0, QUARTER),) if q < 2 else ((0, EIGHTH), (EIGHTH, QUARTER))
+            for lo, hi in runs:
+                at = PARTS0_AT + q * PARTS_BYTES + PARTS_BYTES // 2 + 16 * lo
+                left_part[q, lo] = placed([P, 2, hi - lo, 2], F32, "left_part%d_%d" % (q, lo), at)
+                for u in range(2):
+                    nc.vector.scalar_tensor_tensor(
+                        left_part[q, lo][:, u], fractions(q, u)[:, lo:hi], 1.0, sums(("w2", q, u))[:, lo:hi],
+                        ALU.subtract, ALU.mult,
+                    )
+
+        def rounded_tile(key, width, at, pad):
+            padded = placed([P, 4 * width + pad // 2], BF16, "h_rounded%d_%d" % key, at)
+            h_rounded[key] = padded[:, : 4 * width].rearrange("p (j u e) -> p j u e", u=2, e=2)
 
         def join(engine, q, lo, hi):
-            if lo == 0:
-                padded = placed([P, ROUNDED_BYTES // 2], BF16, "h_rounded%d" % q, q * ROUNDED_STEP)
-                h_rounded[q] = padded[:, : 4 * QUARTER].rearrange("p (j u e) -> p j u e", u=2, e=2)
             engine.tensor_tensor(
-                h_rounded[q][:, lo:hi, :, :],
-                parts[q][:, 1, :, lo:hi, :].rearrange("p u j e -> p j u e"),
-                parts[q][:, 0, :, lo:hi, :].rearrange("p u j e -> p j u e"),
-                ALU.subtract,
+                h_rounded[q, lo],
+                right_part[q][:, :, lo:hi].rearrange("p u j e -> p j u e"),
+                left_part[q, lo][:].rearrange("p u j e -> p j u e"),
+                ALU.add,
             )
 
+        def scale_difference():
+            right_part[last] = held([P, 2, QUARTER, 2], F32, "scaled_difference")
+            for u in range(2):
+                nc.vector.tensor_tensor(right_part[last][:, u], fractions(last, u), sums(("difference", u)), ALU.mult)
+
+        def add_left():
+            whole = held([P, QUARTER, 2, 2], BF16, "h_rounded_last")
+            h_rounded[last, 0] = whole[:]
+            for side in range(2):
+                cols = slice(side * EIGHTH, (side + 1) * EIGHTH)
+                nc.vector.tensor_tensor(
+                    h_rounded[last, 0][:, cols],
+                    right_part[last][:, :, cols, :].rearrange("p u j e -> p j u e"),
+                    banks["left", side][:].rearrange("p (u e) j -> p j u e", u=2),
+                    ALU.subtract,
+                )
+
+        def code_tiles(q, codes_at, scales_at):
+            h_codes[q] = placed([P, QUARTER], U32, "h_codes%d" % q, codes_at)
+            h_scales[q] = placed([P, QUARTER], U8, "h_scales%d" % q, scales_at)
+
         def quantise_h(q, lo, hi):
-            if lo == 0:
-                at = FRACTION_AT[(q + 1) % QUARTERS]
-                h_codes[q] = placed([P, QUARTER], U32, "h_codes%d" % q, at)
-                h_scales[q] = placed([P, QUARTER], U8, "h_scales%d" % q, at + 4 * QUARTER)
             nc.vector.quantize_mx(
                 out=h_codes[q][:, lo:hi].bitcast(FP8X4),
                 scales=h_scales[q][:, lo:hi],
-                in_=h_rounded[q][:, lo:hi, :, :].rearrange("p j u e -> p (j u e)"),
+                in_=h_rounded[q, lo].rearrange("p j u e -> p (j u e)"),
             )
 
-        def tendencies(q, lo, hi, share_with_vector=False):
+        def tendencies(step, number, runs, on_vector=()):
             for first in range(0, N_TILES, 2):
-                bank = bank_tile(OUT_PAIR[q, lo], first // 2)
+                bank = bank_tile(("out", step, first), number[first // 2], [2, QUARTER])
                 tiles = range(first, min(first + 2, N_TILES))
                 for c in tiles:
                     nc.tensor.matmul_mx(
-                        out=bank[:, c - first, lo:hi],
+                        out=bank[:, c - first, :],
                         lhsT=second["w4_codes"][:, P * c : P * (c + 1)].bitcast(FP8X4),
                         lhsT_scale=second["w4_scales"][:, P * c : P * (c + 1)],
-                        rhs=h_codes[q][:, lo:hi].bitcast(FP8X4),
-                        rhs_scale=h_scales[q][:, lo:hi],
+                        rhs=h_codes[step][:].bitcast(FP8X4),
+                        rhs_scale=h_scales[step][:],
                         start=True,
                         stop=True,
                     )
                 for c in tiles:
-                    dst, acc, bias = result[q][:, c, lo:hi], bank[:, c - first, lo:hi], src_col[:, c : c + 1]
-                    if share_with_vector and first == 0:
+                    dst, acc, bias = result[step][:, c, :], bank[:, c - first, :], src_col[:, c : c + 1]
+                    if c in on_vector:
                         nc.vector.tensor_scalar(dst, acc, bias, None, ALU.add)
                     else:
                         nc.scalar.activation(dst, acc, ACT.Identity, bias=bias)
-            nc.sync.dma_start(out_rows[:, :, q * QUARTER + lo : q * QUARTER + hi], result[q][:, :, lo:hi])
+                    if step >= 2:
+                        nc.sync.dma_start(out_rows[:, c, step * QUARTER : (step + 1) * QUARTER], dst)
+            if step < 2:
+                nc.sync.dma_start(out_rows[:, :, step * QUARTER : (step + 1) * QUARTER], result[step][:])
 
-        last, middle = QUARTERS - 1, QUARTER // 2
-        for a in range(PASSES):
-            for half in range(2):
-                fraction_product(half, a)
         for u in range(2):
-            round_w2(0, u, nc.scalar.copy)
+            round_w2_on_scalar(0, u)
             quantise_w2(0, u)
         round_w2_on_vector(1, 0)
         round_w2_on_vector(1, 1)
-        for half in range(2):
-            take_fractions(half)
         quantise_w2(1, 0)
         quantise_w2(1, 1)
-        product("w3", 0)
-        product("w2", 0)
-        product("w3", 1)
-        product("w2", 1)
+        for a in range(PASSES):
+            for half in range(2):
+                fraction_product(half, a)
+        for half in range(2):
+            take_fractions(half)
+        product(0, 0)
+        product(1, 4)
         round_w4()
         weigh(0)
 
-        for q in range(last):
-            join(nc.gpsimd, q, 0, QUARTER)
-            weigh(q + 1)
-            if q + 2 < QUARTERS:
-                product("w3", q + 2)
-                product("w2", q + 2)
-            if q == 0:
-                quantise_w4()
-            quantise_h(q, 0, QUARTER)
-            tendencies(q, 0, QUARTER)
+        rounded_tile((0, 0), QUARTER, 0, OVERLAP)
+        join(nc.gpsimd, 0, 0, QUARTER)
+        weigh(1)
+        product(2, 0)
+        for u in range(2):
+            difference_product(last, u, 4 + u)
+        quantise_w4()
+        code_tiles(0, FRACTION_AT[1], FRACTION_AT[1] + 4 * QUARTER)
+        quantise_h(0, 0, QUARTER)
 
-        join(nc.vector, last, 0, middle)
-        join(nc.vector, last, middle, QUARTER)
-        quantise_h(last, 0, middle)
-        quantise_h(last, middle, QUARTER)
-        tendencies(last, 0, middle)
-        tendencies(last, middle, QUARTER, share_with_vector=True)
+        rounded_tile((1, 0), QUARTER, 8 * QUARTER, OVERLAP)
+        join(nc.gpsimd, 1, 0, QUARTER)
+        weigh(2)
+        tendencies(0, (0, 1), [(0, QUARTER)])
+        for side in range(2):
+            left_product(last, side, 6 + side)
+        scale_difference()
+        code_tiles(1, FRACTION_AT[3], FRACTION_AT[2])
+        quantise_h(1, 0, QUARTER)
+        tendencies(1, (2, 3), [(QUARTER, QUARTER)])
+
+        rounded_tile((2, 0), EIGHTH, 16 * QUARTER, 0)
+        join(nc.gpsimd, 2, 0, EIGHTH)
+        add_left()
+        freed = PARTS0_AT + 2 * PARTS_BYTES + PARTS_BYTES // 2
+        code_tiles(last, freed, FRACTION_AT[0])
+        quantise_h(last, 0, QUARTER)
+        tendencies(last, (4, 5), [(last * QUARTER, QUARTER)])
+        rounded_tile((2, EIGHTH), EIGHTH, freed + 4 * QUARTER, 0)
+        join(nc.vector, 2, EIGHTH, QUARTER)
+        code_tiles(2, FRACTION_AT[0] + 2 * QUARTER, FRACTION_AT[0] + QUARTER)
+        quantise_h(2, 0, EIGHTH)
+        quantise_h(2, EIGHTH, QUARTER)
+        tendencies(2, (6, 7), [(2 * QUARTER, QUARTER)], on_vector=(0, 1))

@@ -20,34 +20,36 @@ P = 128
 K_PASS = 4 * P
 PASSES = K // K_PASS
 PER_COLUMN = 16
-BANKS = 8
 QUARTER = 256
 QUARTERS = S // QUARTER
+EIGHTH = QUARTER // 2
 HALF = S // 2
 N_TILES = N // P
 W1_AT, W3_AT, V_AT, PLANE = 0, H, 2 * H, 2 * H + S
 W4_SPLIT = 256
 SRC_AT = 4 * N
 SRC_PAD = 8
-EIGHTH = QUARTER // 2
-PARTS_BYTES = 4 * 4 * 2 * QUARTER
 OVERLAP = 64
-ROUNDED_BYTES = PARTS_BYTES + 2 * OVERLAP
-ROUNDED_STEP = ROUNDED_BYTES - OVERLAP
-PARTS0_AT = QUARTERS * ROUNDED_STEP + OVERLAP
+W1_CODES_AT = 0
+V0_AT = (W1_CODES_AT + PASSES * 2 * H, W1_CODES_AT + PASSES * 2 * H + 4 * HALF)
+PICKED_AT = V0_AT[0] - OVERLAP
+PICKED_BYTES = 2 * 4 * HALF + 2 * OVERLAP
+RAW_W3_AT = PICKED_AT + PICKED_BYTES
+RAW_W4_AT = RAW_W3_AT + PASSES * 4 * H
 RAW_W2_BYTES = 4 * 4 * H
-FRACTION_BYTES = 4 * 4 * QUARTER
-W1_CODES_AT = PARTS0_AT + 3 * PARTS_BYTES
-PICKED_AT = W1_CODES_AT + PASSES * 2 * H - OVERLAP
-PICKED_BYTES = 4 * HALF + 2 * OVERLAP
-V0_AT = (PICKED_AT + OVERLAP, PICKED_AT + OVERLAP + 4 * HALF)
-WINDOW1_AT = V0_AT[1] + 4 * HALF
-RAW_W1_AT = WINDOW1_AT + 4 * T - OVERLAP
-ROUNDED_W2_BYTES = 2 * 2 * H
-RAW_W1_BYTES = 2 * ROUNDED_W2_BYTES + 2 * OVERLAP
-RAW_W2_1_AT = RAW_W1_AT + RAW_W1_BYTES - OVERLAP
-RAW_W2_AT = (RAW_W2_1_AT + RAW_W2_BYTES, RAW_W2_1_AT)
-FRACTION_AT = [RAW_W2_AT[q // 2] + q % 2 * FRACTION_BYTES for q in range(QUARTERS)]
+RAW_W2_0_AT = RAW_W4_AT + 4 * (SRC_AT + 2 * SRC_PAD)
+RAW_W1_AT = RAW_W2_0_AT + RAW_W2_BYTES - OVERLAP
+RAW_W1_BYTES = PASSES * 2 * H + 2 * OVERLAP
+RAW_W2_AT = (RAW_W2_0_AT, RAW_W1_AT + RAW_W1_BYTES - OVERLAP)
+ROUNDED_BYTES = 2 * 4 * QUARTER
+ROUNDED_AT = RAW_W2_AT[1] + RAW_W2_BYTES
+SLOT_BYTES = 4 * 2 * QUARTER
+SLOTS_AT = ROUNDED_AT + 3 * ROUNDED_BYTES
+FRACTION_AT = dict(
+    [((q, u), RAW_W2_AT[1] + (q % 2 * 2 + u) * SLOT_BYTES) for q in (2, 3) for u in range(2)] + [((1, 1), SLOTS_AT)]
+)
+SCALED_AT = SLOTS_AT + 4 * SLOT_BYTES
+LEFT_PART_AT = {(0, 0): SLOTS_AT + SLOT_BYTES, (2, 0): SLOTS_AT + 3 * SLOT_BYTES}
 
 
 def tile_list_tracer_departure_blend_kernel(
@@ -57,18 +59,18 @@ def tile_list_tracer_departure_blend_kernel(
     with ExitStack() as ctx:
         keep = ctx.enter_context(tc.tile_pool(name="keep", bufs=1))
         psum = ctx.enter_context(tc.psum_pool(name="psum", bufs=1))
-
         chain = ctx.enter_context(tc.tile_pool(name="chain", bufs=1))
 
         def placed(shape, dtype, name, at):
             return chain.tile(shape, dtype, name=name, offset=at, align_bytes=64)
 
-        def held(shape, dtype, name, tag=""):
-            return keep.tile(shape, dtype, name=name, tag=tag or name, align_bytes=64)
+        def held(shape, dtype, name, at=None):
+            if at is not None:
+                return placed(shape, dtype, name, at)
+            return keep.tile(shape, dtype, name=name, align_bytes=64)
 
         offsets = keep.tile([P, S // PER_COLUMN], U16, name="offsets")
         nc.sync.dma_start(offsets[:], offs)
-
         padded_w1 = placed([P, RAW_W1_BYTES // 4], I32, "raw_w1", RAW_W1_AT)
         raw_w1 = padded_w1[:, :H].rearrange("p (a c) -> p a c", a=PASSES)
         nc.sync.dma_start(raw_w1, w1_words.bitcast(I32).rearrange("a p c -> p a c"))
@@ -91,20 +93,21 @@ def tile_list_tracer_departure_blend_kernel(
 
         word_window, raw_w2 = {}, {}
 
-        def load_words(a, window):
-            nc.sync.dma_start(window[:], tab_words[a].rearrange("p t i -> p (t i)").bitcast(I32))
-            word_window[a] = window
+        def load_words(a):
+            word_window[a] = held([P, T], I32, "word_window%d" % a)
+            nc.sync.dma_start(word_window[a][:], tab_words[a].rearrange("p t i -> p (t i)").bitcast(I32))
 
-        def load_w2(a, raw):
-            raw_w2[a] = raw[:, : 4 * H].rearrange("p (j r) -> p j r", j=4)
+        def load_w2(a):
+            raw = placed([P, 4 * H], F32, "raw_w2_%d" % a, RAW_W2_AT[a])
+            raw_w2[a] = raw[:].rearrange("p (j r) -> p j r", j=4)
             nc.sync.dma_start(raw_w2[a], w2[K_PASS * a : K_PASS * (a + 1), :].rearrange("(p j) r -> p j r", j=4))
 
-        load_words(0, held([P, T], I32, "word_window0"))
-        load_w2(0, placed([P, 4 * H + OVERLAP // 4], F32, "raw_w2_0", RAW_W2_AT[0]))
-
-        raw_w3 = held([P, PASSES, H], I32, "raw_w3")
+        load_words(0)
+        load_words(1)
+        padded_w3 = placed([P, PASSES * H + OVERLAP // 4], I32, "raw_w3", RAW_W3_AT)
+        raw_w3 = padded_w3[:, : PASSES * H].rearrange("p (a c) -> p a c", a=PASSES)
         nc.sync.dma_start(
-            raw_w3[:], w3_words.rearrange("a p c i -> a p (c i)").bitcast(I32).rearrange("a p c -> p a c")
+            raw_w3, w3_words.rearrange("a p c i -> a p (c i)").bitcast(I32).rearrange("a p c -> p a c")
         )
 
         picked = placed([P, PICKED_BYTES], U8, "picked_scales", PICKED_AT)[:, :S]
@@ -124,34 +127,34 @@ def tile_list_tracer_departure_blend_kernel(
             w1_codes[:].bitcast(I32).rearrange("p a t (c i) -> p a t c i", i=2),
             raw_w1.rearrange("p a (c t i) -> p a t c i", t=4, i=2),
         )
-        load_words(1, placed([P, T], I32, "word_window1", WINDOW1_AT))
-        load_w2(1, placed([P, 4 * H], F32, "raw_w2_1", RAW_W2_AT[1]))
+        load_w2(0)
+        load_w2(1)
 
         def v_scales(a, lo, width):
             return plane[:, a, V_AT + lo : V_AT + lo + width]
 
-        v_codes, v_halves = {}, {}
+        v_halves = {}
 
-        def gather_words(a, q, count, tag=""):
-            shape, name = [P, count * QUARTER], "v_codes_%d_%d" % (a, q)
-            picked = placed(shape, U32, name, V0_AT[q // 2]) if a == 0 else held(shape, U32, name)
-            cols = slice(q * QUARTER // PER_COLUMN, (q + count) * QUARTER // PER_COLUMN)
-            nc.vector.tensor_copy(picked[:], word_window[a][:].bitcast(U32).indirect(offsets[:, cols]))
-            v_halves[a, q // 2] = picked
-            for n in range(count):
-                v_codes[a, q + n] = picked[:, n * QUARTER : (n + 1) * QUARTER]
+        def gather_words(a, half):
+            name = "v_codes_%d_%d" % (a, half)
+            v_halves[a, half] = held([P, HALF], U32, name, V0_AT[half] if a == 0 else None)
+            cols = slice(half * HALF // PER_COLUMN, (half + 1) * HALF // PER_COLUMN)
+            nc.vector.tensor_copy(v_halves[a, half][:], word_window[a][:].bitcast(U32).indirect(offsets[:, cols]))
 
-        gather_words(0, 0, 2)
-        gather_words(0, 2, 2)
-        w3_codes = held([P, PASSES, 4, P], I32, "w3_codes", tag="word_window0")
+        def v_codes(a, lo, width):
+            return v_halves[a, lo // HALF][:, lo % HALF : lo % HALF + width].bitcast(FP8X4)
+
+        gather_words(0, 0)
+        gather_words(0, 1)
+        gather_words(1, 0)
+        w3_codes = held([P, PASSES, 4, P], I32, "w3_codes")
         nc.vector.tensor_copy(
             w3_codes[:].rearrange("p a t (c i) -> p a t c i", i=4),
-            raw_w3[:].rearrange("p a (c t i) -> p a t c i", t=4, i=4),
+            raw_w3.rearrange("p a (c t i) -> p a t c i", t=4, i=4),
         )
-        gather_words(1, 0, 2)
-        gather_words(1, 2, 2)
+        gather_words(1, 1)
 
-        raw4 = placed([P, SRC_AT + SRC_PAD], F32, "raw_w4", RAW_W2_AT[0] + RAW_W2_BYTES)
+        raw4 = placed([P, SRC_AT + SRC_PAD], F32, "raw_w4", RAW_W4_AT)
         raw_w4 = raw4[:, :SRC_AT].rearrange("p (t n) -> p t n", t=4)
         src_col = raw4[:, SRC_AT : SRC_AT + N_TILES]
         w4_rows = w4.rearrange("(c t i) n -> t c i n", t=4, i=4)
@@ -163,9 +166,7 @@ def tile_list_tracer_departure_blend_kernel(
         w2_rounded, w2_codes, w2_scales = {}, {}, {}
         for a in range(PASSES):
             for u in range(2):
-                shape, name = [P, 2, 32, 4, 4], "w2_rounded%d_%d" % (a, u)
-                at = RAW_W1_AT + OVERLAP + u * ROUNDED_W2_BYTES
-                w2_rounded[a, u] = placed(shape, BF16, name, at) if a == 0 else held(shape, BF16, name)
+                w2_rounded[a, u] = held([P, 2, 32, 4, 4], BF16, "w2_rounded%d_%d" % (a, u))
                 w2_codes[a, u] = held([P, 2 * P], U32, "w2_codes%d_%d" % (a, u))
                 w2_scales[a, u] = held([P, 2 * P], U8, "w2_scales%d_%d" % (a, u))
 
@@ -173,6 +174,11 @@ def tile_list_tracer_departure_blend_kernel(
             for e in range(2):
                 rows = raw_w2[a].rearrange("p j (c t i) -> p t c i j", t=4, i=4)[:, 2 * u + e]
                 nc.vector.tensor_scalar(w2_rounded[a, u][:, e], rows, -1.0, None, ALU.mult)
+
+        def round_w2_on_gpsimd(a, u):
+            for e in range(2):
+                rows = raw_w2[a].rearrange("p j (c t i) -> p t c i j", t=4, i=4)[:, 2 * u + e]
+                nc.gpsimd.tensor_scalar(w2_rounded[a, u][:, e], rows, -1.0, 0.0, ALU.mult, ALU.add)
 
         def round_w2_on_scalar(a, u):
             for e in range(2):
@@ -198,8 +204,8 @@ def tile_list_tracer_departure_blend_kernel(
         second = {}
 
         def quantise_w4():
-            second["w4_codes"] = placed([P, N], U32, "w4_codes", PARTS0_AT)
-            second["w4_scales"] = placed([P, N], U8, "w4_scales", FRACTION_AT[1] + FRACTION_BYTES // 2)
+            second["w4_codes"] = placed([P, N], U32, "w4_codes", LEFT_PART_AT[0, 0])
+            second["w4_scales"] = placed([P, N], U8, "w4_scales", FRACTION_AT[1, 1] + 5 * QUARTER)
             for lo, hi in ((0, W4_SPLIT), (W4_SPLIT, N)):
                 nc.vector.quantize_mx(
                     out=second["w4_codes"][:, lo:hi].bitcast(FP8X4),
@@ -223,209 +229,196 @@ def tile_list_tracer_departure_blend_kernel(
             banks[key] = psum.tile([P] + shape, F32, name="bank", tag="bank%d" % number)
             return banks[key]
 
-        def one_pass(dst, weight, a, t, q, lo, width, start, stop):
+        def one_pass(dst, weight, a, t, lo, width, start, stop):
             codes_of, scales_of = weights[weight]
             nc.tensor.matmul_mx(
                 out=dst,
                 lhsT=codes_of(a, t),
                 lhsT_scale=scales_of(a, t),
-                rhs=v_codes[a, q][:, lo : lo + width].bitcast(FP8X4),
-                rhs_scale=v_scales(a, q * QUARTER + lo, width),
+                rhs=v_codes(a, lo, width),
+                rhs_scale=v_scales(a, lo, width),
                 start=start,
                 stop=stop,
             )
 
-        def multiply(weight, q, u, number, passes):
-            if passes[0] == 0:
-                bank_tile((weight, q, u), number, [2, QUARTER])
-            for a in passes:
-                for e in range(2):
-                    one_pass(
-                        banks[weight, q, u][:, e, :], weight, a, 2 * u + e, q, 0, QUARTER,
-                        a == 0 and e == 0, a == PASSES - 1 and e == 1,
+        def product(key, names, q, numbers, passes=(0, 1)):
+            for u in range(2):
+                bank = bank_tile((key, q, u), numbers[u], [2, QUARTER])
+                steps = [(w, a, e) for w in names for a in passes for e in range(2)]
+                for n, (w, a, e) in enumerate(steps):
+                    one_pass(bank[:, e, :], w, a, 2 * u + e, q * QUARTER, QUARTER, n == 0, n == len(steps) - 1)
+
+        def left_by_cells(q, sides, number):
+            for side in sides:
+                bank = bank_tile(("by_cells", side), number, [4, EIGHTH])
+                steps = [(a, t) for a in range(PASSES) for t in range(4)]
+                for n, (a, t) in enumerate(steps):
+                    lo = q * QUARTER + side * EIGHTH
+                    one_pass(bank[:, t, :], "w2", a, t, lo, EIGHTH, n == 0, n == len(steps) - 1)
+
+        def fraction_product(half, slots, first):
+            for a in range(PASSES):
+                for t in slots:
+                    if a == 0:
+                        bank_tile(("w1", half, t), first + t, [HALF])
+                    nc.tensor.matmul_mx(
+                        out=banks["w1", half, t][:],
+                        lhsT=w1_codes[:, a, t, :].bitcast(FP4X4),
+                        lhsT_scale=plane[:, a, W1_AT + P * t : W1_AT + P * (t + 1)],
+                        rhs=v_codes(a, half * HALF, HALF),
+                        rhs_scale=v_scales(a, half * HALF, HALF),
+                        start=(a == 0),
+                        stop=(a == PASSES - 1),
                     )
 
-        def product(q, first, passes=(0, 1)):
-            for n, weight in enumerate(("w3", "w2")):
-                for u in range(2):
-                    multiply(weight, q, u, first + 2 * n + u, passes)
-
-        def difference_product(q, u, number):
-            bank = bank_tile(("difference", u), number, [2, QUARTER])
-            steps = [(w, a, e) for w in ("w3", "w2") for a in range(PASSES) for e in range(2)]
-            for n, (w, a, e) in enumerate(steps):
-                one_pass(bank[:, e, :], w, a, 2 * u + e, q, 0, QUARTER, n == 0, n == len(steps) - 1)
-
-        def left_product(q, side, number):
-            bank = bank_tile(("left", side), number, [4, EIGHTH])
-            steps = [(a, t) for a in range(PASSES) for t in range(4)]
-            for n, (a, t) in enumerate(steps):
-                one_pass(bank[:, t, :], "w2", a, t, q, side * EIGHTH, EIGHTH, n == 0, n == len(steps) - 1)
-
-        def fraction_product(half, a):
-            for t in range(4):
-                if a == 0:
-                    bank_tile(("w1", half, t), 4 * half + t, [HALF])
-                nc.tensor.matmul_mx(
-                    out=banks["w1", half, t][:],
-                    lhsT=w1_codes[:, a, t, :].bitcast(FP4X4),
-                    lhsT_scale=plane[:, a, W1_AT + P * t : W1_AT + P * (t + 1)],
-                    rhs=v_halves[a, half][:].bitcast(FP8X4),
-                    rhs_scale=v_scales(a, half * HALF, HALF),
-                    start=(a == 0),
-                    stop=(a == PASSES - 1),
-                )
-
-        def sums(key):
-            return banks[key][:].rearrange("p e j -> p j e")
+        def sums(key, q, u):
+            return banks[key, q, u][:].rearrange("p e j -> p j e")
 
         out_rows = out.rearrange("(c p) j -> p c j", p=P)
-        fraction = {}
-        h_codes, h_scales = {}, {}
-        result = [held([P, N_TILES, QUARTER], F32, "result%d" % q) for q in range(QUARTERS)]
-        parts, h_rounded = {}, {}
+        fraction, right_part, left_part = {}, {}, {}
+        h_rounded, h_codes, h_scales = {}, {}, {}
 
-        def take_fractions(half):
-            for q in (2 * half, 2 * half + 1):
-                fraction[q] = placed([P, 4, QUARTER], F32, "fraction%d" % q, FRACTION_AT[q])
-            for t in range(4):
-                for n in range(2):
-                    sums_t = banks["w1", half, t][:, n * QUARTER : (n + 1) * QUARTER]
-                    nc.scalar.activation(fraction[2 * half + n][:, t, :], sums_t, ACT.Sigmoid)
+        def take_fractions(half, slots):
+            for t in slots:
+                for q in (2 * half, 2 * half + 1):
+                    if t % 2 == 0:
+                        name = "fraction%d_%d" % (q, t // 2)
+                        fraction[q, t // 2] = held([P, 2, QUARTER], F32, name, FRACTION_AT.get((q, t // 2)))
+                    sums_t = banks["w1", half, t][:, q % 2 * QUARTER : (q % 2 + 1) * QUARTER]
+                    nc.scalar.activation(fraction[q, t // 2][:, t % 2, :], sums_t, ACT.Sigmoid)
 
         def fractions(q, u):
-            return fraction[q][:, 2 * u : 2 * u + 2, :].rearrange("p e j -> p j e")
+            return fraction[q, u][:].rearrange("p e j -> p j e")
 
-        last = QUARTERS - 1
-        right_part, left_part = {}, {}
+        def weigh_right(key, q, pairs=(0, 1)):
+            if pairs[0] == 0:
+                at = SCALED_AT if key == "difference" else None
+                right_part[q] = held([P, 2, QUARTER, 2], F32, "right_part%d" % q, at)
+            for u in pairs:
+                nc.vector.tensor_tensor(right_part[q][:, u], fractions(q, u), sums(key, q, u), ALU.mult)
 
-        def weigh(q):
-            right_part[q] = placed([P, 2, QUARTER, 2], F32, "right_part%d" % q, PARTS0_AT + q * PARTS_BYTES)
+        def weigh_left(q, lo, hi):
+            name = "left_part%d_%d" % (q, lo)
+            left_part[q, lo] = held([P, 2, hi - lo, 2], F32, name, LEFT_PART_AT.get((q, lo)))
             for u in range(2):
-                nc.vector.tensor_tensor(right_part[q][:, u], fractions(q, u), sums(("w3", q, u)), ALU.mult)
-            runs = ((0, QUARTER),) if q < 2 else ((0, EIGHTH), (EIGHTH, QUARTER))
-            for lo, hi in runs:
-                at = PARTS0_AT + q * PARTS_BYTES + PARTS_BYTES // 2 + 16 * lo
-                left_part[q, lo] = placed([P, 2, hi - lo, 2], F32, "left_part%d_%d" % (q, lo), at)
-                for u in range(2):
-                    nc.vector.scalar_tensor_tensor(
-                        left_part[q, lo][:, u], fractions(q, u)[:, lo:hi], 1.0, sums(("w2", q, u))[:, lo:hi],
-                        ALU.subtract, ALU.mult,
-                    )
-
-        def rounded_tile(key, width, at, pad):
-            padded = placed([P, 4 * width + pad // 2], BF16, "h_rounded%d_%d" % key, at)
-            h_rounded[key] = padded[:, : 4 * width].rearrange("p (j u e) -> p j u e", u=2, e=2)
-
-        def join(engine, q, lo, hi):
-            engine.tensor_tensor(
-                h_rounded[q, lo],
-                right_part[q][:, :, lo:hi].rearrange("p u j e -> p j u e"),
-                left_part[q, lo][:].rearrange("p u j e -> p j u e"),
-                ALU.add,
-            )
-
-        def scale_difference():
-            right_part[last] = held([P, 2, QUARTER, 2], F32, "scaled_difference")
-            for u in range(2):
-                nc.vector.tensor_tensor(right_part[last][:, u], fractions(last, u), sums(("difference", u)), ALU.mult)
-
-        def add_left():
-            whole = held([P, QUARTER, 2, 2], BF16, "h_rounded_last")
-            h_rounded[last, 0] = whole[:]
-            for side in range(2):
-                cols = slice(side * EIGHTH, (side + 1) * EIGHTH)
-                nc.vector.tensor_tensor(
-                    h_rounded[last, 0][:, cols],
-                    right_part[last][:, :, cols, :].rearrange("p u j e -> p j u e"),
-                    banks["left", side][:].rearrange("p (u e) j -> p j u e", u=2),
-                    ALU.subtract,
+                nc.vector.scalar_tensor_tensor(
+                    left_part[q, lo][:, u], fractions(q, u)[:, lo:hi], 1.0, sums("left", q, u)[:, lo:hi],
+                    ALU.subtract, ALU.mult,
                 )
 
-        def code_tiles(q, codes_at, scales_at):
-            h_codes[q] = placed([P, QUARTER], U32, "h_codes%d" % q, codes_at)
-            h_scales[q] = placed([P, QUARTER], U8, "h_scales%d" % q, scales_at)
+        def rounded_tile(name, width, at, pad=0):
+            padded = held([P, 4 * width + pad // 2], BF16, name, at)
+            return padded[:, : 4 * width].rearrange("p (j u e) -> p j u e", u=2, e=2)
 
-        def quantise_h(q, lo, hi):
+        def right_of(q, lo, hi):
+            return right_part[q][:, :, lo:hi, :].rearrange("p u j e -> p j u e")
+
+        def join(engine, q, lo, hi, dst):
+            left = left_part[q, lo][:].rearrange("p u j e -> p j u e")
+            engine.tensor_tensor(dst, right_of(q, lo, hi), left, ALU.add)
+
+        def add_left(q, side, dst):
+            left = banks["by_cells", side][:].rearrange("p (u e) j -> p j u e", u=2)
+            lo, hi = side * EIGHTH, (side + 1) * EIGHTH
+            nc.vector.tensor_tensor(dst[:, lo:hi], right_of(q, lo, hi), left, ALU.subtract)
+
+        def code_tiles(q, codes_at=None, scales_at=None):
+            h_codes[q] = held([P, QUARTER], U32, "h_codes%d" % q, codes_at)
+            h_scales[q] = held([P, QUARTER], U8, "h_scales%d" % q, scales_at)
+
+        def quantise_h(q, cols, rounded):
             nc.vector.quantize_mx(
-                out=h_codes[q][:, lo:hi].bitcast(FP8X4),
-                scales=h_scales[q][:, lo:hi],
-                in_=h_rounded[q, lo].rearrange("p j u e -> p (j u e)"),
+                out=h_codes[q][:, cols].bitcast(FP8X4),
+                scales=h_scales[q][:, cols],
+                in_=rounded.rearrange("p j u e -> p (j u e)"),
             )
 
-        def tendencies(step, number, runs, on_vector=()):
+        def tendencies(q, numbers, on_vector=()):
+            result = held([P, N_TILES, QUARTER], F32, "result%d" % q)
             for first in range(0, N_TILES, 2):
-                bank = bank_tile(("out", step, first), number[first // 2], [2, QUARTER])
+                bank = bank_tile(("out", q, first), numbers[first // 2], [2, QUARTER])
                 tiles = range(first, min(first + 2, N_TILES))
                 for c in tiles:
                     nc.tensor.matmul_mx(
                         out=bank[:, c - first, :],
                         lhsT=second["w4_codes"][:, P * c : P * (c + 1)].bitcast(FP8X4),
                         lhsT_scale=second["w4_scales"][:, P * c : P * (c + 1)],
-                        rhs=h_codes[step][:].bitcast(FP8X4),
-                        rhs_scale=h_scales[step][:],
+                        rhs=h_codes[q][:].bitcast(FP8X4),
+                        rhs_scale=h_scales[q][:],
                         start=True,
                         stop=True,
                     )
                 for c in tiles:
-                    dst, acc, bias = result[step][:, c, :], bank[:, c - first, :], src_col[:, c : c + 1]
+                    dst, acc, bias = result[:, c, :], bank[:, c - first, :], src_col[:, c : c + 1]
                     if c in on_vector:
                         nc.vector.tensor_scalar(dst, acc, bias, None, ALU.add)
                     else:
                         nc.scalar.activation(dst, acc, ACT.Identity, bias=bias)
-                    if step >= 2:
-                        nc.sync.dma_start(out_rows[:, c, step * QUARTER : (step + 1) * QUARTER], dst)
-            if step < 2:
-                nc.sync.dma_start(out_rows[:, :, step * QUARTER : (step + 1) * QUARTER], result[step][:])
+                    if q >= 2:
+                        nc.sync.dma_start(out_rows[:, c, q * QUARTER : (q + 1) * QUARTER], dst)
+            if q < 2:
+                nc.sync.dma_start(out_rows[:, :, q * QUARTER : (q + 1) * QUARTER], result[:])
 
+        whole = slice(0, QUARTER)
+        fraction_product(0, range(4), 0)
+        take_fractions(0, range(4))
+        product("right", ["w3"], 0, (6, 7))
         for u in range(2):
-            round_w2_on_scalar(0, u)
+            round_w2_on_vector(0, u)
+        for u in range(2):
             quantise_w2(0, u)
         round_w2_on_vector(1, 0)
-        round_w2_on_vector(1, 1)
+        round_w2_on_scalar(1, 1)
+        weigh_right("right", 0, (0,))
         quantise_w2(1, 0)
+        weigh_right("right", 0, (1,))
         quantise_w2(1, 1)
-        for a in range(PASSES):
-            for half in range(2):
-                fraction_product(half, a)
-        for half in range(2):
-            take_fractions(half)
-        product(0, 0)
-        product(1, 4)
+        product("left", ["w2"], 0, (0, 1))
+        fraction_product(1, (0, 1), 4)
+        take_fractions(1, (0, 1))
+        fraction_product(1, (2, 3), 4)
+        take_fractions(1, (2, 3))
         round_w4()
-        weigh(0)
+        product("right", ["w3"], 1, (4, 5))
+        product("left", ["w2"], 1, (2, 3), (1, 0))
+        weigh_left(0, 0, QUARTER)
 
-        rounded_tile((0, 0), QUARTER, 0, OVERLAP)
-        join(nc.gpsimd, 0, 0, QUARTER)
-        weigh(1)
-        product(2, 0)
-        for u in range(2):
-            difference_product(last, u, 4 + u)
+        h_rounded[0] = rounded_tile("h_rounded0", QUARTER, ROUNDED_AT, OVERLAP)
+        join(nc.gpsimd, 0, 0, QUARTER, h_rounded[0])
+        weigh_right("right", 1)
+        weigh_left(1, 0, QUARTER)
+        product("right", ["w3"], 2, (0, 1))
+        product("left", ["w2"], 2, (6, 7))
+        product("difference", ["w3", "w2"], 3, (4, 5))
         quantise_w4()
-        code_tiles(0, FRACTION_AT[1], FRACTION_AT[1] + 4 * QUARTER)
-        quantise_h(0, 0, QUARTER)
+        code_tiles(0, FRACTION_AT[1, 1], FRACTION_AT[1, 1] + 4 * QUARTER)
+        quantise_h(0, whole, h_rounded[0])
 
-        rounded_tile((1, 0), QUARTER, 8 * QUARTER, OVERLAP)
-        join(nc.gpsimd, 1, 0, QUARTER)
-        weigh(2)
-        tendencies(0, (0, 1), [(0, QUARTER)])
+        h_rounded[1] = rounded_tile("h_rounded1", QUARTER, ROUNDED_AT + ROUNDED_BYTES, OVERLAP)
+        join(nc.gpsimd, 1, 0, QUARTER, h_rounded[1])
+        weigh_right("right", 2)
+        weigh_left(2, 0, EIGHTH)
+        weigh_left(2, EIGHTH, QUARTER)
+        left_by_cells(3, (0,), 2)
+        left_by_cells(3, (1,), 3)
+        tendencies(0, (0, 1))
+        weigh_right("difference", 3, (0,))
+        code_tiles(1, FRACTION_AT[3, 0], FRACTION_AT[2, 1])
+        quantise_h(1, whole, h_rounded[1])
+        tendencies(1, (6, 7))
+
+        first_cells = rounded_tile("h_rounded2_first", EIGHTH, ROUNDED_AT + 2 * ROUNDED_BYTES)
+        join(nc.gpsimd, 2, 0, EIGHTH, first_cells)
+        weigh_right("difference", 3, (1,))
+        h_rounded[3] = rounded_tile("h_rounded3", QUARTER, None)
         for side in range(2):
-            left_product(last, side, 6 + side)
-        scale_difference()
-        code_tiles(1, FRACTION_AT[3], FRACTION_AT[2])
-        quantise_h(1, 0, QUARTER)
-        tendencies(1, (2, 3), [(QUARTER, QUARTER)])
-
-        rounded_tile((2, 0), EIGHTH, 16 * QUARTER, 0)
-        join(nc.gpsimd, 2, 0, EIGHTH)
-        add_left()
-        freed = PARTS0_AT + 2 * PARTS_BYTES + PARTS_BYTES // 2
-        code_tiles(last, freed, FRACTION_AT[0])
-        quantise_h(last, 0, QUARTER)
-        tendencies(last, (4, 5), [(last * QUARTER, QUARTER)])
-        rounded_tile((2, EIGHTH), EIGHTH, freed + 4 * QUARTER, 0)
-        join(nc.vector, 2, EIGHTH, QUARTER)
-        code_tiles(2, FRACTION_AT[0] + 2 * QUARTER, FRACTION_AT[0] + QUARTER)
-        quantise_h(2, 0, EIGHTH)
-        quantise_h(2, EIGHTH, QUARTER)
-        tendencies(2, (6, 7), [(2 * QUARTER, QUARTER)], on_vector=(0, 1))
+            add_left(3, side, h_rounded[3])
+        code_tiles(3, LEFT_PART_AT[2, 0])
+        quantise_h(3, whole, h_rounded[3])
+        tendencies(3, (4, 5))
+        last_cells = rounded_tile("h_rounded2_last", EIGHTH, SCALED_AT + 8 * QUARTER)
+        join(nc.vector, 2, EIGHTH, QUARTER, last_cells)
+        code_tiles(2, SCALED_AT + 4 * QUARTER, SCALED_AT + QUARTER)
+        quantise_h(2, slice(0, EIGHTH), first_cells)
+        quantise_h(2, slice(EIGHTH, QUARTER), last_cells)
+        tendencies(2, (2, 3), on_vector=(0, 1))

@@ -40,7 +40,8 @@ RAW_W2_BYTES = 4 * 4 * H
 RAW_W2_0_AT = RAW_W4_AT + 4 * (SRC_AT + 2 * SRC_PAD)
 RAW_W1_AT = RAW_W2_0_AT + RAW_W2_BYTES - OVERLAP
 RAW_W1_BYTES = PASSES * 2 * H + 2 * OVERLAP
-RAW_W2_AT = (RAW_W2_0_AT, RAW_W1_AT + RAW_W1_BYTES - OVERLAP)
+WINDOW1_AT = RAW_W2_0_AT
+RAW_W2_AT = (None, RAW_W1_AT + RAW_W1_BYTES - OVERLAP)
 ROUNDED_BYTES = 2 * 4 * QUARTER
 ROUNDED_AT = RAW_W2_AT[1] + RAW_W2_BYTES
 SLOT_BYTES = 4 * 2 * QUARTER
@@ -94,16 +95,16 @@ def tile_list_tracer_departure_blend_kernel(
         word_window, raw_w2 = {}, {}
 
         def load_words(a):
-            word_window[a] = held([P, T], I32, "word_window%d" % a)
+            word_window[a] = held([P, T], I32, "word_window%d" % a, WINDOW1_AT if a == 1 else None)
             nc.sync.dma_start(word_window[a][:], tab_words[a].rearrange("p t i -> p (t i)").bitcast(I32))
 
         def load_w2(a):
-            raw = placed([P, 4 * H], F32, "raw_w2_%d" % a, RAW_W2_AT[a])
+            raw = held([P, 4 * H], F32, "raw_w2_%d" % a, RAW_W2_AT[a])
             raw_w2[a] = raw[:].rearrange("p (j r) -> p j r", j=4)
             nc.sync.dma_start(raw_w2[a], w2[K_PASS * a : K_PASS * (a + 1), :].rearrange("(p j) r -> p j r", j=4))
 
         load_words(0)
-        load_words(1)
+        load_w2(0)
         padded_w3 = placed([P, PASSES * H + OVERLAP // 4], I32, "raw_w3", RAW_W3_AT)
         raw_w3 = padded_w3[:, : PASSES * H].rearrange("p (a c) -> p a c", a=PASSES)
         nc.sync.dma_start(
@@ -119,7 +120,7 @@ def tile_list_tracer_departure_blend_kernel(
                 raw[:].rearrange("p (c t) -> p t c", t=4),
             )
         nc.vector.tensor_copy(spread[:, V_AT // 4 :], picked.bitcast(I32))
-        for d in range(4):
+        for d in (0, 2, 1, 3):
             nc.sync.dma_start(plane_words[32 * d : 32 * d + 4, :], spread[32 * d : 32 * d + 32 : 4, :])
 
         w1_codes = placed([P, PASSES, 4, 2 * P], U8, "w1_codes", W1_CODES_AT)
@@ -127,7 +128,7 @@ def tile_list_tracer_departure_blend_kernel(
             w1_codes[:].bitcast(I32).rearrange("p a t (c i) -> p a t c i", i=2),
             raw_w1.rearrange("p a (c t i) -> p a t c i", t=4, i=2),
         )
-        load_w2(0)
+        load_words(1)
         load_w2(1)
 
         def v_scales(a, lo, width):
@@ -146,12 +147,12 @@ def tile_list_tracer_departure_blend_kernel(
 
         gather_words(0, 0)
         gather_words(0, 1)
-        gather_words(1, 0)
         w3_codes = held([P, PASSES, 4, P], I32, "w3_codes")
         nc.vector.tensor_copy(
             w3_codes[:].rearrange("p a t (c i) -> p a t c i", i=4),
             raw_w3.rearrange("p a (c t i) -> p a t c i", t=4, i=4),
         )
+        gather_words(1, 0)
         gather_words(1, 1)
 
         raw4 = placed([P, SRC_AT + SRC_PAD], F32, "raw_w4", RAW_W4_AT)
@@ -182,9 +183,8 @@ def tile_list_tracer_departure_blend_kernel(
 
         def round_w2_on_scalar(a, u):
             for e in range(2):
-                rows = raw_w2[a].rearrange("p j (c t i) -> p t c j i", t=4, i=4)[:, 2 * u + e]
-                dst = w2_rounded[a, u][:, e].rearrange("p c i j -> p c j i")
-                nc.scalar.activation(dst, rows, ACT.Copy, scale=-1.0)
+                rows = raw_w2[a].rearrange("p j (c t i) -> p t c i j", t=4, i=4)[:, 2 * u + e]
+                nc.scalar.activation(w2_rounded[a, u][:, e], rows, ACT.Copy, scale=-1.0)
 
         def quantise_w2(a, u):
             nc.vector.quantize_mx(
@@ -333,18 +333,19 @@ def tile_list_tracer_departure_blend_kernel(
                 in_=rounded.rearrange("p j u e -> p (j u e)"),
             )
 
-        def tendencies(q, numbers, on_vector=()):
-            result = held([P, N_TILES, QUARTER], F32, "result%d" % q)
+        def tendencies(q, lo, hi, numbers, on_vector=(), by_tile=False):
+            result = held([P, N_TILES, hi - lo], F32, "result%d_%d" % (q, lo))
+            cols = slice(q * QUARTER + lo, q * QUARTER + hi)
             for first in range(0, N_TILES, 2):
-                bank = bank_tile(("out", q, first), numbers[first // 2], [2, QUARTER])
+                bank = bank_tile(("out", q, first), numbers[first // 2], [2, hi - lo])
                 tiles = range(first, min(first + 2, N_TILES))
                 for c in tiles:
                     nc.tensor.matmul_mx(
                         out=bank[:, c - first, :],
                         lhsT=second["w4_codes"][:, P * c : P * (c + 1)].bitcast(FP8X4),
                         lhsT_scale=second["w4_scales"][:, P * c : P * (c + 1)],
-                        rhs=h_codes[q][:].bitcast(FP8X4),
-                        rhs_scale=h_scales[q][:],
+                        rhs=h_codes[q][:, lo:hi].bitcast(FP8X4),
+                        rhs_scale=h_scales[q][:, lo:hi],
                         start=True,
                         stop=True,
                     )
@@ -354,33 +355,29 @@ def tile_list_tracer_departure_blend_kernel(
                         nc.vector.tensor_scalar(dst, acc, bias, None, ALU.add)
                     else:
                         nc.scalar.activation(dst, acc, ACT.Identity, bias=bias)
-                    if q >= 2:
-                        nc.sync.dma_start(out_rows[:, c, q * QUARTER : (q + 1) * QUARTER], dst)
-            if q < 2:
-                nc.sync.dma_start(out_rows[:, :, q * QUARTER : (q + 1) * QUARTER], result[:])
+                    if by_tile:
+                        nc.sync.dma_start(out_rows[:, c, cols], dst)
+            if not by_tile:
+                nc.sync.dma_start(out_rows[:, :, cols], result[:])
 
         whole = slice(0, QUARTER)
-        fraction_product(0, range(4), 0)
-        take_fractions(0, range(4))
-        product("right", ["w3"], 0, (6, 7))
         for u in range(2):
-            round_w2_on_vector(0, u)
-        for u in range(2):
+            round_w2_on_scalar(0, u)
             quantise_w2(0, u)
-        round_w2_on_vector(1, 0)
-        round_w2_on_scalar(1, 1)
-        weigh_right("right", 0, (0,))
-        quantise_w2(1, 0)
-        weigh_right("right", 0, (1,))
-        quantise_w2(1, 1)
-        product("left", ["w2"], 0, (0, 1))
-        fraction_product(1, (0, 1), 4)
-        take_fractions(1, (0, 1))
-        fraction_product(1, (2, 3), 4)
-        take_fractions(1, (2, 3))
-        round_w4()
+        for u in range(2):
+            round_w2_on_vector(1, u)
+        for u in range(2):
+            quantise_w2(1, u)
+        for half in range(2):
+            fraction_product(half, range(4), 4 * half)
+        for half in range(2):
+            take_fractions(half, range(4))
+        product("right", ["w3"], 0, (0, 1))
+        product("left", ["w2"], 0, (2, 3))
         product("right", ["w3"], 1, (4, 5))
-        product("left", ["w2"], 1, (2, 3), (1, 0))
+        product("left", ["w2"], 1, (6, 7))
+        round_w4()
+        weigh_right("right", 0)
         weigh_left(0, 0, QUARTER)
 
         h_rounded[0] = rounded_tile("h_rounded0", QUARTER, ROUNDED_AT, OVERLAP)
@@ -388,7 +385,7 @@ def tile_list_tracer_departure_blend_kernel(
         weigh_right("right", 1)
         weigh_left(1, 0, QUARTER)
         product("right", ["w3"], 2, (0, 1))
-        product("left", ["w2"], 2, (6, 7))
+        product("left", ["w2"], 2, (2, 3))
         product("difference", ["w3", "w2"], 3, (4, 5))
         quantise_w4()
         code_tiles(0, FRACTION_AT[1, 1], FRACTION_AT[1, 1] + 4 * QUARTER)
@@ -399,13 +396,13 @@ def tile_list_tracer_departure_blend_kernel(
         weigh_right("right", 2)
         weigh_left(2, 0, EIGHTH)
         weigh_left(2, EIGHTH, QUARTER)
-        left_by_cells(3, (0,), 2)
-        left_by_cells(3, (1,), 3)
-        tendencies(0, (0, 1))
+        left_by_cells(3, (0,), 6)
+        left_by_cells(3, (1,), 7)
+        tendencies(0, 0, QUARTER, (0, 1))
         weigh_right("difference", 3, (0,))
         code_tiles(1, FRACTION_AT[3, 0], FRACTION_AT[2, 1])
         quantise_h(1, whole, h_rounded[1])
-        tendencies(1, (6, 7))
+        tendencies(1, 0, QUARTER, (2, 3))
 
         first_cells = rounded_tile("h_rounded2_first", EIGHTH, ROUNDED_AT + 2 * ROUNDED_BYTES)
         join(nc.gpsimd, 2, 0, EIGHTH, first_cells)
@@ -413,12 +410,13 @@ def tile_list_tracer_departure_blend_kernel(
         h_rounded[3] = rounded_tile("h_rounded3", QUARTER, None)
         for side in range(2):
             add_left(3, side, h_rounded[3])
-        code_tiles(3, LEFT_PART_AT[2, 0])
-        quantise_h(3, whole, h_rounded[3])
-        tendencies(3, (4, 5))
-        last_cells = rounded_tile("h_rounded2_last", EIGHTH, SCALED_AT + 8 * QUARTER)
-        join(nc.vector, 2, EIGHTH, QUARTER, last_cells)
         code_tiles(2, SCALED_AT + 4 * QUARTER, SCALED_AT + QUARTER)
         quantise_h(2, slice(0, EIGHTH), first_cells)
+        tendencies(2, 0, EIGHTH, (0, 1))
+        code_tiles(3, LEFT_PART_AT[2, 0])
+        quantise_h(3, whole, h_rounded[3])
+        tendencies(3, 0, QUARTER, (4, 5), by_tile=True)
+        last_cells = rounded_tile("h_rounded2_last", EIGHTH, SCALED_AT + 8 * QUARTER)
+        join(nc.vector, 2, EIGHTH, QUARTER, last_cells)
         quantise_h(2, slice(EIGHTH, QUARTER), last_cells)
-        tendencies(2, (2, 3), on_vector=(0, 1))
+        tendencies(2, EIGHTH, QUARTER, (6, 7), on_vector=(0, 1))

@@ -34,10 +34,11 @@ W1_CODES_AT = 0
 V0_AT = (W1_CODES_AT + PASSES * 2 * H, W1_CODES_AT + PASSES * 2 * H + 4 * HALF)
 PICKED_AT = V0_AT[0] - OVERLAP
 PICKED_BYTES = 2 * 4 * HALF + 2 * OVERLAP
-RAW_W3_AT = PICKED_AT + PICKED_BYTES
+WINDOW0_AT = PICKED_AT + PICKED_BYTES
+RAW_W3_AT = WINDOW0_AT
 RAW_W4_AT = RAW_W3_AT + PASSES * 4 * H
 RAW_W2_BYTES = 4 * 4 * H
-RAW_W2_0_AT = RAW_W4_AT + 4 * (SRC_AT + 2 * SRC_PAD)
+RAW_W2_0_AT = RAW_W4_AT + 4 * T
 RAW_W1_AT = RAW_W2_0_AT + RAW_W2_BYTES - OVERLAP
 RAW_W1_BYTES = PASSES * 2 * H + 2 * OVERLAP
 WINDOW1_AT = RAW_W2_0_AT
@@ -50,7 +51,8 @@ FRACTION_AT = dict(
     [((q, u), RAW_W2_AT[1] + (q % 2 * 2 + u) * SLOT_BYTES) for q in (2, 3) for u in range(2)] + [((1, 1), SLOTS_AT)]
 )
 SCALED_AT = SLOTS_AT + 4 * SLOT_BYTES
-LEFT_PART_AT = {(0, 0): SLOTS_AT + SLOT_BYTES, (2, 0): SLOTS_AT + 3 * SLOT_BYTES}
+RIGHT_PART_AT = {(0, EIGHTH): SLOTS_AT + SLOT_BYTES}
+LEFT_PART_AT = { (2, 0): SLOTS_AT + 3 * SLOT_BYTES}
 
 
 def tile_list_tracer_departure_blend_kernel(
@@ -95,7 +97,7 @@ def tile_list_tracer_departure_blend_kernel(
         word_window, raw_w2 = {}, {}
 
         def load_words(a):
-            word_window[a] = held([P, T], I32, "word_window%d" % a, WINDOW1_AT if a == 1 else None)
+            word_window[a] = held([P, T], I32, "word_window%d" % a, (WINDOW0_AT, WINDOW1_AT)[a])
             nc.sync.dma_start(word_window[a][:], tab_words[a].rearrange("p t i -> p (t i)").bitcast(I32))
 
         def load_w2(a):
@@ -105,11 +107,6 @@ def tile_list_tracer_departure_blend_kernel(
 
         load_words(0)
         load_w2(0)
-        padded_w3 = placed([P, PASSES * H + OVERLAP // 4], I32, "raw_w3", RAW_W3_AT)
-        raw_w3 = padded_w3[:, : PASSES * H].rearrange("p (a c) -> p a c", a=PASSES)
-        nc.sync.dma_start(
-            raw_w3, w3_words.rearrange("a p c i -> a p (c i)").bitcast(I32).rearrange("a p c -> p a c")
-        )
 
         picked = placed([P, PICKED_BYTES], U8, "picked_scales", PICKED_AT)[:, :S]
         nc.vector.tensor_copy(picked, scale_window[:].indirect(offsets[:]))
@@ -147,10 +144,9 @@ def tile_list_tracer_departure_blend_kernel(
 
         gather_words(0, 0)
         gather_words(0, 1)
-        w3_codes = held([P, PASSES, 4, P], I32, "w3_codes")
-        nc.vector.tensor_copy(
-            w3_codes[:].rearrange("p a t (c i) -> p a t c i", i=4),
-            raw_w3.rearrange("p a (c t i) -> p a t c i", t=4, i=4),
+        raw_w3 = placed([P, PASSES, H], I32, "raw_w3", RAW_W3_AT)
+        nc.sync.dma_start(
+            raw_w3[:], w3_words.rearrange("a p c i -> a p (c i)").bitcast(I32).rearrange("a p c -> p a c")
         )
         gather_words(1, 0)
         gather_words(1, 1)
@@ -163,6 +159,14 @@ def tile_list_tracer_departure_blend_kernel(
             nc.sync.dma_start(raw_w4[:, t, :], w4_rows[t])
         with nc.allow_non_contiguous_dma(reason="one source value a partition"):
             nc.sync.dma_start(src_col, src.rearrange("(c p) -> p c", p=P))
+
+        w3_codes = held([P, PASSES, 4, P], I32, "w3_codes")
+
+        def move_w3():
+            nc.vector.tensor_copy(
+                w3_codes[:].rearrange("p a t (c i) -> p a t c i", i=4),
+                raw_w3[:].rearrange("p a (c t i) -> p a t c i", t=4, i=4),
+            )
 
         w2_rounded, w2_codes, w2_scales = {}, {}, {}
         for a in range(PASSES):
@@ -204,7 +208,7 @@ def tile_list_tracer_departure_blend_kernel(
         second = {}
 
         def quantise_w4():
-            second["w4_codes"] = placed([P, N], U32, "w4_codes", LEFT_PART_AT[0, 0])
+            second["w4_codes"] = placed([P, N], U32, "w4_codes", RIGHT_PART_AT[0, EIGHTH])
             second["w4_scales"] = placed([P, N], U8, "w4_scales", FRACTION_AT[1, 1] + 5 * QUARTER)
             for lo, hi in ((0, W4_SPLIT), (W4_SPLIT, N)):
                 nc.vector.quantize_mx(
@@ -290,12 +294,13 @@ def tile_list_tracer_departure_blend_kernel(
         def fractions(q, u):
             return fraction[q, u][:].rearrange("p e j -> p j e")
 
-        def weigh_right(key, q, pairs=(0, 1)):
-            if pairs[0] == 0:
-                at = SCALED_AT if key == "difference" else None
-                right_part[q] = held([P, 2, QUARTER, 2], F32, "right_part%d" % q, at)
-            for u in pairs:
-                nc.vector.tensor_tensor(right_part[q][:, u], fractions(q, u), sums(key, q, u), ALU.mult)
+        def weigh_right(key, q, lo=0, hi=QUARTER):
+            at = SCALED_AT if key == "difference" else RIGHT_PART_AT.get((q, lo))
+            right_part[q, lo] = held([P, 2, hi - lo, 2], F32, "right_part%d_%d" % (q, lo), at)
+            for u in range(2):
+                nc.vector.tensor_tensor(
+                    right_part[q, lo][:, u], fractions(q, u)[:, lo:hi], sums(key, q, u)[:, lo:hi], ALU.mult
+                )
 
         def weigh_left(q, lo, hi):
             name = "left_part%d_%d" % (q, lo)
@@ -310,12 +315,15 @@ def tile_list_tracer_departure_blend_kernel(
             padded = held([P, 4 * width + pad // 2], BF16, name, at)
             return padded[:, : 4 * width].rearrange("p (j u e) -> p j u e", u=2, e=2)
 
+        def cells_of(parts, q, lo, hi):
+            first = lo if (q, lo) in parts else 0
+            return parts[q, first][:, :, lo - first : hi - first, :].rearrange("p u j e -> p j u e")
+
         def right_of(q, lo, hi):
-            return right_part[q][:, :, lo:hi, :].rearrange("p u j e -> p j u e")
+            return cells_of(right_part, q, lo, hi)
 
         def join(engine, q, lo, hi, dst):
-            left = left_part[q, lo][:].rearrange("p u j e -> p j u e")
-            engine.tensor_tensor(dst, right_of(q, lo, hi), left, ALU.add)
+            engine.tensor_tensor(dst, right_of(q, lo, hi), cells_of(left_part, q, lo, hi), ALU.add)
 
         def add_left(q, side, dst):
             left = banks["by_cells", side][:].rearrange("p (u e) j -> p j u e", u=2)
@@ -368,20 +376,21 @@ def tile_list_tracer_departure_blend_kernel(
             round_w2_on_vector(1, u)
         for u in range(2):
             quantise_w2(1, u)
+        move_w3()
         for half in range(2):
             fraction_product(half, range(4), 4 * half)
         for half in range(2):
             take_fractions(half, range(4))
-        product("right", ["w3"], 0, (0, 1))
-        product("left", ["w2"], 0, (2, 3))
+        product("left", ["w2"], 0, (0, 1))
+        product("right", ["w3"], 0, (2, 3))
         product("right", ["w3"], 1, (4, 5))
         product("left", ["w2"], 1, (6, 7))
         round_w4()
-        weigh_right("right", 0)
         weigh_left(0, 0, QUARTER)
-
         h_rounded[0] = rounded_tile("h_rounded0", QUARTER, ROUNDED_AT, OVERLAP)
-        join(nc.gpsimd, 0, 0, QUARTER, h_rounded[0])
+        for lo in (0, EIGHTH):
+            weigh_right("right", 0, lo, lo + EIGHTH)
+            join(nc.gpsimd, 0, lo, lo + EIGHTH, h_rounded[0][:, lo : lo + EIGHTH])
         weigh_right("right", 1)
         weigh_left(1, 0, QUARTER)
         product("right", ["w3"], 2, (0, 1))
@@ -399,14 +408,13 @@ def tile_list_tracer_departure_blend_kernel(
         left_by_cells(3, (0,), 6)
         left_by_cells(3, (1,), 7)
         tendencies(0, 0, QUARTER, (0, 1))
-        weigh_right("difference", 3, (0,))
-        code_tiles(1, FRACTION_AT[3, 0], FRACTION_AT[2, 1])
+        weigh_right("difference", 3)
+        code_tiles(1, FRACTION_AT[3, 1], FRACTION_AT[2, 1])
         quantise_h(1, whole, h_rounded[1])
         tendencies(1, 0, QUARTER, (2, 3))
 
         first_cells = rounded_tile("h_rounded2_first", EIGHTH, ROUNDED_AT + 2 * ROUNDED_BYTES)
         join(nc.gpsimd, 2, 0, EIGHTH, first_cells)
-        weigh_right("difference", 3, (1,))
         h_rounded[3] = rounded_tile("h_rounded3", QUARTER, None)
         for side in range(2):
             add_left(3, side, h_rounded[3])

@@ -25,26 +25,23 @@ QUARTERS = S // QUARTER
 EIGHTH = QUARTER // 2
 HALF = S // 2
 N_TILES = N // P
-W1_AT, W3_AT, V_AT, PLANE = 0, H, 2 * H, 2 * H + S
 W4_SPLIT = 256
 SRC_AT = 4 * N
 SRC_PAD = 8
 OVERLAP = 64
-W1_CODES_AT = 0
+PLANE = H + S
+RAW_W2_BYTES = 4 * 4 * H
+WINDOW1_AT = 0
+PICKED_AT = WINDOW1_AT + 4 * T - OVERLAP
+W1_CODES_AT = PICKED_AT + OVERLAP
 V0_AT = (W1_CODES_AT + PASSES * 2 * H, W1_CODES_AT + PASSES * 2 * H + 4 * HALF)
-PICKED_AT = V0_AT[0] - OVERLAP
-PICKED_BYTES = 2 * 4 * HALF + 2 * OVERLAP
-WINDOW0_AT = PICKED_AT + PICKED_BYTES
+PICKED_BYTES = PASSES * 2 * H + 2 * 4 * HALF + 2 * OVERLAP
+RAW_W2_AT = (None, PICKED_AT + PICKED_BYTES - OVERLAP)
+WINDOW0_AT = RAW_W2_AT[1] + RAW_W2_BYTES
 RAW_W3_AT = WINDOW0_AT
 RAW_W4_AT = RAW_W3_AT + PASSES * 4 * H
-RAW_W2_BYTES = 4 * 4 * H
-RAW_W2_0_AT = RAW_W4_AT + 4 * T
-RAW_W1_AT = RAW_W2_0_AT + RAW_W2_BYTES - OVERLAP
-RAW_W1_BYTES = PASSES * 2 * H + 2 * OVERLAP
-WINDOW1_AT = RAW_W2_0_AT
-RAW_W2_AT = (None, RAW_W1_AT + RAW_W1_BYTES - OVERLAP)
 ROUNDED_BYTES = 2 * 4 * QUARTER
-ROUNDED_AT = RAW_W2_AT[1] + RAW_W2_BYTES
+ROUNDED_AT = WINDOW0_AT + 6 * T
 SLOT_BYTES = 4 * 2 * QUARTER
 SLOTS_AT = ROUNDED_AT + 3 * ROUNDED_BYTES
 FRACTION_AT = dict(
@@ -52,7 +49,7 @@ FRACTION_AT = dict(
 )
 SCALED_AT = SLOTS_AT + 4 * SLOT_BYTES
 RIGHT_PART_AT = {(0, EIGHTH): SLOTS_AT + SLOT_BYTES}
-LEFT_PART_AT = { (2, 0): SLOTS_AT + 3 * SLOT_BYTES}
+LEFT_PART_AT = {(0, 0): RAW_W3_AT, (2, 0): SLOTS_AT + 3 * SLOT_BYTES}
 
 
 def tile_list_tracer_departure_blend_kernel(
@@ -74,8 +71,8 @@ def tile_list_tracer_departure_blend_kernel(
 
         offsets = keep.tile([P, S // PER_COLUMN], U16, name="offsets")
         nc.sync.dma_start(offsets[:], offs)
-        padded_w1 = placed([P, RAW_W1_BYTES // 4], I32, "raw_w1", RAW_W1_AT)
-        raw_w1 = padded_w1[:, :H].rearrange("p (a c) -> p a c", a=PASSES)
+        landing = held([P, H], I32, "landing")
+        raw_w1 = landing[:].rearrange("p (a c) -> p a c", a=PASSES)
         nc.sync.dma_start(raw_w1, w1_words.bitcast(I32).rearrange("a p c -> p a c"))
 
         scale_window = held([P, T], U8, "scale_window")
@@ -83,16 +80,14 @@ def tile_list_tracer_departure_blend_kernel(
         nc.sync.dma_start(
             scale_window[:].bitcast(I32)[0:P:4, :], tab_scales.bitcast(I32).rearrange("a q t -> q a t")
         )
-        raw_scales = []
-        for w, scales in enumerate((w1_scales, w3_scales)):
-            raw = held([P, H // 4], I32, "raw_scales%d" % w)
-            nc.vector.memset(raw[:], 0)
-            nc.sync.dma_start(raw[0:P:4, :], scales.bitcast(I32).rearrange("a q c -> q a c"))
-            raw_scales.append(raw)
 
-        plane = held([P, PASSES, PLANE], U8, "plane")
-        plane_words = plane[:].rearrange("p a s -> p (a s)").bitcast(I32)
-        nc.vector.memset(plane_words, 0)
+        def move_scales(name, raw):
+            ordered = held([P, PASSES, H], U8, name)
+            nc.vector.tensor_copy(
+                ordered[:].bitcast(I32).rearrange("p a (t c) -> p a t c", t=4),
+                raw.rearrange("p a (c t) -> p a t c", t=4),
+            )
+            return ordered
 
         word_window, raw_w2 = {}, {}
 
@@ -105,18 +100,23 @@ def tile_list_tracer_departure_blend_kernel(
             raw_w2[a] = raw[:].rearrange("p (j r) -> p j r", j=4)
             nc.sync.dma_start(raw_w2[a], w2[K_PASS * a : K_PASS * (a + 1), :].rearrange("(p j) r -> p j r", j=4))
 
+        raw_w1_scales = held([P, H // 4], I32, "raw_w1_scales")
+        nc.vector.memset(raw_w1_scales[:], 0)
+        nc.sync.dma_start(raw_w1_scales[0:P:4, :], w1_scales.bitcast(I32).rearrange("a q c -> q a c"))
         load_words(0)
         load_w2(0)
+        plane = held([P, PASSES, PLANE], U8, "plane")
+        plane_words = plane[:].rearrange("p a s -> p (a s)").bitcast(I32)
+        nc.vector.memset(plane_words, 0)
 
         picked = placed([P, PICKED_BYTES], U8, "picked_scales", PICKED_AT)[:, :S]
         nc.vector.tensor_copy(picked, scale_window[:].indirect(offsets[:]))
         spread = held([P, PLANE // 4], I32, "spread")
-        for w, raw in enumerate(raw_scales):
-            nc.vector.tensor_copy(
-                spread[:, w * H // 4 : (w + 1) * H // 4].rearrange("p (t c) -> p t c", t=4),
-                raw[:].rearrange("p (c t) -> p t c", t=4),
-            )
-        nc.vector.tensor_copy(spread[:, V_AT // 4 :], picked.bitcast(I32))
+        nc.vector.tensor_copy(
+            spread[:, : H // 4].rearrange("p (t c) -> p t c", t=4),
+            raw_w1_scales[:].rearrange("p (c t) -> p t c", t=4),
+        )
+        nc.vector.tensor_copy(spread[:, H // 4 :], picked.bitcast(I32))
         for d in (0, 2, 1, 3):
             nc.sync.dma_start(plane_words[32 * d : 32 * d + 4, :], spread[32 * d : 32 * d + 32 : 4, :])
 
@@ -125,11 +125,16 @@ def tile_list_tracer_departure_blend_kernel(
             w1_codes[:].bitcast(I32).rearrange("p a t (c i) -> p a t c i", i=2),
             raw_w1.rearrange("p a (c t i) -> p a t c i", t=4, i=2),
         )
+        planes = {}
         load_words(1)
         load_w2(1)
+        raw_w3_scales = landing[:, : PASSES * H // 4].rearrange("p (a c) -> p a c", a=PASSES)
+        w3_scale_rows = w3_scales.bitcast(I32).rearrange("a q c -> q a c")
+        for d in (0, 2, 1, 3):
+            nc.sync.dma_start(raw_w3_scales[32 * d : 32 * d + 4], w3_scale_rows[4 * d : 4 * d + 4])
 
         def v_scales(a, lo, width):
-            return plane[:, a, V_AT + lo : V_AT + lo + width]
+            return plane[:, a, H + lo : H + lo + width]
 
         v_halves = {}
 
@@ -163,6 +168,7 @@ def tile_list_tracer_departure_blend_kernel(
         w3_codes = held([P, PASSES, 4, P], I32, "w3_codes")
 
         def move_w3():
+            planes["w3"] = move_scales("w3_plane", raw_w3_scales)
             nc.vector.tensor_copy(
                 w3_codes[:].rearrange("p a t (c i) -> p a t c i", i=4),
                 raw_w3[:].rearrange("p a (c t i) -> p a t c i", t=4, i=4),
@@ -224,7 +230,7 @@ def tile_list_tracer_departure_blend_kernel(
             ),
             "w3": (
                 lambda a, t: w3_codes[:, a, t, :].bitcast(FP8X4),
-                lambda a, t: plane[:, a, W3_AT + P * t : W3_AT + P * (t + 1)],
+                lambda a, t: planes["w3"][:, a, P * t : P * (t + 1)],
             ),
         }
         banks = {}
@@ -268,7 +274,7 @@ def tile_list_tracer_departure_blend_kernel(
                     nc.tensor.matmul_mx(
                         out=banks["w1", half, t][:],
                         lhsT=w1_codes[:, a, t, :].bitcast(FP4X4),
-                        lhsT_scale=plane[:, a, W1_AT + P * t : W1_AT + P * (t + 1)],
+                        lhsT_scale=plane[:, a, P * t : P * (t + 1)],
                         rhs=v_codes(a, half * HALF, HALF),
                         rhs_scale=v_scales(a, half * HALF, HALF),
                         start=(a == 0),
@@ -384,16 +390,16 @@ def tile_list_tracer_departure_blend_kernel(
         product("left", ["w2"], 0, (0, 1))
         product("right", ["w3"], 0, (2, 3))
         product("right", ["w3"], 1, (4, 5))
-        product("left", ["w2"], 1, (6, 7))
         round_w4()
         weigh_left(0, 0, QUARTER)
+        product("left", ["w2"], 1, (0, 1))
         h_rounded[0] = rounded_tile("h_rounded0", QUARTER, ROUNDED_AT, OVERLAP)
         for lo in (0, EIGHTH):
             weigh_right("right", 0, lo, lo + EIGHTH)
             join(nc.gpsimd, 0, lo, lo + EIGHTH, h_rounded[0][:, lo : lo + EIGHTH])
         weigh_right("right", 1)
         weigh_left(1, 0, QUARTER)
-        product("right", ["w3"], 2, (0, 1))
+        product("right", ["w3"], 2, (6, 7))
         product("left", ["w2"], 2, (2, 3))
         product("difference", ["w3", "w2"], 3, (4, 5))
         quantise_w4()
@@ -405,9 +411,9 @@ def tile_list_tracer_departure_blend_kernel(
         weigh_right("right", 2)
         weigh_left(2, 0, EIGHTH)
         weigh_left(2, EIGHTH, QUARTER)
-        left_by_cells(3, (0,), 6)
-        left_by_cells(3, (1,), 7)
-        tendencies(0, 0, QUARTER, (0, 1))
+        left_by_cells(3, (0,), 0)
+        left_by_cells(3, (1,), 1)
+        tendencies(0, 0, QUARTER, (6, 7))
         weigh_right("difference", 3)
         code_tiles(1, FRACTION_AT[3, 1], FRACTION_AT[2, 1])
         quantise_h(1, whole, h_rounded[1])
@@ -420,11 +426,11 @@ def tile_list_tracer_departure_blend_kernel(
             add_left(3, side, h_rounded[3])
         code_tiles(2, SCALED_AT + 4 * QUARTER, SCALED_AT + QUARTER)
         quantise_h(2, slice(0, EIGHTH), first_cells)
-        tendencies(2, 0, EIGHTH, (0, 1))
+        tendencies(2, 0, EIGHTH, (6, 7))
         code_tiles(3, LEFT_PART_AT[2, 0])
         quantise_h(3, whole, h_rounded[3])
         tendencies(3, 0, QUARTER, (4, 5), by_tile=True)
         last_cells = rounded_tile("h_rounded2_last", EIGHTH, SCALED_AT + 8 * QUARTER)
         join(nc.vector, 2, EIGHTH, QUARTER, last_cells)
         quantise_h(2, slice(EIGHTH, QUARTER), last_cells)
-        tendencies(2, EIGHTH, QUARTER, (6, 7), on_vector=(0, 1))
+        tendencies(2, EIGHTH, QUARTER, (0, 1), on_vector=(0, 1))

@@ -295,7 +295,11 @@ def tile_list_tracer_departure_blend_kernel(
                         name = "fraction%d_%d" % (q, t // 2)
                         fraction[q, t // 2] = held([P, 2, QUARTER], F32, name, FRACTION_AT.get((q, t // 2)))
                     sums_t = banks["w1", half, t][:, q % 2 * QUARTER : (q % 2 + 1) * QUARTER]
-                    nc.scalar.activation(fraction[q, t // 2][:, t % 2, :], sums_t, ACT.Sigmoid)
+                    nc.scalar.activation(fraction[q, t // 2][:, t % 2, :], sums_t, ACT.Tanh, scale=0.5)
+
+        def to_sigmoid(q):
+            for u in range(2):
+                nc.scalar.activation(fraction[q, u][:], fraction[q, u][:], ACT.Copy, scale=0.5, bias=0.5)
 
         def fractions(q, u):
             return fraction[q, u][:].rearrange("p e j -> p j e")
@@ -304,9 +308,13 @@ def tile_list_tracer_departure_blend_kernel(
             at = SCALED_AT if key == "difference" else RIGHT_PART_AT.get((q, lo))
             right_part[q, lo] = held([P, 2, hi - lo, 2], F32, "right_part%d_%d" % (q, lo), at)
             for u in range(2):
-                nc.vector.tensor_tensor(
-                    right_part[q, lo][:, u], fractions(q, u)[:, lo:hi], sums(key, q, u)[:, lo:hi], ALU.mult
-                )
+                if key == "difference":
+                    nc.vector.tensor_tensor(right_part[q, lo][:, u], fractions(q, u), sums(key, q, u), ALU.mult)
+                else:
+                    nc.vector.scalar_tensor_tensor(
+                        right_part[q, lo][:, u], fractions(q, u)[:, lo:hi], 1.0, sums(key, q, u)[:, lo:hi],
+                        ALU.add, ALU.mult,
+                    )
 
         def weigh_left(q, lo, hi):
             name = "left_part%d_%d" % (q, lo)
@@ -366,9 +374,9 @@ def tile_list_tracer_departure_blend_kernel(
                 for c in tiles:
                     dst, acc, bias = result[:, c, :], bank[:, c - first, :], src_col[:, c : c + 1]
                     if c in on_vector:
-                        nc.vector.tensor_scalar(dst, acc, bias, None, ALU.add)
+                        nc.vector.tensor_scalar(dst, acc, 0.5, bias, ALU.mult, ALU.add)
                     else:
-                        nc.scalar.activation(dst, acc, ACT.Identity, bias=bias)
+                        nc.scalar.activation(dst, acc, ACT.Identity, bias=bias, scale=1.0 if q == 3 else 0.5)
                     if by_tile:
                         nc.sync.dma_start(out_rows[:, c, cols], dst)
             if not by_tile:
@@ -390,6 +398,7 @@ def tile_list_tracer_departure_blend_kernel(
         product("left", ["w2"], 0, (0, 1))
         product("right", ["w3"], 0, (2, 3))
         product("right", ["w3"], 1, (4, 5))
+        to_sigmoid(3)
         round_w4()
         weigh_left(0, 0, QUARTER)
         product("left", ["w2"], 1, (0, 1))

@@ -36,7 +36,7 @@ PICKED_AT = WINDOW1_AT + 4 * T - OVERLAP
 W1_CODES_AT = PICKED_AT + OVERLAP
 V0_AT = (W1_CODES_AT + PASSES * 2 * H, W1_CODES_AT + PASSES * 2 * H + 4 * HALF)
 PICKED_BYTES = PASSES * 2 * H + 2 * 4 * HALF + 2 * OVERLAP
-RAW_W2_AT = (None, PICKED_AT + PICKED_BYTES - OVERLAP)
+RAW_W2_AT = (WINDOW1_AT, PICKED_AT + PICKED_BYTES - OVERLAP)
 WINDOW0_AT = RAW_W2_AT[1] + RAW_W2_BYTES
 RAW_W3_AT = WINDOW0_AT
 RAW_W4_AT = RAW_W3_AT + PASSES * 4 * H
@@ -45,7 +45,7 @@ ROUNDED_AT = WINDOW0_AT + 6 * T
 SLOT_BYTES = 4 * 2 * QUARTER
 SLOTS_AT = ROUNDED_AT + 3 * ROUNDED_BYTES
 FRACTION_AT = dict(
-    [((q, u), RAW_W2_AT[1] + (q % 2 * 2 + u) * SLOT_BYTES) for q in (2, 3) for u in range(2)] + [((1, 1), SLOTS_AT)]
+    [((q, u), RAW_W2_AT[q // 2] + (q % 2 * 2 + u) * SLOT_BYTES) for q in range(QUARTERS) for u in range(2)]
 )
 SCALED_AT = SLOTS_AT + 4 * SLOT_BYTES
 RIGHT_PART_AT = {(0, EIGHTH): SLOTS_AT + SLOT_BYTES}
@@ -92,7 +92,7 @@ def tile_list_tracer_departure_blend_kernel(
         word_window, raw_w2 = {}, {}
 
         def load_words(a):
-            word_window[a] = held([P, T], I32, "word_window%d" % a, (WINDOW0_AT, WINDOW1_AT)[a])
+            word_window[a] = held([P, T], I32, "word_window%d" % a, (WINDOW0_AT, None)[a])
             nc.sync.dma_start(word_window[a][:], tab_words[a].rearrange("p t i -> p (t i)").bitcast(I32))
 
         def load_w2(a):
@@ -104,7 +104,7 @@ def tile_list_tracer_departure_blend_kernel(
         nc.vector.memset(raw_w1_scales[:], 0)
         nc.sync.dma_start(raw_w1_scales[0:P:4, :], w1_scales.bitcast(I32).rearrange("a q c -> q a c"))
         load_words(0)
-        load_w2(0)
+        load_words(1)
         plane = held([P, PASSES, PLANE], U8, "plane")
         plane_words = plane[:].rearrange("p a s -> p (a s)").bitcast(I32)
         nc.vector.memset(plane_words, 0)
@@ -126,7 +126,7 @@ def tile_list_tracer_departure_blend_kernel(
             raw_w1.rearrange("p a (c t i) -> p a t c i", t=4, i=2),
         )
         planes = {}
-        load_words(1)
+        load_w2(0)
         load_w2(1)
         raw_w3_scales = landing[:, : PASSES * H // 4].rearrange("p (a c) -> p a c", a=PASSES)
         w3_scale_rows = w3_scales.bitcast(I32).rearrange("a q c -> q a c")
@@ -383,8 +383,9 @@ def tile_list_tracer_departure_blend_kernel(
                 nc.sync.dma_start(out_rows[:, :, cols], result[:])
 
         whole = slice(0, QUARTER)
+        round_w2_on_vector(0, 0)
+        round_w2_on_scalar(0, 1)
         for u in range(2):
-            round_w2_on_scalar(0, u)
             quantise_w2(0, u)
         for u in range(2):
             round_w2_on_vector(1, u)

@@ -25,7 +25,6 @@ QUARTERS = S // QUARTER
 EIGHTH = QUARTER // 2
 HALF = S // 2
 N_TILES = N // P
-W4_SPLIT = 256
 SRC_AT = 4 * N
 SRC_PAD = 8
 OVERLAP = 64
@@ -49,7 +48,8 @@ FRACTION_AT = dict(
 )
 SCALED_AT = SLOTS_AT + 4 * SLOT_BYTES
 RIGHT_PART_AT = {(0, EIGHTH): SLOTS_AT + SLOT_BYTES}
-LEFT_PART_AT = {(0, 0): RAW_W3_AT, (2, 0): SLOTS_AT + 3 * SLOT_BYTES}
+LEFT_PART_AT = {(0, 0): RAW_W3_AT, (1, 0): FRACTION_AT[0, 0], (2, 0): SLOTS_AT + 3 * SLOT_BYTES,
+                (2, EIGHTH): ROUNDED_AT + ROUNDED_BYTES}
 
 
 def tile_list_tracer_departure_blend_kernel(
@@ -81,14 +81,6 @@ def tile_list_tracer_departure_blend_kernel(
             scale_window[:].bitcast(I32)[0:P:4, :], tab_scales.bitcast(I32).rearrange("a q t -> q a t")
         )
 
-        def move_scales(name, raw):
-            ordered = held([P, PASSES, H], U8, name)
-            nc.vector.tensor_copy(
-                ordered[:].bitcast(I32).rearrange("p a (t c) -> p a t c", t=4),
-                raw.rearrange("p a (c t) -> p a t c", t=4),
-            )
-            return ordered
-
         word_window, raw_w2 = {}, {}
 
         def load_words(a):
@@ -100,9 +92,10 @@ def tile_list_tracer_departure_blend_kernel(
             raw_w2[a] = raw[:].rearrange("p (j r) -> p j r", j=4)
             nc.sync.dma_start(raw_w2[a], w2[K_PASS * a : K_PASS * (a + 1), :].rearrange("(p j) r -> p j r", j=4))
 
-        raw_w1_scales = held([P, H // 4], I32, "raw_w1_scales")
-        nc.vector.memset(raw_w1_scales[:], 0)
-        nc.sync.dma_start(raw_w1_scales[0:P:4, :], w1_scales.bitcast(I32).rearrange("a q c -> q a c"))
+        raw_scales = held([P, 2, H // 4], I32, "raw_scales")
+        nc.vector.memset(raw_scales[:], 0)
+        for n, rows in enumerate((w1_scales, w3_scales)):
+            nc.sync.dma_start(raw_scales[0:P:4, n, :], rows.bitcast(I32).rearrange("a q c -> q a c"))
         load_words(0)
         load_words(1)
         plane = held([P, PASSES, PLANE], U8, "plane")
@@ -114,24 +107,28 @@ def tile_list_tracer_departure_blend_kernel(
         spread = held([P, PLANE // 4], I32, "spread")
         nc.vector.tensor_copy(
             spread[:, : H // 4].rearrange("p (t c) -> p t c", t=4),
-            raw_w1_scales[:].rearrange("p (c t) -> p t c", t=4),
+            raw_scales[:, 0, :].rearrange("p (c t) -> p t c", t=4),
         )
         nc.vector.tensor_copy(spread[:, H // 4 :], picked.bitcast(I32))
         for d in (0, 2, 1, 3):
             nc.sync.dma_start(plane_words[32 * d : 32 * d + 4, :], spread[32 * d : 32 * d + 32 : 4, :])
 
         w1_codes = placed([P, PASSES, 4, 2 * P], U8, "w1_codes", W1_CODES_AT)
-        nc.vector.tensor_copy(
-            w1_codes[:].bitcast(I32).rearrange("p a t (c i) -> p a t c i", i=2),
-            raw_w1.rearrange("p a (c t i) -> p a t c i", t=4, i=2),
+        nc.scalar.copy(
+            w1_codes[:].bitcast(U32).rearrange("p a t (c i) -> p a t c i", i=2),
+            raw_w1.bitcast(U32).rearrange("p a (c t i) -> p a t c i", t=4, i=2),
         )
-        planes = {}
+        w3_spread = held([P, H // 4], I32, "w3_spread")
+        nc.scalar.copy(
+            w3_spread[:].bitcast(U32).rearrange("p (t c) -> p t c", t=4),
+            raw_scales[:, 1, :].bitcast(U32).rearrange("p (c t) -> p t c", t=4),
+        )
         load_w2(0)
         load_w2(1)
-        raw_w3_scales = landing[:, : PASSES * H // 4].rearrange("p (a c) -> p a c", a=PASSES)
-        w3_scale_rows = w3_scales.bitcast(I32).rearrange("a q c -> q a c")
+        w3_plane_words = landing[:, : PASSES * H // 4]
+        w3_plane = w3_plane_words.bitcast(U8).rearrange("p (a c) -> p a c", a=PASSES)
         for d in (0, 2, 1, 3):
-            nc.sync.dma_start(raw_w3_scales[32 * d : 32 * d + 4], w3_scale_rows[4 * d : 4 * d + 4])
+            nc.sync.dma_start(w3_plane_words[32 * d : 32 * d + 4, :], w3_spread[32 * d : 32 * d + 32 : 4, :])
 
         def v_scales(a, lo, width):
             return plane[:, a, H + lo : H + lo + width]
@@ -168,7 +165,6 @@ def tile_list_tracer_departure_blend_kernel(
         w3_codes = held([P, PASSES, 4, P], I32, "w3_codes")
 
         def move_w3():
-            planes["w3"] = move_scales("w3_plane", raw_w3_scales)
             nc.vector.tensor_copy(
                 w3_codes[:].rearrange("p a t (c i) -> p a t c i", i=4),
                 raw_w3[:].rearrange("p a (c t i) -> p a t c i", t=4, i=4),
@@ -181,8 +177,8 @@ def tile_list_tracer_departure_blend_kernel(
                 w2_codes[a, u] = held([P, 2 * P], U32, "w2_codes%d_%d" % (a, u))
                 w2_scales[a, u] = held([P, 2 * P], U8, "w2_scales%d_%d" % (a, u))
 
-        def round_w2_on_vector(a, u):
-            for e in range(2):
+        def round_w2_on_vector(a, u, slots=(0, 1)):
+            for e in slots:
                 rows = raw_w2[a].rearrange("p j (c t i) -> p t c i j", t=4, i=4)[:, 2 * u + e]
                 nc.vector.tensor_scalar(w2_rounded[a, u][:, e], rows, -1.0, None, ALU.mult)
 
@@ -191,8 +187,8 @@ def tile_list_tracer_departure_blend_kernel(
                 rows = raw_w2[a].rearrange("p j (c t i) -> p t c i j", t=4, i=4)[:, 2 * u + e]
                 nc.gpsimd.tensor_scalar(w2_rounded[a, u][:, e], rows, -1.0, 0.0, ALU.mult, ALU.add)
 
-        def round_w2_on_scalar(a, u):
-            for e in range(2):
+        def round_w2_on_scalar(a, u, slots):
+            for e in slots:
                 rows = raw_w2[a].rearrange("p j (c t i) -> p t c i j", t=4, i=4)[:, 2 * u + e]
                 nc.scalar.activation(w2_rounded[a, u][:, e], rows, ACT.Copy, scale=-1.0)
 
@@ -216,12 +212,11 @@ def tile_list_tracer_departure_blend_kernel(
         def quantise_w4():
             second["w4_codes"] = placed([P, N], U32, "w4_codes", RIGHT_PART_AT[0, EIGHTH])
             second["w4_scales"] = placed([P, N], U8, "w4_scales", FRACTION_AT[1, 1] + 5 * QUARTER)
-            for lo, hi in ((0, W4_SPLIT), (W4_SPLIT, N)):
-                nc.vector.quantize_mx(
-                    out=second["w4_codes"][:, lo:hi].bitcast(FP8X4),
-                    scales=second["w4_scales"][:, lo:hi],
-                    in_=w4_rounded[:, lo:hi, :].rearrange("p n t -> p (n t)"),
-                )
+            nc.vector.quantize_mx(
+                out=second["w4_codes"][:].bitcast(FP8X4),
+                scales=second["w4_scales"][:],
+                in_=w4_rounded[:].rearrange("p n t -> p (n t)"),
+            )
 
         weights = {
             "w2": (
@@ -230,7 +225,7 @@ def tile_list_tracer_departure_blend_kernel(
             ),
             "w3": (
                 lambda a, t: w3_codes[:, a, t, :].bitcast(FP8X4),
-                lambda a, t: planes["w3"][:, a, P * t : P * (t + 1)],
+                lambda a, t: w3_plane[:, a, P * t : P * (t + 1)],
             ),
         }
         banks = {}
@@ -384,7 +379,8 @@ def tile_list_tracer_departure_blend_kernel(
 
         whole = slice(0, QUARTER)
         round_w2_on_vector(0, 0)
-        round_w2_on_scalar(0, 1)
+        round_w2_on_vector(0, 1, (0,))
+        round_w2_on_scalar(0, 1, (1,))
         for u in range(2):
             quantise_w2(0, u)
         for u in range(2):
@@ -397,37 +393,37 @@ def tile_list_tracer_departure_blend_kernel(
         for half in range(2):
             take_fractions(half, range(4))
         product("left", ["w2"], 0, (0, 1))
-        product("right", ["w3"], 0, (2, 3))
-        product("right", ["w3"], 1, (4, 5))
+        product("right", ["w3"], 0, (4, 5))
+        product("left", ["w2"], 1, (2, 3))
+        product("right", ["w3"], 1, (6, 7))
         to_sigmoid(3)
         round_w4()
         weigh_left(0, 0, QUARTER)
-        product("left", ["w2"], 1, (0, 1))
+        product("right", ["w3"], 2, (0, 1))
         h_rounded[0] = rounded_tile("h_rounded0", QUARTER, ROUNDED_AT, OVERLAP)
         for lo in (0, EIGHTH):
             weigh_right("right", 0, lo, lo + EIGHTH)
             join(nc.gpsimd, 0, lo, lo + EIGHTH, h_rounded[0][:, lo : lo + EIGHTH])
-        weigh_right("right", 1)
+        product("left", ["w2"], 2, (4, 5))
         weigh_left(1, 0, QUARTER)
-        product("right", ["w3"], 2, (6, 7))
-        product("left", ["w2"], 2, (2, 3))
-        product("difference", ["w3", "w2"], 3, (4, 5))
+        product("difference", ["w3", "w2"], 3, (2, 3))
+        weigh_right("right", 1)
         quantise_w4()
         code_tiles(0, FRACTION_AT[1, 1], FRACTION_AT[1, 1] + 4 * QUARTER)
         quantise_h(0, whole, h_rounded[0])
 
         h_rounded[1] = rounded_tile("h_rounded1", QUARTER, ROUNDED_AT + ROUNDED_BYTES, OVERLAP)
         join(nc.gpsimd, 1, 0, QUARTER, h_rounded[1])
+        tendencies(0, 0, QUARTER, (6, 7))
         weigh_right("right", 2)
         weigh_left(2, 0, EIGHTH)
-        weigh_left(2, EIGHTH, QUARTER)
         left_by_cells(3, (0,), 0)
         left_by_cells(3, (1,), 1)
-        tendencies(0, 0, QUARTER, (6, 7))
         weigh_right("difference", 3)
-        code_tiles(1, FRACTION_AT[3, 1], FRACTION_AT[2, 1])
+        code_tiles(1, FRACTION_AT[3, 1], FRACTION_AT[3, 1] + 4 * QUARTER)
         quantise_h(1, whole, h_rounded[1])
         tendencies(1, 0, QUARTER, (2, 3))
+        weigh_left(2, EIGHTH, QUARTER)
 
         first_cells = rounded_tile("h_rounded2_first", EIGHTH, ROUNDED_AT + 2 * ROUNDED_BYTES)
         join(nc.gpsimd, 2, 0, EIGHTH, first_cells)

@@ -179,8 +179,9 @@ def tile_list_tracer_departure_blend_kernel(
 
         def round_w2_on_vector(a, u, slots=(0, 1)):
             for e in slots:
-                rows = raw_w2[a].rearrange("p j (c t i) -> p t c i j", t=4, i=4)[:, 2 * u + e]
-                nc.vector.tensor_scalar(w2_rounded[a, u][:, e], rows, -1.0, None, ALU.mult)
+                rows = raw_w2[a].rearrange("p j (c t i) -> p t c j i", t=4, i=4)[:, 2 * u + e]
+                dst = w2_rounded[a, u][:, e].rearrange("p c i j -> p c j i")
+                nc.vector.tensor_scalar(dst, rows, -1.0, None, ALU.mult)
 
         def round_w2_on_gpsimd(a, u):
             for e in range(2):

from contextlib import ExitStack

import concourse.mybir as mybir

K, T, S, H, N = 1024, 2048, 1024, 512, 384
FLOPS = 2 * S * (3 * K * H + H * N)

F32 = mybir.dt.float32
BF16 = mybir.dt.bfloat16
I32 = mybir.dt.int32
U32 = mybir.dt.uint32
U16 = mybir.dt.uint16
U8 = mybir.dt.uint8
FP8X4 = mybir.dt.float8_e4m3fn_x4
FP4X4 = mybir.dt.float4_e2m1fn_x4
ALU = mybir.AluOpType
ACT = mybir.ActivationFunctionType

P = 128
K_PASS = 4 * P
PASSES = K // K_PASS
PER_COLUMN = 16
QUARTER = 256
QUARTERS = S // QUARTER
EIGHTH = QUARTER // 2
HALF = S // 2
N_TILES = N // P
SRC_AT = 4 * N
SRC_PAD = 8
OVERLAP = 64
PLANE = H + S
RAW_W2_BYTES = 4 * 4 * H
WINDOW1_AT = 0
PICKED_AT = WINDOW1_AT + 4 * T - OVERLAP
W1_CODES_AT = PICKED_AT + OVERLAP
V0_AT = (W1_CODES_AT + PASSES * 2 * H, W1_CODES_AT + PASSES * 2 * H + 4 * HALF)
PICKED_BYTES = PASSES * 2 * H + 2 * 4 * HALF + 2 * OVERLAP
RAW_W2_AT = (WINDOW1_AT, PICKED_AT + PICKED_BYTES - OVERLAP)
WINDOW0_AT = RAW_W2_AT[1] + RAW_W2_BYTES
RAW_W3_AT = WINDOW0_AT
RAW_W4_AT = RAW_W3_AT + PASSES * 4 * H
ROUNDED_BYTES = 2 * 4 * QUARTER
ROUNDED_AT = WINDOW0_AT + 6 * T
SLOT_BYTES = 4 * 2 * QUARTER
SLOTS_AT = ROUNDED_AT + 3 * ROUNDED_BYTES
FRACTION_AT = dict(
    [((q, u), RAW_W2_AT[q // 2] + (q % 2 * 2 + u) * SLOT_BYTES) for q in range(QUARTERS) for u in range(2)]
)
SCALED_AT = SLOTS_AT + 4 * SLOT_BYTES
RIGHT_PART_AT = {(0, EIGHTH): SLOTS_AT + SLOT_BYTES}
LEFT_PART_AT = {(0, 0): RAW_W3_AT, (1, 0): FRACTION_AT[0, 0], (2, 0): SLOTS_AT + 3 * SLOT_BYTES,
                (2, EIGHTH): ROUNDED_AT + ROUNDED_BYTES}


def tile_list_tracer_departure_blend_kernel(
    tc, tab_words, tab_scales, offs, w1_words, w1_scales, w2, w3_words, w3_scales, w4, src, out
):
    nc = tc.nc
    with ExitStack() as ctx:
        keep = ctx.enter_context(tc.tile_pool(name="keep", bufs=1))
        psum = ctx.enter_context(tc.psum_pool(name="psum", bufs=1))
        chain = ctx.enter_context(tc.tile_pool(name="chain", bufs=1))

        def placed(shape, dtype, name, at):
            return chain.tile(shape, dtype, name=name, offset=at, align_bytes=64)

        def held(shape, dtype, name, at=None):
            if at is not None:
                return placed(shape, dtype, name, at)
            return keep.tile(shape, dtype, name=name, align_bytes=64)

        offsets = keep.tile([P, S // PER_COLUMN], U16, name="offsets")
        nc.sync.dma_start(offsets[:], offs)
        landing = held([P, H], I32, "landing")
        raw_w1 = landing[:].rearrange("p (a c) -> p a c", a=PASSES)
        nc.sync.dma_start(raw_w1, w1_words.bitcast(I32).rearrange("a p c -> p a c"))

        scale_window = held([P, T], U8, "scale_window")
        nc.vector.memset(scale_window[:].bitcast(I32), 0)
        nc.sync.dma_start(
            scale_window[:].bitcast(I32)[0:P:4, :], tab_scales.bitcast(I32).rearrange("a q t -> q a t")
        )

        word_window, raw_w2 = {}, {}

        def load_words(a):
            word_window[a] = held([P, T], I32, "word_window%d" % a, (WINDOW0_AT, None)[a])
            nc.sync.dma_start(word_window[a][:], tab_words[a].rearrange("p t i -> p (t i)").bitcast(I32))

        def load_w2(a):
            raw = held([P, 4 * H], F32, "raw_w2_%d" % a, RAW_W2_AT[a])
            raw_w2[a] = raw[:].rearrange("p (j r) -> p j r", j=4)
            nc.sync.dma_start(raw_w2[a], w2[K_PASS * a : K_PASS * (a + 1), :].rearrange("(p j) r -> p j r", j=4))

        raw_scales = held([P, 2, H // 4], I32, "raw_scales")
        nc.vector.memset(raw_scales[:], 0)
        for n, rows in enumerate((w1_scales, w3_scales)):
            nc.sync.dma_start(raw_scales[0:P:4, n, :], rows.bitcast(I32).rearrange("a q c -> q a c"))
        load_words(0)
        load_words(1)
        plane = held([P, PASSES, PLANE], U8, "plane")
        plane_words = plane[:].rearrange("p a s -> p (a s)").bitcast(I32)
        nc.vector.memset(plane_words, 0)

        picked = placed([P, PICKED_BYTES], U8, "picked_scales", PICKED_AT)[:, :S]
        nc.vector.tensor_copy(picked, scale_window[:].indirect(offsets[:]))
        spread = held([P, PLANE // 4], I32, "spread")
        nc.vector.tensor_copy(
            spread[:, : H // 4].rearrange("p (t c) -> p t c", t=4),
            raw_scales[:, 0, :].rearrange("p (c t) -> p t c", t=4),
        )
        nc.vector.tensor_copy(spread[:, H // 4 :], picked.bitcast(I32))
        for d in (0, 2, 1, 3):
            nc.sync.dma_start(plane_words[32 * d : 32 * d + 4, :], spread[32 * d : 32 * d + 32 : 4, :])

        w1_codes = placed([P, PASSES, 4, 2 * P], U8, "w1_codes", W1_CODES_AT)
        nc.scalar.copy(
            w1_codes[:].bitcast(U32).rearrange("p a t (c i) -> p a t c i", i=2),
            raw_w1.bitcast(U32).rearrange("p a (c t i) -> p a t c i", t=4, i=2),
        )
        w3_spread = held([P, H // 4], I32, "w3_spread")
        nc.scalar.copy(
            w3_spread[:].bitcast(U32).rearrange("p (t c) -> p t c", t=4),
            raw_scales[:, 1, :].bitcast(U32).rearrange("p (c t) -> p t c", t=4),
        )
        load_w2(0)
        load_w2(1)
        w3_plane_words = landing[:, : PASSES * H // 4]
        w3_plane = w3_plane_words.bitcast(U8).rearrange("p (a c) -> p a c", a=PASSES)
        for d in (0, 2, 1, 3):
            nc.sync.dma_start(w3_plane_words[32 * d : 32 * d + 4, :], w3_spread[32 * d : 32 * d + 32 : 4, :])

        def v_scales(a, lo, width):
            return plane[:, a, H + lo : H + lo + width]

        v_halves = {}

        def gather_words(a, half):
            name = "v_codes_%d_%d" % (a, half)
            v_halves[a, half] = held([P, HALF], U32, name, V0_AT[half] if a == 0 else None)
            cols = slice(half * HALF // PER_COLUMN, (half + 1) * HALF // PER_COLUMN)
            nc.vector.tensor_copy(v_halves[a, half][:], word_window[a][:].bitcast(U32).indirect(offsets[:, cols]))

        def v_codes(a, lo, width):
            return v_halves[a, lo // HALF][:, lo % HALF : lo % HALF + width].bitcast(FP8X4)

        gather_words(0, 0)
        gather_words(0, 1)
        raw_w3 = placed([P, PASSES, H], I32, "raw_w3", RAW_W3_AT)
        nc.sync.dma_start(
            raw_w3[:], w3_words.rearrange("a p c i -> a p (c i)").bitcast(I32).rearrange("a p c -> p a c")
        )
        gather_words(1, 0)
        gather_words(1, 1)

        raw4 = placed([P, SRC_AT + SRC_PAD], F32, "raw_w4", RAW_W4_AT)
        raw_w4 = raw4[:, :SRC_AT].rearrange("p (t n) -> p t n", t=4)
        src_col = raw4[:, SRC_AT : SRC_AT + N_TILES]
        w4_rows = w4.rearrange("(c t i) n -> t c i n", t=4, i=4)
        for t in range(4):
            nc.sync.dma_start(raw_w4[:, t, :], w4_rows[t])
        with nc.allow_non_contiguous_dma(reason="one source value a partition"):
            nc.sync.dma_start(src_col, src.rearrange("(c p) -> p c", p=P))

        w3_codes = held([P, PASSES, 4, P], I32, "w3_codes")

        def move_w3():
            nc.vector.tensor_copy(
                w3_codes[:].rearrange("p a t (c i) -> p a t c i", i=4),
                raw_w3[:].rearrange("p a (c t i) -> p a t c i", t=4, i=4),
            )

        w2_rounded, w2_codes, w2_scales = {}, {}, {}
        for a in range(PASSES):
            for u in range(2):
                w2_rounded[a, u] = held([P, 2, 32, 4, 4], BF16, "w2_rounded%d_%d" % (a, u))
                w2_codes[a, u] = held([P, 2 * P], U32, "w2_codes%d_%d" % (a, u))
                w2_scales[a, u] = held([P, 2 * P], U8, "w2_scales%d_%d" % (a, u))

        def round_w2_on_vector(a, u, slots=(0, 1)):
            for e in slots:
                rows = raw_w2[a].rearrange("p j (c t i) -> p t c j i", t=4, i=4)[:, 2 * u + e]
                dst = w2_rounded[a, u][:, e].rearrange("p c i j -> p c j i")
                nc.vector.tensor_scalar(dst, rows, -1.0, None, ALU.mult)

        def round_w2_on_gpsimd(a, u):
            for e in range(2):
                rows = raw_w2[a].rearrange("p j (c t i) -> p t c i j", t=4, i=4)[:, 2 * u + e]
                nc.gpsimd.tensor_scalar(w2_rounded[a, u][:, e], rows, -1.0, 0.0, ALU.mult, ALU.add)

        def round_w2_on_scalar(a, u, slots):
            for e in slots:
                rows = raw_w2[a].rearrange("p j (c t i) -> p t c i j", t=4, i=4)[:, 2 * u + e]
                nc.scalar.activation(w2_rounded[a, u][:, e], rows, ACT.Copy, scale=-1.0)

        def quantise_w2(a, u):
            nc.vector.quantize_mx(
                out=w2_codes[a, u][:].bitcast(FP8X4),
                scales=w2_scales[a, u][:],
                in_=w2_rounded[a, u][:].rearrange("p t c i j -> p (t c i j)"),
            )

        w4_rounded = held([P, N, 4], BF16, "w4_rounded")

        def round_w4():
            nc.scalar.copy(
                w4_rounded[:].rearrange("p (n e) t -> p n t e", e=2),
                raw_w4.rearrange("p t (n e) -> p n t e", e=2),
            )

        second = {}

        def quantise_w4():
            second["w4_codes"] = placed([P, N], U32, "w4_codes", RIGHT_PART_AT[0, EIGHTH])
            second["w4_scales"] = placed([P, N], U8, "w4_scales", FRACTION_AT[1, 1] + 5 * QUARTER)
            nc.vector.quantize_mx(
                out=second["w4_codes"][:].bitcast(FP8X4),
                scales=second["w4_scales"][:],
                in_=w4_rounded[:].rearrange("p n t -> p (n t)"),
            )

        weights = {
            "w2": (
                lambda a, t: w2_codes[a, t // 2][:, P * (t % 2) : P * (t % 2 + 1)].bitcast(FP8X4),
                lambda a, t: w2_scales[a, t // 2][:, P * (t % 2) : P * (t % 2 + 1)],
            ),
            "w3": (
                lambda a, t: w3_codes[:, a, t, :].bitcast(FP8X4),
                lambda a, t: w3_plane[:, a, P * t : P * (t + 1)],
            ),
        }
        banks = {}

        def bank_tile(key, number, shape):
            banks[key] = psum.tile([P] + shape, F32, name="bank", tag="bank%d" % number)
            return banks[key]

        def one_pass(dst, weight, a, t, lo, width, start, stop):
            codes_of, scales_of = weights[weight]
            nc.tensor.matmul_mx(
                out=dst,
                lhsT=codes_of(a, t),
                lhsT_scale=scales_of(a, t),
                rhs=v_codes(a, lo, width),
                rhs_scale=v_scales(a, lo, width),
                start=start,
                stop=stop,
            )

        def product(key, names, q, numbers, passes=(0, 1)):
            for u in range(2):
                bank = bank_tile((key, q, u), numbers[u], [2, QUARTER])
                steps = [(w, a, e) for w in names for a in passes for e in range(2)]
                for n, (w, a, e) in enumerate(steps):
                    one_pass(bank[:, e, :], w, a, 2 * u + e, q * QUARTER, QUARTER, n == 0, n == len(steps) - 1)

        def left_by_cells(q, sides, number):
            for side in sides:
                bank = bank_tile(("by_cells", side), number, [4, EIGHTH])
                steps = [(a, t) for a in range(PASSES) for t in range(4)]
                for n, (a, t) in enumerate(steps):
                    lo = q * QUARTER + side * EIGHTH
                    one_pass(bank[:, t, :], "w2", a, t, lo, EIGHTH, n == 0, n == len(steps) - 1)

        def fraction_product(half, slots, first):
            for a in range(PASSES):
                for t in slots:
                    if a == 0:
                        bank_tile(("w1", half, t), first + t, [HALF])
                    nc.tensor.matmul_mx(
                        out=banks["w1", half, t][:],
                        lhsT=w1_codes[:, a, t, :].bitcast(FP4X4),
                        lhsT_scale=plane[:, a, P * t : P * (t + 1)],
                        rhs=v_codes(a, half * HALF, HALF),
                        rhs_scale=v_scales(a, half * HALF, HALF),
                        start=(a == 0),
                        stop=(a == PASSES - 1),
                    )

        def sums(key, q, u):
            return banks[key, q, u][:].rearrange("p e j -> p j e")

        out_rows = out.rearrange("(c p) j -> p c j", p=P)
        fraction, right_part, left_part = {}, {}, {}
        h_rounded, h_codes, h_scales = {}, {}, {}

        def take_fractions(half, slots):
            for t in slots:
                for q in (2 * half, 2 * half + 1):
                    if t % 2 == 0:
                        name = "fraction%d_%d" % (q, t // 2)
                        fraction[q, t // 2] = held([P, 2, QUARTER], F32, name, FRACTION_AT.get((q, t // 2)))
                    sums_t = banks["w1", half, t][:, q % 2 * QUARTER : (q % 2 + 1) * QUARTER]
                    nc.scalar.activation(fraction[q, t // 2][:, t % 2, :], sums_t, ACT.Tanh, scale=0.5)

        def to_sigmoid(q):
            for u in range(2):
                nc.scalar.activation(fraction[q, u][:], fraction[q, u][:], ACT.Copy, scale=0.5, bias=0.5)

        def fractions(q, u):
            return fraction[q, u][:].rearrange("p e j -> p j e")

        def weigh_right(key, q, lo=0, hi=QUARTER):
            at = SCALED_AT if key == "difference" else RIGHT_PART_AT.get((q, lo))
            right_part[q, lo] = held([P, 2, hi - lo, 2], F32, "right_part%d_%d" % (q, lo), at)
            for u in range(2):
                if key == "difference":
                    nc.vector.tensor_tensor(right_part[q, lo][:, u], fractions(q, u), sums(key, q, u), ALU.mult)
                else:
                    nc.vector.scalar_tensor_tensor(
                        right_part[q, lo][:, u], fractions(q, u)[:, lo:hi], 1.0, sums(key, q, u)[:, lo:hi],
                        ALU.add, ALU.mult,
                    )

        def weigh_left(q, lo, hi):
            name = "left_part%d_%d" % (q, lo)
            left_part[q, lo] = held([P, 2, hi - lo, 2], F32, name, LEFT_PART_AT.get((q, lo)))
            for u in range(2):
                nc.vector.scalar_tensor_tensor(
                    left_part[q, lo][:, u], fractions(q, u)[:, lo:hi], 1.0, sums("left", q, u)[:, lo:hi],
                    ALU.subtract, ALU.mult,
                )

        def rounded_tile(name, width, at, pad=0):
            padded = held([P, 4 * width + pad // 2], BF16, name, at)
            return padded[:, : 4 * width].rearrange("p (j u e) -> p j u e", u=2, e=2)

        def cells_of(parts, q, lo, hi):
            first = lo if (q, lo) in parts else 0
            return parts[q, first][:, :, lo - first : hi - first, :].rearrange("p u j e -> p j u e")

        def right_of(q, lo, hi):
            return cells_of(right_part, q, lo, hi)

        def join(engine, q, lo, hi, dst):
            engine.tensor_tensor(dst, right_of(q, lo, hi), cells_of(left_part, q, lo, hi), ALU.add)

        def add_left(q, side, dst):
            left = banks["by_cells", side][:].rearrange("p (u e) j -> p j u e", u=2)
            lo, hi = side * EIGHTH, (side + 1) * EIGHTH
            nc.vector.tensor_tensor(dst[:, lo:hi], right_of(q, lo, hi), left, ALU.subtract)

        def code_tiles(q, codes_at=None, scales_at=None):
            h_codes[q] = held([P, QUARTER], U32, "h_codes%d" % q, codes_at)
            h_scales[q] = held([P, QUARTER], U8, "h_scales%d" % q, scales_at)

        def quantise_h(q, cols, rounded):
            nc.vector.quantize_mx(
                out=h_codes[q][:, cols].bitcast(FP8X4),
                scales=h_scales[q][:, cols],
                in_=rounded.rearrange("p j u e -> p (j u e)"),
            )

        def tendencies(q, lo, hi, numbers, on_vector=(), by_tile=False):
            result = held([P, N_TILES, hi - lo], F32, "result%d_%d" % (q, lo))
            cols = slice(q * QUARTER + lo, q * QUARTER + hi)
            for first in range(0, N_TILES, 2):
                bank = bank_tile(("out", q, first), numbers[first // 2], [2, hi - lo])
                tiles = range(first, min(first + 2, N_TILES))
                for c in tiles:
                    nc.tensor.matmul_mx(
                        out=bank[:, c - first, :],
                        lhsT=second["w4_codes"][:, P * c : P * (c + 1)].bitcast(FP8X4),
                        lhsT_scale=second["w4_scales"][:, P * c : P * (c + 1)],
                        rhs=h_codes[q][:, lo:hi].bitcast(FP8X4),
                        rhs_scale=h_scales[q][:, lo:hi],
                        start=True,
                        stop=True,
                    )
                for c in tiles:
                    dst, acc, bias = result[:, c, :], bank[:, c - first, :], src_col[:, c : c + 1]
                    if c in on_vector:
                        nc.vector.tensor_scalar(dst, acc, 0.5, bias, ALU.mult, ALU.add)
                    else:
                        nc.scalar.activation(dst, acc, ACT.Identity, bias=bias, scale=1.0 if q == 3 else 0.5)
                    if by_tile:
                        nc.sync.dma_start(out_rows[:, c, cols], dst)
            if not by_tile:
                nc.sync.dma_start(out_rows[:, :, cols], result[:])

        whole = slice(0, QUARTER)
        round_w2_on_vector(0, 0)
        round_w2_on_vector(0, 1, (0,))
        round_w2_on_scalar(0, 1, (1,))
        for u in range(2):
            quantise_w2(0, u)
        for u in range(2):
            round_w2_on_vector(1, u)
        for u in range(2):
            quantise_w2(1, u)
        move_w3()
        for half in range(2):
            fraction_product(half, range(4), 4 * half)
        for half in range(2):
            take_fractions(half, range(4))
        product("left", ["w2"], 0, (0, 1))
        product("right", ["w3"], 0, (4, 5))
        product("left", ["w2"], 1, (2, 3))
        product("right", ["w3"], 1, (6, 7))
        to_sigmoid(3)
        round_w4()
        weigh_left(0, 0, QUARTER)
        product("right", ["w3"], 2, (0, 1))
        h_rounded[0] = rounded_tile("h_rounded0", QUARTER, ROUNDED_AT, OVERLAP)
        for lo in (0, EIGHTH):
            weigh_right("right", 0, lo, lo + EIGHTH)
            join(nc.gpsimd, 0, lo, lo + EIGHTH, h_rounded[0][:, lo : lo + EIGHTH])
        product("left", ["w2"], 2, (4, 5))
        weigh_left(1, 0, QUARTER)
        product("difference", ["w3", "w2"], 3, (2, 3))
        weigh_right("right", 1)
        quantise_w4()
        code_tiles(0, FRACTION_AT[1, 1], FRACTION_AT[1, 1] + 4 * QUARTER)
        quantise_h(0, whole, h_rounded[0])

        h_rounded[1] = rounded_tile("h_rounded1", QUARTER, ROUNDED_AT + ROUNDED_BYTES, OVERLAP)
        join(nc.gpsimd, 1, 0, QUARTER, h_rounded[1])
        tendencies(0, 0, QUARTER, (6, 7))
        weigh_right("right", 2)
        weigh_left(2, 0, EIGHTH)
        left_by_cells(3, (0,), 0)
        left_by_cells(3, (1,), 1)
        weigh_right("difference", 3)
        code_tiles(1, FRACTION_AT[3, 1], FRACTION_AT[3, 1] + 4 * QUARTER)
        quantise_h(1, whole, h_rounded[1])
        tendencies(1, 0, QUARTER, (2, 3))
        weigh_left(2, EIGHTH, QUARTER)

        first_cells = rounded_tile("h_rounded2_first", EIGHTH, ROUNDED_AT + 2 * ROUNDED_BYTES)
        join(nc.gpsimd, 2, 0, EIGHTH, first_cells)
        h_rounded[3] = rounded_tile("h_rounded3", QUARTER, None)
        for side in range(2):
            add_left(3, side, h_rounded[3])
        code_tiles(2, SCALED_AT + 4 * QUARTER, SCALED_AT + QUARTER)
        quantise_h(2, slice(0, EIGHTH), first_cells)
        tendencies(2, 0, EIGHTH, (6, 7))
        code_tiles(3, LEFT_PART_AT[2, 0])
        quantise_h(3, whole, h_rounded[3])
        tendencies(3, 0, QUARTER, (4, 5), by_tile=True)
        last_cells = rounded_tile("h_rounded2_last", EIGHTH, SCALED_AT + 8 * QUARTER)
        join(nc.vector, 2, EIGHTH, QUARTER, last_cells)
        quantise_h(2, slice(EIGHTH, QUARTER), last_cells)
        tendencies(2, EIGHTH, QUARTER, (0, 1), on_vector=(0, 1))
